import numpy as np, ml_dtypes
CORES = [13,21,141,149]
N = 4
BF = ml_dtypes.bfloat16
def gentries(a):
    return np.ascontiguousarray(a.reshape(8, 16, -1).transpose(0, 2, 1)).reshape(8, -1)
def gtable(e):
    e = np.asarray(e); return np.ascontiguousarray(e.reshape(8, -1, 16).transpose(0, 2, 1)).reshape(128, -1).astype(np.int32)
W, K, E, X, S, RO = 4096, 1536, 96, 2, 4, 2
ANY = np.arange(256); LEN = np.arange(1, 13)
def place(u1, u2, m):
    return ((((u1 & 4095) * (u2 & 4095)) >> 5) + u2 + 97 * m) & (W - 1)
def hashes(st, m, wt):
    u = np.where(np.arange(12) < m[:, None], st, 0) @ wt
    return place(u[:, 0], u[:, 1], m)
def ropes(rng, shape, lens):
    n = np.minimum(rng.integers(0, 8, shape), 4)
    return np.where(np.arange(4) < n[..., None], lens[rng.integers(0, len(lens), shape + (4,))], 0)
def fill(rng):
    return np.concatenate([rng.integers(0, 256, (N, 8, 12, W)), np.moveaxis(ropes(rng, (N, 8, W), LEN), 3, 2)], axis=2)
def pool(rng, M, vals):
    st = vals[rng.integers(0, len(vals), (M, 12))]; h = max(M // 8, 1); keep = rng.integers(0, 13, M); keep[:h] = 0
    return np.where(np.arange(12) < keep[:, None], st[rng.integers(0, h, M)], st)
def plant(T, st, m, ro, wt):
    h = hashes(st, m, wt); T[:, h] = np.concatenate([st.T, ro.T])
def asks(rng, st, vals, lens):
    x = st[rng.integers(0, len(st), K)]; cut = np.where(rng.random(K) < 0.3, rng.integers(0, 13, K), 12)
    x = np.where(np.arange(12) < cut[:, None], x, vals[rng.integers(0, len(vals), (K, 12))])
    return np.concatenate([x.T, ropes(rng, (K,), lens).T])
def parts(rng, wt, M, n, vals, lens):
    P = fill(rng); q = np.zeros((N, 8, 16, K), np.int64)
    for g in range(8):
        st = pool(rng, int(M[g]), vals)
        for a in range(N):
            plant(P[a, g], st[rng.integers(0, len(st), n)], lens[rng.integers(0, len(lens), n)], ropes(rng, (n,), lens), wt[a, g])
            q[a, g] = asks(rng, st, vals, lens)
    return P, q
def alike_ropes(n, l):
    return np.tile(np.array((tuple(l) + (0, 0, 0, 0))[:4]), (n, 1))
def steer(rng, c):
    v = ((np.diff(c, axis=1, prepend=0) - 194) & (W - 1)) + W * rng.integers(0, 65280 // W, c.shape)
    return np.stack([v % 255, v // 255], axis=2).reshape(len(c), 12)
def meetings(rng, ends):
    n = 6; F = 2 + 2 * S; cut = 2 + n * np.arange(7); four = (6, 8, 10, 12)
    c = 1 + rng.permutation(W - 2)[:(2 + 7 * n) * 6].reshape(-1, 6)
    d, s1, e1, q2, s3, o3, q4, s5 = np.split(c, cut)
    for i in range(2): d[i, ends[i][0]] = ends[i][1]
    s1[:, 1] = s1[:, 0]; e1[:, 0] = s1[:, 0]
    q2[:, S] = q2[:, 1]
    s3[:, S - 1] = s3[:, S]; o3[:, :2] = s3[:, :2]
    q4[:, 3] = q4[:, 1]
    s5[:, 5] = s5[:, 2]
    x = steer(rng, c); d, s1, e1, q2, s3, o3, q4, s5 = np.split(x, cut)
    e1[:, :2] = s1[:, :2]; o3[:, :4] = s3[:, :4]
    r2 = q2.copy(); r2[:, 4:] = (r2[:, 4:] + rng.integers(1, 256, (n, 8))) & 255
    r4 = q4.copy(); r4[:, 4:] = (r4[:, 4:] + rng.integers(1, 256, (n, 8))) & 255
    marks = [(d, 4, four), (d, F + 2, ()), (s1, 4, four), (s1, F + 2, ()), (r2, 4, four), (q2, F + 2, ()), (s3, 4, four), (s3, F + 2, ()), (o3, F, ()), (r4, 4, ()), (s5, 4, (6,))]
    ask = [(d, (4,)), (s1, (4,)), (q2, (F,)), (s3, (4,)), (o3, (4,)), (q4, (8,)), (s5, (4,)), (s5, (12,)), (e1, (12, 2)), (q2, (4,)), (q4, (8, 4))]
    return marks, np.concatenate([y for y, l in ask]), np.concatenate([alike_ropes(len(y), l) for y, l in ask]), 2 + 7 * n
def pack(P, q, wt):
    w = np.concatenate([wt, np.zeros((N, 8, 4, 2), np.int64)], axis=2)
    return {"mk": P.reshape(N, 128, W).astype(np.float32).astype(BF), "qs": q.reshape(N, 128, K).astype(np.float32).astype(BF), "wt": w.reshape(N, 128, 2).astype(np.float32).astype(BF)}
def setup_inputs(rng):
    wt = rng.integers(0, 256, (N, 8, 12, 2)); P, q = parts(rng, wt, [512] * 8, 3 * W // 4, ANY, LEN)
    return pack(P, q, wt)
def setup_inputs_alike(rng):
    wt = rng.integers(0, 256, (N, 8, 12, 2)); P, q = parts(rng, wt, rng.integers(16, 33, 8), 160, ANY, LEN)
    return pack(P, q, wt)
def setup_inputs_ends(rng):
    wt = rng.choice(np.array([0, 1, 255]), (N, 8, 12, 2)); wt[:, 3] = 0; wt[:, 5] = 255
    for g in (0, 1, 6):
        wt[:, g] = 0; wt[:, g, 0::2, 1] = 1; wt[:, g, 1::2, 1] = 255
    P, q = parts(rng, wt, [64] * 8, W // 4, np.array([0, 255, 0, 1, 254]), np.array([1, 12, 1, 12, 2, 11]))
    for g, ends in ((0, ((S, 0), (1, W - 1))), (1, ((S + 1, 0), (S + 1, W - 1))), (6, ((S, W - 1), (1, 0)))):
        marks, st, ro, look = meetings(rng, ends)
        for a in range(N):
            for y, m, l in marks: plant(P[a, g], y, np.full(len(y), m), alike_ropes(len(y), l), wt[a, g])
            j = np.concatenate([rng.permutation(len(st)), rng.integers(0, look, K - len(st))])
            q[a, g] = np.concatenate([st[j].T, ro[j].T])
    x = rng.integers(225, 256, (2048, 12)); x = x[np.unique(np.sum(x, axis=1), return_index=True)[1]]
    u = 255 * np.sum(x, axis=1); x = x[np.argsort(-((((u & 4095) ** 2) >> 5) + u))[:24]]
    for a in range(N):
        plant(P[a, 5], x, np.full(len(x), 12), np.zeros((len(x), 4), np.int64), wt[a, 5])
        t = rng.permutation(K)[:96]; q[a, 5][:12, t] = x[np.arange(96) % len(x)].T; q[a, 5][12:, t] = np.array([12, 0, 0, 0])[:, None]
    return pack(P, q, wt)
def setup_inputs_full(rng):
    w = rng.integers(0, 256, (8, 12, 2)); wt = np.stack([w] * N); P = fill(rng); q = np.zeros((N, 8, 16, K), np.int64)
    for g in range(8):
        st = rng.integers(0, 256, (2048, 12)); hs = np.stack([hashes(st, np.full(2048, m), w[g]) for m in [5] + [9 + i for i in range(S)]])
        used = set(); keep = []
        for i in range(2048):
            c = set(hs[:, i].tolist())
            if len(keep) < E and len(c) == S + 1 and not (c & used):
                used |= c; keep.append(i)
        x = st[np.array(keep)]; n = len(keep)
        for a in range(N):
            plant(P[a, g], x, np.full(n, 5), np.stack([np.array([9, 10, 11, 12])] * n), w[g])
            plant(P[a, g], x, np.full(n, 8 + S), np.zeros((n, 4), np.int64), w[g])
            j = np.concatenate([rng.permutation(n), rng.integers(0, n, K - n)])
            first = (rng.random(K) < 0.5) | (np.arange(K) < n)
            ro = np.where(first[:, None], np.array([5, 8, 0, 0]), np.array([7 + S, 5, 12, 0]))
            q[a, g] = np.concatenate([x[j].T, ro.T])
    return pack(P, q, wt)
def setup_inputs_still(rng):
    wt = rng.integers(0, 256, (N, 8, 12, 2)); P, q = parts(rng, wt, [256] * 8, W // 2, ANY, LEN); e = rng.permutation(8)
    q[:, :, 12:] = np.where(rng.random((N, 8, 1, K)) < 0.5, 0, q[:, :, 12:])
    q[:, e[0], 12:] = 0; P[:, e[1], 12:] = 0; q[:, e[2], :12] = rng.integers(0, 256, (N, 12, K))
    q[:, e[2], 12:] = np.where(q[:, e[2], 12:] > 0, np.maximum(q[:, e[2], 12:], 4), 0)
    return pack(P, q, wt)
def setup_inputs_spread(rng):
    vals = np.minimum(np.exp2(8.01 * rng.random(512)).astype(np.int64), 256) - 1
    wt = vals[rng.integers(0, 512, (N, 8, 12, 2))]; P, q = parts(rng, wt, 2 ** rng.integers(3, 12, 8), W // 2, vals, LEN)
    return pack(P, q, wt)
def check_inputs(d):
    bad = []
    for k, n in (("mk", W), ("qs", K), ("wt", 2)):
        v = np.asarray(d[k]).astype(np.float32).reshape(N, 8, 16, n)
        if not np.all(v == np.floor(v)): bad.append("whole numbers of " + k)
        if not (np.min(v) >= 0 and np.max(v[:, :, :12]) <= 255): bad.append("range of " + k)
        if not np.max(v[:, :, 12:]) <= (0 if k == "wt" else 12): bad.append("last four rows of " + k)
        if k != "wt" and np.any((v[:, :, 12:15] == 0) & (v[:, :, 13:] > 0)): bad.append("ropes of " + k)
    return bad
def reference(mk, qs, wt):
    P = mk.astype(np.float32).astype(np.int32).reshape(N, 8, 16, W); q = qs.astype(np.float32).astype(np.int32).reshape(N, 8, 16, K)
    w = np.ascontiguousarray(wt.astype(np.float32).astype(np.int32).reshape(N, 8, 16, 2)[:, :, :12].transpose(0, 1, 3, 2))
    p = np.arange(12, dtype=np.int32)[:, None]
    for rnd in range(RO):
        sy = q[:, :, :12]; ro = q[:, :, 12:]
        b = np.full((N, 8, K), -1, np.int32); f = np.full((N, 8, K), -1, np.int32); mb = np.zeros((N, 8, K), np.int32); mf = np.zeros((N, 8, K), np.int32)
        for step in range(S):
            m = ro[:, :, 0]
            u = np.matmul(w, np.where(p < m[:, :, None], sy, 0))
            h = place(u[:, :, 0], u[:, :, 1], m)
            v = np.take_along_axis(P, h[:, :, None], axis=3)
            same = np.all((v[:, :, :12] == sy) | (p >= m[:, :, None]), axis=2)
            hit = (m > 0) & same; miss = (m > 0) & ~same
            b = np.where(hit, h, b); mb = np.where(hit, m, mb)
            f = np.where(miss, h, np.where(hit, -1, f)); mf = np.where(miss, m, mf)
            less = np.concatenate([ro[:, :, 1:], np.zeros((N, 8, 1, K), np.int32)], axis=2)
            ro = np.where(hit[:, :, None], v[:, :, 12:], np.where(miss[:, :, None], less, ro))
        old = np.take_along_axis(P, np.maximum(b, 0)[:, :, None], axis=3)[:, :, :12]
        new = q.copy(); new[:, :, :12] = np.where((b >= 0)[:, :, None] & (p < mb[:, :, None] + X), old, sy)
        if rnd < RO - 1:
            for a in range(N):
                for g in range(8):
                    T = P[a, g]; c = np.nonzero((b[a, g, :E] >= 0) & (f[a, g, :E] >= 0))[0]
                    t = c[np.unique(f[a, g, c], return_index=True)[1]]
                    T[:, f[a, g, t]] = np.concatenate([sy[a, g][:, t], ro[a, g][:, t]])
                    t = c[np.unique(b[a, g, c], return_index=True)[1]]
                    have = T[12:15, b[a, g, t]]
                    T[12:, b[a, g, t]] = np.concatenate([mf[a, g, t][None], have])
            q = np.ascontiguousarray(new.reshape(N, 8, 16, N, K // N).transpose(3, 1, 2, 0, 4)).reshape(N, 8, 16, K)
    return {"yq": new.reshape(N, 128, K).astype(np.float32).astype(BF), "yb": np.stack([gtable(x) for x in b]).astype(np.float32)}

@@ -1,0 +1,632 @@
+from concourse.mybir import AluOpType as Op, ActivationFunctionType as Fn, AxisListType
+
+W, K, NB = 4096, 1536, 384
+CH, NJ = 768, 48
+MKW = W + 128
+LN256 = 5.545177444479562
+CYC, PEC, WAKE, SLACK = 0.00083, 0.00042, 0.17, 0.04
+
+_sets = ["LX", "LY", "LN", "LV0", "LV1", "LV2", "LV3", "LB", "BIG"]
+_mats = ["JR", "JA", "JP", "BD", "ID", "HI", "NI", "R0", "ISY", "SRC", "CAQ", "CA", "RS", "DN", "R12"]
+SCRATCH = {"mkT": ("sbuf", [128, MKW], "bfloat16"), "land": ("sbuf", [128, NB], "bfloat16")}
+for _n in ("qN", "qA", "qB", "qF", "zz", "nn", "vv", "dd", "sd"):
+    SCRATCH[_n] = ("sbuf", [128, K], "bfloat16")
+for _n in ("qj", "zp"):
+    SCRATCH[_n] = ("sbuf", [128, K], "float32")
+for _n in _sets:
+    SCRATCH[_n] = ("sbuf", [128, 2048], "bfloat16")
+for _n in _mats:
+    SCRATCH[_n] = ("sbuf", [128, 128], "bfloat16")
+
+
+def _add(dtype, **widths):
+    for n, w in widths.items():
+        SCRATCH[n] = ("sbuf", [128, w], dtype)
+
+
+_add("bfloat16", wS=2, Aw=384, tm=288, Lb=96, khb=32, sb=16, cm=96, Eb=96, vb=96, mf=96, Sb=96)
+_add("int32", pi=1, ki=1, ci=4, U=288, UA=288, P=96, Wd=96, S=96, H=96, codeS=384, ch=96, B=96, Hb=96, Li=96, y0=96,
+     fc=192, f1=32, FB=12, cl=12, key=12, kh=24, si=16)
+_add("float32", col=32, E256=16, geo=64, IT=96, LM=576, DU=12, hitS=384, th=96, m97=96, mt=192, y1=96, y2=96, y3=96, yS=96,
+     al=192, ms=192, ed=32, ed2=12, nk=12, key1=12, LK=1152, EQ=1152, CNT=12, w1=64, mk1=96)
+_add("uint16", OFF=96, OB=96, OE=12)
+BANKS = ("g00", "g01", "g10", "g11", "h0", "h1", "k0", "k1")
+for _n in BANKS:
+    SCRATCH[_n] = ("psum", [128, 512], "float32")
+SEMAPHORES = ["sV", "sA", "sP", "sG", "dw", "dq0", "dq1", "dq2", "dq3", "dm0", "dm1", "dy0", "dy1", "dy2", "dy3",
+              "db0", "db1", "db2", "db3", "arr0", "arr1", "arr2", "arr3", "sent", "rin", "rls"]
+
+
+def relay_of(src, dst, cores, topo):
+    k = 0
+    for d in cores:
+        if d == src or topo.may_write(src, d):
+            if d == dst:
+                return None
+            continue
+        own = [c for c in topo.cores_of(src) if c != src and topo.may_write(c, d)]
+        near = [c for c in own if topo.die(c) == topo.die(src)]
+        far = [c for c in own if topo.die(c) != topo.die(src)]
+        if d == dst:
+            return near[0] if k % 2 == 0 else far[0]
+        k += 1
+    return None
+
+
+def held_order(rank):
+    return [(rank + k) % 4 for k in (0, 1, 3, 2)], [(rank - k) % 4 for k in (0, 1, 3, 2)]
+
+
+def count(mask):
+    return bin(mask).count("1")
+
+
+def off_chip_mask(src, cores, topo):
+    for d in cores:
+        if d != src and topo.may_write(src, d):
+            return topo.mask(src, d)
+    return 0
+
+
+def rank_program(g, core, T, topo):
+    cores = list(T.cores)
+    rank = T.rank_of(core)
+    if rank is None:
+        for a in cores:
+            for b in cores:
+                if a == b or relay_of(a, b, cores, topo) != core:
+                    continue
+                r = T.rank_of(a)
+                m_in = off_chip_mask(a, cores, topo) & topo.mask(a, core)
+                m_out = topo.mask(core, b)
+                rid, pid = topo.addr(b, core)
+                p = NB * held_order(T.rank_of(b))[1].index(r)
+                g.wait_ge(T.sem.rin, count(m_in))
+                g.remote_dma(T.qB[:, p:p + NB], T.land[:], T.sem["arr%d" % r], T.sem.rls, pid, rid, m_out)
+                g.wait_ge(T.sem.rls, count(m_out))
+        return
+
+    Q = {"v": g.vector, "a": g.scalar, "p": g.tensor, "g": g, "s": g.sync}
+    SEM = {"v": "sV", "a": "sA", "p": "sP", "g": "sG"}
+    ops = []
+    rec = {}
+
+    def emit(q, fn, reads, writes, sem=None, cost=0.1, ev=None, after=()):
+        i = len(ops)
+        waits, order = set(after), set()
+        for kind, lst in (("r", reads), ("w", writes)):
+            for b in lst:
+                nm, lo, hi = b[0], b[1], b[2]
+                r = rec.setdefault(nm, [])
+                if nm in BANKS:
+                    for x in r:
+                        if x[3] == i:
+                            continue
+                        if x[2] != q or (x[4] == "w" and q != "p"):
+                            waits.add(x[3])
+                        else:
+                            order.add(x[3])
+                    r[:] = [x for x in r if x[2] == q or x[3] == i]
+                else:
+                    for x in r:
+                        if x[3] != i and x[0] < hi and lo < x[1] and (kind == "w" or x[4] == "w"):
+                            waits.add(x[3])
+                    if kind == "w":
+                        r[:] = [x for x in r if not (lo <= x[0] and x[1] <= hi)]
+                r.append((lo, hi, q, i, kind))
+        ops.append((q, fn, sem, cost, waits, order - waits, ev))
+        return i
+
+    def place():
+        n = len(ops)
+        succ = [[] for _ in ops]
+        need = [0] * n
+        for i in range(n):
+            for d in ops[i][4] | ops[i][5]:
+                succ[d].append(i)
+                need[i] += 1
+        prio = [0.0] * n
+        for i in reversed(range(n)):
+            prio[i] = ops[i][3] + max([prio[j] + (WAKE if i in ops[j][4] else 0.0) for j in succ[i]] + [0.0])
+        at = [0.0] * n
+        ready = [i for i in range(n) if need[i] == 0]
+        free = {}
+        seq = []
+        while ready:
+            st = [max(free.get(ops[i][0], 0.0), at[i]) for i in ready]
+            t = min(st)
+            q = ops[ready[st.index(t)]][0]
+            i = -max((prio[i], -i) for i, x in zip(ready, st) if ops[i][0] == q and x <= t + SLACK)[1]
+            t = max(free.get(q, 0.0), at[i])
+            ready.remove(i)
+            seq.append(i)
+            end = t + ops[i][3]
+            free[q] = t + 0.05 if ops[i][2] is not None else end
+            for j in succ[i]:
+                at[j] = max(at[j], end + WAKE if i in ops[j][4] else t)
+                need[j] -= 1
+                if need[j] == 0:
+                    ready.append(j)
+        return seq
+
+    def issue(seq):
+        cnt = {"v": 0, "a": 0, "p": 0, "g": 0}
+        clock = {q: {} for q in Q}
+        clkat, evs, total = {}, {}, {}
+
+        def see(q, ev):
+            c = clock[q]
+            for s, x in list(clkat.get(ev, {}).items()) + [ev]:
+                if c.get(s, 0) < x:
+                    c[s] = x
+
+        def await_all(q, want):
+            best = {}
+            for s, x in want:
+                best[s] = max(best.get(s, 0), x)
+            todo = [(s, x) for s, x in best.items() if clock[q].get(s, 0) < x]
+            for e in [e for e in todo if not any(o != e and clkat.get(o, {}).get(e[0], 0) >= e[1] for o in todo)]:
+                Q[q].wait_ge(T.sem[e[0]], e[1])
+                see(q, e)
+
+        for i in seq:
+            q, fn, sem, cost, waits, order, ev = ops[i]
+            if fn is None:
+                evs[i] = ev
+                clkat[ev] = {}
+                total[ev[0]] = ev[1]
+                continue
+            await_all(q, [evs[d] for d in waits if evs.get(d) is not None])
+            ins = fn()
+            if ev is not None:
+                total[ev[0]] = total.get(ev[0], 0) + ev[1]
+                continue
+            if sem is None:
+                cnt[q] += 1
+                evs[i] = (SEM[q], cnt[q])
+                ins.then_inc(T.sem[SEM[q]], 1)
+            else:
+                evs[i] = (sem, 16)
+                ins.then_inc(T.sem[sem], 16)
+            total[evs[i][0]] = evs[i][1]
+            c = dict(clock[q])
+            c[evs[i][0]] = evs[i][1]
+            clkat[evs[i]] = c
+        await_all("g", list(total.items()))
+
+    def wide(b):
+        return (b[2] - b[1] + (b[3] - 1 if len(b) > 3 else 0)) // (b[3] if len(b) > 3 else 1)
+
+    def cost(out, ins, two=False):
+        n = wide(out)
+        if two:
+            n *= 1 if any(b[0] in BANKS for b in ins) else 2
+        elif all(SCRATCH[b[0]][2] in ("bfloat16", "uint16") for b in [out] + ins):
+            n /= 2
+        return max(64, n) * CYC + 0.03
+
+    def ap(b):
+        if len(b) > 3:
+            return T[b[0]][:, b[1]:b[2]:b[3]]
+        return T[b[0]][:, b[1]:b[2]]
+
+    def isap(x):
+        return isinstance(x, tuple)
+
+    def tt(out, a, b, op):
+        return emit("v", lambda: g.vector.tensor_tensor(ap(out), ap(a), ap(b), op), [a, b], [out], cost=cost(out, [a, b], True))
+
+    def ts(out, a, s1, op0, s2=None, op1=None):
+        rd = [a] + [s for s in (s1, s2) if isap(s)]
+        x1 = ap(s1) if isap(s1) else s1
+        x2 = ap(s2) if isap(s2) else s2
+        if op1 is None:
+            return emit("v", lambda: g.vector.tensor_scalar(ap(out), ap(a), x1, None, op0), rd, [out], cost=cost(out, [a]))
+        return emit("v", lambda: g.vector.tensor_scalar(ap(out), ap(a), x1, x2, op0, op1), rd, [out], cost=cost(out, [a]))
+
+    def cp(out, a):
+        return emit("v", lambda: g.vector.tensor_copy(ap(out), ap(a)), [a], [out], cost=cost(out, [a]))
+
+    def fill(out, x):
+        return emit("v", lambda: g.vector.memset(ap(out), x), [], [out])
+
+    def act(out, a, fn, bias=0.0, scale=1.0, accum=None):
+        rd = [a] + [s for s in (bias, scale) if isap(s)]
+        kw = {}
+        if isap(bias) or bias != 0.0:
+            kw["bias"] = ap(bias) if isap(bias) else bias
+        if isap(scale) or scale != 1.0:
+            kw["scale"] = ap(scale) if isap(scale) else scale
+        wr = [out]
+        if accum is not None:
+            kw["accum_out"] = ap(accum)
+            wr = [out, accum]
+        return emit("a", lambda: g.scalar.activation(ap(out), ap(a), fn, **kw), rd, wr, cost=wide(out) * CYC + 0.05)
+
+    def mm(seq, reads, writes):
+        def go():
+            ins = None
+            for o, l, r, st, sp in seq:
+                ins = g.tensor.matmul(ap(o), ap(l), ap(r), st, sp)
+            return ins
+        return emit("p", go, reads, writes, cost=sum(max(64, wide(o)) for o, l, r, st, sp in seq) * PEC + 0.03)
+
+    def LJ(nm, j):
+        return (nm, 128 * j, 128 * j + 128)
+
+    def M(nm):
+        return (nm, 0, 128)
+
+    def full(nm):
+        return (nm, 0, 2048)
+
+    def word(nm, out, src, base, w, extra=None, strided=True):
+        seq = []
+        if extra is not None:
+            seq.append((out, extra[0], extra[1], True, False))
+        for j in range(16):
+            r = (src, base + j, base + 16 * w, 16) if strided else (src, base + w * j, base + w * (j + 1))
+            seq.append((out, LJ(nm, j), r, extra is None and j == 0, j == 15))
+        rd = [full(nm), (src, base, base + 16 * w)]
+        if extra is not None:
+            rd += [extra[0], extra[1]]
+        return mm(seq, rd, [out])
+
+    goes, came = held_order(rank)
+    emit("a", lambda: g.scalar.dma_start(ap(("wS", 0, 2)), T.wt[:]), [], [("wS", 0, 2)], "dw", 2.0)
+    for p in range(4):
+        b = ("qN", NB * p, NB * p + NB)
+        emit("s", lambda b=b, x=NB * goes[p]: g.sync.dma_start(ap(b), T.qs[:, x:x + NB]), [], [b], "dq%d" % p, 2.5 + 0.5 * p)
+    emit("a", lambda: g.scalar.dma_start(ap(("mkT", 0, 2048)), T.mk[:, 0:2048]), [], [("mkT", 0, 2048)], "dm0", 7.0)
+    emit("s", lambda: g.sync.dma_start(ap(("mkT", 2048, W)), T.mk[:, 2048:W]), [], [("mkT", 2048, W)], "dm1", 7.0)
+
+    def C(i):
+        return ("col", i, i + 1)
+    KC, PB, NBI, LBI, WN, KP1, RCOL, KK, T0, T1, R120 = [C(i) for i in range(11)]
+    RC = [C(12 + r) for r in range(4)]
+    KJ = [C(16 + J) for J in range(6)]
+    KLT = C(22)
+    T2, T3, T4, T5 = [C(24 + i) for i in range(4)]
+
+    def iota(out, pattern, base, cm, flag=True):
+        if flag:
+            return emit("g", lambda: g.iota(ap(out), pattern, base, cm, allow_small_or_imprecise_dtypes=True), [], [out])
+        return emit("g", lambda: g.iota(ap(out), pattern, base, cm), [], [out])
+
+    def pick(out, a, pattern, op, x, base, cm):
+        return emit("g", lambda: g.affine_select(ap(out), ap(a), pattern, op, x, base, cm), [a], [out],
+                    cost=0.17 + 2 * wide(out) * CYC)
+
+    iota(("pi", 0, 1), [[0, 1]], 0, 1, False)
+    iota(M("JR"), [[0, 8], [1, 16]], 0, 0)
+    pick(M("JA"), M("JR"), [[-16, 8], [0, 16]], Op.is_ge, 99.0, 0, 1)
+    pick(M("JP"), M("JA"), [[16, 8], [0, 16]], Op.is_ge, 99.0, 15, -1)
+    ts(("ki", 0, 1), ("pi", 0, 1), 15, Op.bitwise_and)
+    cp(KC, ("ki", 0, 1))
+    ts(PB, KC, 256.0, Op.mult)
+    ts(NBI, KC, -256.0, Op.mult)
+    for r in range(4):
+        ts(RC[r], KC, float(12 + r), Op.is_equal)
+    ts(M("ID"), M("JP"), KC, Op.is_equal)
+    ts(M("BD"), M("JP"), 15.5, Op.is_le)
+    ts(M("R0"), M("BD"), RC[0], Op.mult, 256.0, Op.mult)
+    for j in range(16):
+        ts(LJ("BIG", j), M("JP"), float(j), Op.is_equal)
+    ts(full("LX"), full("BIG"), ("wS", 0, 1), Op.mult)
+    ts(full("LY"), full("BIG"), ("wS", 1, 2), Op.mult)
+    act(full("LV0"), full("BIG"), Fn.Copy, scale=RC[0])
+    for r in (1, 2):
+        pick(full("LV%d" % r), full("BIG"), [[0, 16], [-16, 8], [0, 16]], Op.is_equal, 0.0, -12 - r, 1)
+    iota(M("SRC"), [[0, 8], [1, 4], [1, 4]], 13, 0)
+    iota(("IT", 0, 96), [[1, 96]], 0, 0)
+    iota(("w1", 0, 12), [[0, 2], [16, 6]], W, 0)
+
+    def consts_search():
+        ts(("E256", 0, 16), ("JR", 0, 16), KC, Op.is_equal, 256.0, Op.mult)
+        fill(("geo", 0, 16), 1.0 / 256)
+        fill(("geo", 16, 32), 0.0)
+        emit("v", lambda: g.vector.tensor_tensor_scan(ap(("geo", 32, 48)), ap(("geo", 0, 16)), ap(("geo", 16, 32)), -128.0,
+                                                      Op.mult, Op.add), [("geo", 0, 32)], [("geo", 32, 48)])
+        tt(("geo", 48, 60), ("geo", 32, 44), ("E256", 0, 12), Op.mult)
+        emit("v", lambda: g.vector.tensor_reduce(ap(WN), ap(("geo", 48, 60)), AxisListType.X, Op.add), [("geo", 48, 60)], [WN])
+        ts(full("LN"), full("BIG"), WN, Op.mult, 1.0 / 256, Op.mult)
+        ts(full("LV3"), full("BIG"), RC[3], Op.mult)
+        ts(M("NI"), M("ID"), -1.0, Op.mult)
+        for j in range(16):
+            ts(LJ("LB", j), M("BD"), ("E256", j, j + 1), Op.mult)
+        ts(M("HI"), M("ID"), 0.5, Op.mult)
+        ts(T0, KC, 11.5, Op.is_gt, -100000.0, Op.mult)
+        ts(T1, NBI, 128.0, Op.subtract)
+        tt(LBI, T0, T1, Op.add)
+        fill(("mkT", W, MKW), 0.0)
+
+    def consts_edits():
+        ts(KLT, KC, 11.5, Op.is_lt)
+        ts(M("ISY"), M("ID"), KLT, Op.mult)
+        ts(M("CAQ"), M("SRC"), KC, Op.is_equal)
+        tt(M("CA"), M("CAQ"), M("BD"), Op.mult)
+        ts(("ci", 0, 1), ("ki", 0, 1), 3, Op.bitwise_and)
+        ts(T2, KC, 11.5, Op.is_gt, 50.0, Op.mult)
+        ts(T3, ("ci", 0, 1), 12.0, Op.add)
+        tt(RCOL, T2, T3, Op.add)
+        ts(M("RS"), M("JP"), RCOL, Op.is_equal)
+        ts(("ci", 1, 2), ("ki", 0, 1), 2, Op.arith_shift_right)
+        ts(KK, ("ci", 1, 2), -256.0, Op.mult, 768.0, Op.add)
+        ts(T4, KC, 11.5, Op.is_lt, 50.0, Op.mult)
+        ts(T5, KC, 1.0, Op.add)
+        tt(KP1, T4, T5, Op.add)
+        ts(M("DN"), M("JP"), KP1, Op.is_equal)
+        ts(R120, RC[0], 1.0 / 256, Op.mult)
+        ts(M("R12"), M("ID"), R120, Op.mult)
+        ts(("DU", 0, 12), ("w1", 0, 12), KC, Op.add)
+        for J in range(6):
+            ts(KJ[J], KC, 16.0 * J, Op.add)
+            ts(("LM", 96 * J, 96 * J + 96), ("IT", 0, 96), KJ[J], Op.is_lt)
+
+    def sm(nm, c, k=0, n=1):
+        lo = c * NJ * n + k * NJ
+        return (nm, lo, lo + NJ)
+
+    def half(nm, c, h):
+        lo = c * CH + h * NB
+        return (nm, lo, lo + NB)
+
+    def chunk(nm, c):
+        return (nm, c * CH, c * CH + CH)
+
+    def gb(c, h):
+        return "g%d%d" % (c, h)
+
+    def jmajor(c, src):
+        for h, bk in ((0, "h%d" % c), (1, "k%d" % c)):
+            seq = []
+            for x in range(8):
+                seq.append(((bk, x * NJ, x * NJ + NJ), M("ID"), (src, c * CH + 8 * h + x, c * CH + CH, 16), True, True))
+            mm(seq, [M("ID"), chunk(src, c)], [(bk, 0, NB)])
+            act(half("qj", c, h), (bk, 0, NB), Fn.Identity, bias=PB)
+
+    def lengths(c, src, rs):
+        for r in rs:
+            word("LV%d" % r, ("k%d" % c, r * NJ, r * NJ + NJ), src, c * CH, NJ)
+        lo, hi = rs[0] * NJ, rs[-1] * NJ + NJ
+        act(("Aw", c * 192 + lo, c * 192 + hi), ("k%d" % c, lo, hi), Fn.Copy)
+
+    def P1(c, s, src):
+        m = sm("Aw", c, s - 1, 4)
+        for h in range(2):
+            seq = []
+            for x in range(8):
+                j = 8 * h + x
+                o = (gb(c, h), x * NJ, x * NJ + NJ)
+                if s == 1:
+                    seq.append((o, M("R0"), (src, c * CH + j, c * CH + CH, 16), True, True))
+                else:
+                    seq.append((o, LJ("LB", j), m, True, True))
+            mm(seq, [M("R0"), chunk(src, c)] if s == 1 else [full("LB"), m], [(gb(c, h), 0, NB)])
+
+    def V1(c):
+        for h in range(2):
+            tt(half("zp", c, h), half("qj", c, h), (gb(c, h), 0, NB), Op.min)
+
+    def A1(c):
+        for h in range(2):
+            act(half("zz", c, h), half("zp", c, h), Fn.Relu, bias=NBI)
+
+    def A2(c, s):
+        m = sm("Aw", c, s - 1, 4)
+        act(sm("m97", c), m, Fn.Copy, scale=97.0)
+        act(sm("th", c), m, Fn.Silu, scale=-LN256)
+        act(sm("mt", c, s % 2, 2), m, Fn.Copy, bias=8192.0 + 65536.0 * s, scale=4096.0)
+
+    def P2(c):
+        word("LX", ("h%d" % c, 0, NJ), "zz", c * CH, NJ, strided=False)
+        word("LY", ("h%d" % c, NJ, 2 * NJ), "zz", c * CH, NJ, strided=False)
+
+    def V2(c):
+        hb, o = "h%d" % c, c * 3 * NJ
+        cp(("U", o, o + 2 * NJ), (hb, 0, 2 * NJ))
+        tt(sm("U", c, 2, 3), (hb, NJ, 2 * NJ), sm("m97", c), Op.add)
+        ts(("UA", o, o + 3 * NJ), ("U", o, o + 3 * NJ), 4095, Op.bitwise_and)
+        tt(sm("P", c), sm("UA", c, 0, 3), sm("UA", c, 1, 3), Op.mult)
+        ts(sm("Wd", c), sm("UA", c, 2, 3), 32.0, Op.mult, -131072.0, Op.add)
+        tt(sm("S", c), sm("P", c), sm("Wd", c), Op.add)
+        ts(sm("H", c), sm("S", c), 5, Op.arith_shift_right, 4095, Op.bitwise_and)
+        cp(sm("OFF", c), sm("H", c))
+
+    def win(off, w=W):
+        return T.mkT[:, 0:w].indirect(ap(off))
+
+    def gathered(o, off, q, op):
+        emit("v", lambda: g.vector.tensor_tensor(ap(o), win(off), ap(q), op), [("mkT", 0, W), off, q], [o],
+             cost=0.08 + 1.5 * CYC * wide(o))
+
+    def A3(c):
+        o, off = chunk("vv", c), sm("OFF", c)
+        emit("a", lambda: g.scalar.activation(ap(o), win(off), Fn.Copy), [("mkT", 0, W), off], [o],
+             cost=0.1 + 1.5 * CYC * wide(o))
+
+    def held(c, w):
+        return ("k%d" % c, NJ, 2 * NJ) if w == 0 else ("h%d" % c, (w - 1) * NJ, w * NJ)
+
+    def P4(c, s):
+        for w in range(4 - s):
+            word("LV%d" % w, held(c, w), "vv", c * CH, NJ, extra=(M("NI"), sm("Aw", c, s + w, 4)))
+
+    def V4(c, s):
+        hit, code = sm("hitS", c, s - 1, 4), sm("codeS", c, s - 1, 4)
+        tt(code, sm("H", c), sm("mt", c, s % 2, 2), Op.add)
+        tt(hit, ("k%d" % c, 0, NJ), sm("th", c), Op.is_gt)
+        for w in range(4 - s):
+            t = ("tm", c * 144 + w * NJ, c * 144 + w * NJ + NJ)
+            tt(t, held(c, w), hit, Op.mult)
+            tt(sm("Aw", c, s + w, 4), sm("Aw", c, s + w, 4), t, Op.add)
+        tt(sm("B" if s == 1 else "ch", c), code, hit, Op.mult)
+        if s > 1:
+            tt(sm("B", c), sm("B", c), sm("ch", c), Op.max)
+
+    def La(c, src):
+        ts(sm("Li", c), sm("B", c), 12, Op.arith_shift_right, 15, Op.bitwise_and)
+        ts(sm("Hb", c), sm("B", c), 4095, Op.bitwise_and)
+        cp(sm("Lb", c), sm("Li", c))
+        cp(sm("OB", c), sm("Hb", c))
+        for h in range(2):
+            r = ("Lb", c * NJ + 24 * h, c * NJ + 24 * h + 24)
+            bk = (gb(c, h), 0, NB)
+            mm([((gb(c, h), j, NB, 16), LJ("LB", j), r, True, True) for j in range(16)], [full("LB"), r], [bk])
+            act(bk, bk, Fn.Sign, bias=LBI)
+            gathered(half("dd", c, h), ("OB", c * NJ + 24 * h, c * NJ + 24 * h + 24), half(src, c, h), Op.subtract)
+
+    def Lb(c, h, src, to):
+        bk, d, sd, q = (gb(c, h), 0, NB), half("dd", c, h), half("sd", c, h), half(src, c, h)
+        tt(sd, d, bk, Op.mult)
+        mm([(bk, M("ID"), q, True, False), (bk, M("HI"), d, False, False), (bk, M("HI"), sd, False, True)],
+           [M("ID"), M("HI"), q, d, sd], [bk])
+        act(half(to, c, h), bk, Fn.Copy)
+
+    def search(src):
+        for s in range(1, 5):
+            for c in range(2):
+                if s == 1:
+                    jmajor(c, src)
+                P1(c, s, src)
+                if s == 1:
+                    lengths(c, src, [0])
+                A2(c, s)
+                V1(c)
+                A1(c)
+                P2(c)
+                if s == 1:
+                    lengths(c, src, [1, 2, 3])
+                V2(c)
+                gathered(chunk("nn", c), sm("OFF", c), chunk(src, c), Op.not_equal)
+                if s < 4:
+                    A3(c)
+                word("LN", ("k%d" % c, 0, NJ), "nn", c * CH, NJ)
+                P4(c, s)
+                V4(c, s)
+
+    def close(src, dest, after):
+        for c in range(2):
+            La(c, src)
+            for h in range(2):
+                Lb(c, h, src, dest(2 * c + h))
+                after(2 * c + h)
+
+    omask = off_chip_mask(core, cores, topo)
+    sends = []
+
+    def send(p):
+        s = goes[p]
+        if s == rank:
+            return
+        b = ("qA", NB * p, NB * p + NB)
+        rel = relay_of(core, cores[s], cores, topo)
+        to = cores[s] if rel is None else rel
+        m = omask & topo.mask(core, to)
+        rid, pid = topo.addr(to, core)
+        x = NB * held_order(s)[1].index(rank)
+        dst, sem = (T.land[:], "rin") if rel is not None else (T.qB[:, x:x + NB], "arr%d" % rank)
+        sends.append(emit("g", lambda: g.remote_dma(dst, ap(b), T.sem[sem], T.sem.sent, pid, rid, m), [b], [], None, 0.3,
+                          ("sent", count(m))))
+
+    def arrivals():
+        for p in range(4):
+            s = came[p]
+            if s != rank:
+                rel = relay_of(cores[s], core, cores, topo)
+                n = count(topo.mask(cores[s] if rel is None else rel, core))
+                emit("x%d" % s, None, [], [("qB", NB * p, NB * p + NB)], None, 4.0 if rel is None else 8.0, ("arr%d" % s, n),
+                     sends[:1] if p < 2 else sends)
+
+    def edits(src):
+        e = goes.index(0)
+        w0, h0 = 192 * (e // 2), 24 * (e % 2)
+        qe, de, Bb = (src, NB * e, NB * e + 96), ("dd", NB * e, NB * e + 96), ("B", 24 * e, 24 * e + 6)
+        fk = [("fc", NJ * k + h0, NJ * k + h0 + 6) for k in range(4)]
+        ts(("al", 0, 192), ("Aw", w0, w0 + 192), 0.0, Op.is_gt)
+        tt(("ms", 0, 192), ("al", 0, 192), ("hitS", w0, w0 + 192), Op.subtract)
+        tt(("fc", 0, 192), ("codeS", w0, w0 + 192), ("ms", 0, 192), Op.mult)
+        tt(("f1", 0, 6), fk[0], fk[1], Op.max)
+        tt(("f1", 8, 14), fk[2], fk[3], Op.max)
+        F = ("FB", 0, 6)
+        tt(F, ("f1", 0, 6), ("f1", 8, 14), Op.max)
+        cp(("FB", 6, 12), Bb)
+        tt(("ed", 0, 6), F, Bb, Op.is_gt)
+        ts(("ed", 8, 14), Bb, 0.0, Op.is_gt)
+        ts(("cl", 0, 12), ("FB", 0, 12), 4095, Op.bitwise_and)
+        ts(("si", 0, 6), F, 12, Op.arith_shift_right, 15, Op.bitwise_and)
+        ts(("si", 8, 14), Bb, 16, Op.arith_shift_right)
+        for o in (0, 6):
+            tt(("ed2", o, o + 6), ("ed", 0, 6), ("ed", 8, 14), Op.mult)
+        ts(("nk", 0, 12), ("ed2", 0, 12), -8192.0, Op.mult, 8192.0, Op.add)
+        tt(("key", 0, 12), ("cl", 0, 12), ("nk", 0, 12), Op.add)
+        ts(("key1", 0, 12), ("key", 0, 12), 1.0, Op.add)
+        ts(("kh", 0, 12), ("key", 0, 12), 6, Op.arith_shift_right)
+        ts(("kh", 12, 24), ("key", 0, 12), 63, Op.bitwise_and)
+        ts(("khb", 0, 12), ("kh", 0, 12), 0.25, Op.mult)
+        ts(("khb", 16, 28), ("kh", 12, 24), 1.0 / 256, Op.mult)
+        ts(("sb", 0, 6), ("si", 0, 6), -2.0, Op.add)
+        cp(("sb", 8, 14), ("si", 8, 14))
+        seq = []
+        for j in range(16):
+            o = ("h0", j, 192, 16)
+            seq += [(o, LJ("LB", j), ("khb", 0, 12), True, False), (o, LJ("LB", j), ("khb", 16, 28), False, True)]
+        mm(seq, [full("LB"), ("khb", 0, 12), ("khb", 16, 28)], [("h0", 0, 192)])
+        mm([(("k0", j, 96, 16), LJ("LB", j), ("sb", 8, 14), True, True) for j in range(16)],
+           [full("LB"), ("sb", 8, 14)], [("k0", 0, 96)])
+        mm([(("k1", j, 96, 16), LJ("LB", j), ("sb", 0, 6), True, True) for j in range(16)],
+           [full("LB"), ("sb", 0, 6)], [("k1", 0, 96)])
+        mm([(("h1", 0, 96), M("CA"), de, True, False), (("h1", 0, 96), M("CA"), qe, False, True)],
+           [M("CA"), de, qe], [("h1", 0, 96)])
+        for x in range(12):
+            J = x % 6
+            act(("LK", 96 * x, 96 * x + 96), ("LM", 96 * J, 96 * J + 96), Fn.Copy, bias=-1.0, scale=("key1", x, x + 1))
+        act(("mf", 0, 96), ("k1", 0, 96), Fn.Copy)
+        ts(("mk1", 0, 96), ("k0", 0, 96), KK, Op.is_equal)
+        tt(("cm", 0, 96), ("h1", 0, 96), ("mk1", 0, 96), Op.mult)
+        mm([(("k0", 0, 96), M("ISY"), qe, True, False), (("k0", 0, 96), M("RS"), ("cm", 0, 96), False, True)],
+           [M("ISY"), M("RS"), qe, ("cm", 0, 96)], [("k0", 0, 96)])
+        for x in range(12):
+            w = x // 6
+            eq = ("EQ", 96 * x, 96 * x + 96)
+            tt(eq, ("LK", 96 * x, 96 * x + 96), ("h0", 96 * w, 96 * w + 96), Op.is_equal)
+            act(eq, eq, Fn.Copy, accum=("CNT", x, x + 1))
+        cp(("Eb", 0, 96), ("k0", 0, 96))
+        ts(("w1", 12, 24), ("CNT", 0, 12), 0.0, Op.is_equal)
+        tt(("w1", 24, 36), ("cl", 0, 12), ("DU", 0, 12), Op.subtract)
+        tt(("w1", 36, 48), ("w1", 12, 24), ("ed2", 0, 12), Op.mult)
+        tt(("w1", 48, 60), ("w1", 24, 36), ("w1", 36, 48), Op.mult)
+        tt(("w1", 12, 24), ("w1", 48, 60), ("DU", 0, 12), Op.add)
+        cp(("OE", 0, 12), ("w1", 12, 24))
+        oF, oB, full_w = ("OE", 0, 6), ("OE", 6, 12), ("mkT", 0, MKW)
+        emit("v", lambda: g.vector.tensor_copy(win(oF, MKW), ap(("Eb", 0, 96))), [oF, ("Eb", 0, 96)], [full_w], cost=0.35)
+        emit("v", lambda: g.vector.tensor_copy(ap(("vb", 0, 96)), win(oB, MKW)), [oB, full_w], [("vb", 0, 96)], cost=0.2)
+        mm([(("h1", 0, 96), M("ISY"), ("vb", 0, 96), True, False), (("h1", 0, 96), M("DN"), ("vb", 0, 96), False, False),
+            (("h1", 0, 96), M("R12"), ("mf", 0, 96), False, True)],
+           [M("ISY"), M("DN"), M("R12"), ("vb", 0, 96), ("mf", 0, 96)], [("h1", 0, 96)])
+        cp(("Sb", 0, 96), ("h1", 0, 96))
+        emit("v", lambda: g.vector.tensor_copy(win(oB, MKW), ap(("Sb", 0, 96))), [oB, ("Sb", 0, 96)], [full_w], cost=0.35)
+
+    consts_search()
+    search("qN")
+    close("qN", lambda p: "qB" if goes[p] == rank else "qA", send)
+    consts_edits()
+    edits("qN")
+    arrivals()
+    search("qB")
+
+    def out(p):
+        b, x = ("qF", NB * p, NB * p + NB), NB * came[p]
+        emit("s", lambda: g.sync.dma_start(T.yq[:, x:x + NB], ap(b)), [b], [], "dy%d" % p, 2.5)
+
+    for c in range(2):
+        ts(sm("y1", c), sm("B", c), 0.0, Op.is_gt)
+        ts(sm("y0", c), sm("B", c), 4095, Op.bitwise_and)
+        ts(sm("y2", c), sm("y0", c), 1.0, Op.add)
+        tt(sm("y3", c), sm("y1", c), sm("y2", c), Op.mult)
+        ts(sm("yS", c), sm("y3", c), -1.0, Op.add)
+        for p in (2 * c, 2 * c + 1):
+            b, x = ("yS", 24 * p, 24 * p + 24), 24 * came[p]
+            emit("s", lambda b=b, x=x: g.sync.dma_start(T.yb[:, x:x + 24], ap(b)), [b], [], "db%d" % p, 2.5)
+    close("qB", lambda p: "qF", out)
+    issue(place())

@@ -1,20 +1,23 @@
+import math
 from concourse.mybir import AluOpType as Op, ActivationFunctionType as Fn, AxisListType
 
 W, K, NB = 4096, 1536, 384
 CH, NJ = 768, 48
 MKW = W + 128
-LN256 = 5.545177444479562
+LN2 = math.log(2.0)
+MO = 136.0
 CYC, PEC, WAKE, SLACK = 0.00083, 0.00042, 0.17, 0.04
+GAT = 1.5
 
-_sets = ["LX", "LY", "LN", "LV0", "LV1", "LV2", "LV3", "LB", "BIG"]
-_mats = ["JR", "JA", "JP", "BD", "ID", "HI", "NI", "R0", "ISY", "SRC", "CAQ", "CA", "RS", "DN", "R12"]
-SCRATCH = {"mkT": ("sbuf", [128, MKW], "bfloat16"), "land": ("sbuf", [128, NB], "bfloat16")}
-for _n in ("qN", "qA", "qB", "qF", "zz", "nn", "vv", "dd", "sd"):
+_words = ["XP", "ZX", "ZY", "ZS", "ZL", "ZH", "ZN", "Z1", "Z2"]
+_mats = ["AB", "ONE", "ID", "NI", "I16", "N16", "R0", "ISY", "SRC", "CAQ", "BD", "CA", "JP", "RS", "DN", "R12"]
+SCRATCH = {"mkT": ("sbuf", [128, MKW], "bfloat16"), "LB": ("sbuf", [128, 2048], "bfloat16")}
+for _n in ("qN", "q0", "q1", "qO", "dR", "dS", "dF", "qF", "qj", "zz", "nn", "dd", "rr"):
     SCRATCH[_n] = ("sbuf", [128, K], "bfloat16")
-for _n in ("qj", "zp"):
+for _n in ("qv", "zp"):
     SCRATCH[_n] = ("sbuf", [128, K], "float32")
-for _n in _sets:
-    SCRATCH[_n] = ("sbuf", [128, 2048], "bfloat16")
+for _n in _words:
+    SCRATCH[_n] = ("sbuf", [128, 144], "bfloat16")
 for _n in _mats:
     SCRATCH[_n] = ("sbuf", [128, 128], "bfloat16")
 
@@ -24,17 +27,19 @@ def _add(dtype, **widths):
         SCRATCH[n] = ("sbuf", [128, w], dtype)
 
 
-_add("bfloat16", wS=2, Aw=384, tm=288, Lb=96, khb=32, sb=16, cm=96, Eb=96, vb=96, mf=96, Sb=96)
-_add("int32", pi=1, ki=1, ci=4, U=288, UA=288, P=96, Wd=96, S=96, H=96, codeS=384, ch=96, B=96, Hb=96, Li=96, y0=96,
-     fc=192, f1=32, FB=12, cl=12, key=12, kh=24, si=16)
-_add("float32", col=32, E256=16, geo=64, IT=96, LM=576, DU=12, hitS=384, th=96, m97=96, mt=192, y1=96, y2=96, y3=96, yS=96,
+_add("bfloat16", wK=2, wS=2, land0=NB, land1=NB, JR=96, LT=96, mo=768, Rb=192, rest=96, m256=96, Cw=192, dead=192, khb=32, sb=16,
+     cm=96, Eb=96, vb=96, mf=96, Sb=96)
+_add("int32", pi=1, ki=1, ci=4, U=288, UA=288, P=96, Wd=96, S=96, H=96, Bi=96, Hb=96, fc=192, f1=32, FB=12, cl=12, key=12,
+     kh=24, si=16)
+_add("float32", col=40, E16=16, geo=32, IT=96, LM=576, DU=12, HT=768, XB=960, Rf=192, m97=192, mt=192, Bm=96, yS=96,
      al=192, ms=192, ed=32, ed2=12, nk=12, key1=12, LK=1152, EQ=1152, CNT=12, w1=64, mk1=96)
-_add("uint16", OFF=96, OB=96, OE=12)
+_add("uint16", OFF=96, OB=96, OL=96, OE=12)
 BANKS = ("g00", "g01", "g10", "g11", "h0", "h1", "k0", "k1")
 for _n in BANKS:
     SCRATCH[_n] = ("psum", [128, 512], "float32")
-SEMAPHORES = ["sV", "sA", "sP", "sG", "dw", "dq0", "dq1", "dq2", "dq3", "dm0", "dm1", "dy0", "dy1", "dy2", "dy3",
-              "db0", "db1", "db2", "db3", "arr0", "arr1", "arr2", "arr3", "sent", "rin", "rls"]
+SEMAPHORES = ["sV", "sA", "sP", "sG", "dw", "dq0", "dq1", "dq2", "dq3", "dq4", "dm0", "dm1", "dy0", "dy1", "dy2", "dy3",
+              "db0", "db1", "db2", "db3", "sent", "rin0", "rin1", "rls"]
+SEMAPHORES += ["arr%d%d" % (_k, _r) for _k in range(2) for _r in range(4)]
 
 
 def relay_of(src, dst, cores, topo):
@@ -53,19 +58,18 @@ def relay_of(src, dst, cores, topo):
     return None
 
 
-def held_order(rank):
-    return [(rank + k) % 4 for k in (0, 1, 3, 2)], [(rank - k) % 4 for k in (0, 1, 3, 2)]
+def held_order(rank, cores, topo):
+    me = cores[rank]
+    far = [s for s in range(len(cores)) if s != rank and not topo.may_write(me, cores[s])]
+    near = [s for s in range(len(cores)) if s != rank and topo.may_write(me, cores[s])]
+    return far + near + [rank]
 
 
 def count(mask):
     return bin(mask).count("1")
 
 
-def off_chip_mask(src, cores, topo):
-    for d in cores:
-        if d != src and topo.may_write(src, d):
-            return topo.mask(src, d)
-    return 0
+LANDS = ("qO", "dR")
 
 
 def rank_program(g, core, T, topo):
@@ -77,13 +81,14 @@ def rank_program(g, core, T, topo):
                 if a == b or relay_of(a, b, cores, topo) != core:
                     continue
                 r = T.rank_of(a)
-                m_in = off_chip_mask(a, cores, topo) & topo.mask(a, core)
                 m_out = topo.mask(core, b)
                 rid, pid = topo.addr(b, core)
-                p = NB * held_order(T.rank_of(b))[1].index(r)
-                g.wait_ge(T.sem.rin, count(m_in))
-                g.remote_dma(T.qB[:, p:p + NB], T.land[:], T.sem["arr%d" % r], T.sem.rls, pid, rid, m_out)
-                g.wait_ge(T.sem.rls, count(m_out))
+                p = NB * held_order(T.rank_of(b), cores, topo).index(r)
+                for k in range(2):
+                    g.wait_ge(T.sem["rin%d" % k], count(topo.mask(a, core)))
+                    g.remote_dma(T[LANDS[k]][:, p:p + NB], T["land%d" % k][:], T.sem["arr%d%d" % (k, r)], T.sem.rls, pid, rid,
+                                 m_out)
+                g.wait_ge(T.sem.rls, 2 * count(m_out))
         return
 
     Q = {"v": g.vector, "a": g.scalar, "p": g.tensor, "g": g, "s": g.sync}
@@ -91,9 +96,9 @@ def rank_program(g, core, T, topo):
     ops = []
     rec = {}
 
-    def emit(q, fn, reads, writes, sem=None, cost=0.1, ev=None, after=()):
+    def emit(q, fn, reads, writes, sem=None, cost=0.1, ev=None, after=(), behind=()):
         i = len(ops)
-        waits, order = set(after), set()
+        waits, order = set(after), set(behind)
         for kind, lst in (("r", reads), ("w", writes)):
             for b in lst:
                 nm, lo, hi = b[0], b[1], b[2]
@@ -228,9 +233,13 @@ def rank_program(g, core, T, topo):
         return emit("v", lambda: g.vector.tensor_copy(ap(out), ap(a)), [a], [out], cost=cost(out, [a]))
 
     def fill(out, x):
-        return emit("v", lambda: g.vector.memset(ap(out), x), [], [out])
+        return emit("v", lambda: g.vector.memset(ap(out), x), [], [out], cost=cost(out, []))
 
-    def act(out, a, fn, bias=0.0, scale=1.0, accum=None):
+    def scan(out, d0, d1, op1):
+        return emit("v", lambda: g.vector.tensor_tensor_scan(ap(out), ap(d0), ap(d1), 0.0, Op.mult, op1), [d0, d1], [out],
+                    cost=cost(out, [d0, d1]))
+
+    def act(out, a, fn, bias=0.0, scale=1.0, accum=None, more=0.0):
         rd = [a] + [s for s in (bias, scale) if isap(s)]
         kw = {}
         if isap(bias) or bias != 0.0:
@@ -241,123 +250,130 @@ def rank_program(g, core, T, topo):
         if accum is not None:
             kw["accum_out"] = ap(accum)
             wr = [out, accum]
-        return emit("a", lambda: g.scalar.activation(ap(out), ap(a), fn, **kw), rd, wr, cost=wide(out) * CYC + 0.05)
+        return emit("a", lambda: g.scalar.activation(ap(out), ap(a), fn, **kw), rd, wr, cost=wide(out) * CYC + 0.05 + more)
 
-    def mm(seq, reads, writes):
+    def mm(seq):
         def go():
             ins = None
             for o, l, r, st, sp in seq:
                 ins = g.tensor.matmul(ap(o), ap(l), ap(r), st, sp)
             return ins
-        return emit("p", go, reads, writes, cost=sum(max(64, wide(o)) for o, l, r, st, sp in seq) * PEC + 0.03)
+        reads = sorted(set(x[1][:3] for x in seq) | set(x[2][:3] for x in seq))
+        return emit("p", go, reads, [seq[0][0]], cost=sum(max(64, wide(x[0])) for x in seq) * PEC + 0.03)
 
-    def LJ(nm, j):
-        return (nm, 128 * j, 128 * j + 128)
+    def LJ(j):
+        return ("LB", 128 * j, 128 * j + 128)
 
     def M(nm):
         return (nm, 0, 128)
 
-    def full(nm):
-        return (nm, 0, 2048)
-
-    def word(nm, out, src, base, w, extra=None, strided=True):
+    def word(nm, out, src, base, strided=True, start=True, stop=True, js=range(16)):
         seq = []
-        if extra is not None:
-            seq.append((out, extra[0], extra[1], True, False))
-        for j in range(16):
-            r = (src, base + j, base + 16 * w, 16) if strided else (src, base + w * j, base + w * (j + 1))
-            seq.append((out, LJ(nm, j), r, extra is None and j == 0, j == 15))
-        rd = [full(nm), (src, base, base + 16 * w)]
-        if extra is not None:
-            rd += [extra[0], extra[1]]
-        return mm(seq, rd, [out])
+        for j in js:
+            r = (src, base + j, base + CH, 16) if strided else (src, base + NJ * j, base + NJ * (j + 1))
+            seq.append((out, (nm, 15 - j, 143 - j), r, start and j == js[0], stop and j == js[-1]))
+        return mm(seq)
 
-    goes, came = held_order(rank)
+    held = held_order(rank, cores, topo)
+    loads = []
+
+    def load(b, src, sem, t):
+        loads.append(emit("s", lambda: g.sync.dma_start(ap(b), src), [], [b], sem, t, behind=loads[-1:]))
+        return loads[-1]
+
     emit("a", lambda: g.scalar.dma_start(ap(("wS", 0, 2)), T.wt[:]), [], [("wS", 0, 2)], "dw", 2.0)
     for p in range(4):
-        b = ("qN", NB * p, NB * p + NB)
-        emit("s", lambda b=b, x=NB * goes[p]: g.sync.dma_start(ap(b), T.qs[:, x:x + NB]), [], [b], "dq%d" % p, 2.5 + 0.5 * p)
-    emit("a", lambda: g.scalar.dma_start(ap(("mkT", 0, 2048)), T.mk[:, 0:2048]), [], [("mkT", 0, 2048)], "dm0", 7.0)
-    emit("s", lambda: g.sync.dma_start(ap(("mkT", 2048, W)), T.mk[:, 2048:W]), [], [("mkT", 2048, W)], "dm1", 7.0)
+        load(("qN", NB * p, NB * p + NB), T.qs[:, NB * held[p]:NB * held[p] + NB], "dq%d" % p, 2.4 + 0.4 * p)
+    tab = [load(("mkT", x, x + W // 2), T.mk[:, x:x + W // 2], "dm%d" % (2 * x // W), 7.0) for x in (0, W // 2)]
+    load(("qO", 3 * NB, K), T.qs[:, NB * rank:NB * rank + NB], "dq4", 7.5)
 
     def C(i):
         return ("col", i, i + 1)
-    KC, PB, NBI, LBI, WN, KP1, RCOL, KK, T0, T1, R120 = [C(i) for i in range(11)]
-    RC = [C(12 + r) for r in range(4)]
+    KC, K15, KA, KLT, NBI, B1, QB, RB, WS, WE, W2, WN, KP1, RCOL, KK = [C(i) for i in range(15)]
     KJ = [C(16 + J) for J in range(6)]
-    KLT = C(22)
-    T2, T3, T4, T5 = [C(24 + i) for i in range(4)]
+    T2, T3, T4, T5, M15 = [C(24 + i) for i in range(5)]
+    RC0, W1, WH = ("E16", 12, 13), ("geo", 10, 11), ("geo", 14, 15)
 
     def iota(out, pattern, base, cm, flag=True):
+        c = 0.13 + 2 * wide(out) * CYC
         if flag:
-            return emit("g", lambda: g.iota(ap(out), pattern, base, cm, allow_small_or_imprecise_dtypes=True), [], [out])
-        return emit("g", lambda: g.iota(ap(out), pattern, base, cm), [], [out])
+            return emit("g", lambda: g.iota(ap(out), pattern, base, cm, allow_small_or_imprecise_dtypes=True), [], [out], cost=c)
+        return emit("g", lambda: g.iota(ap(out), pattern, base, cm), [], [out], cost=c)
 
     def pick(out, a, pattern, op, x, base, cm):
         return emit("g", lambda: g.affine_select(ap(out), ap(a), pattern, op, x, base, cm), [a], [out],
                     cost=0.17 + 2 * wide(out) * CYC)
 
-    iota(("pi", 0, 1), [[0, 1]], 0, 1, False)
-    iota(M("JR"), [[0, 8], [1, 16]], 0, 0)
-    pick(M("JA"), M("JR"), [[-16, 8], [0, 16]], Op.is_ge, 99.0, 0, 1)
-    pick(M("JP"), M("JA"), [[16, 8], [0, 16]], Op.is_ge, 99.0, 15, -1)
-    ts(("ki", 0, 1), ("pi", 0, 1), 15, Op.bitwise_and)
-    cp(KC, ("ki", 0, 1))
-    ts(PB, KC, 256.0, Op.mult)
-    ts(NBI, KC, -256.0, Op.mult)
-    for r in range(4):
-        ts(RC[r], KC, float(12 + r), Op.is_equal)
-    ts(M("ID"), M("JP"), KC, Op.is_equal)
-    ts(M("BD"), M("JP"), 15.5, Op.is_le)
-    ts(M("R0"), M("BD"), RC[0], Op.mult, 256.0, Op.mult)
-    for j in range(16):
-        ts(LJ("BIG", j), M("JP"), float(j), Op.is_equal)
-    ts(full("LX"), full("BIG"), ("wS", 0, 1), Op.mult)
-    ts(full("LY"), full("BIG"), ("wS", 1, 2), Op.mult)
-    act(full("LV0"), full("BIG"), Fn.Copy, scale=RC[0])
-    for r in (1, 2):
-        pick(full("LV%d" % r), full("BIG"), [[0, 16], [-16, 8], [0, 16]], Op.is_equal, 0.0, -12 - r, 1)
-    iota(M("SRC"), [[0, 8], [1, 4], [1, 4]], 13, 0)
-    iota(("IT", 0, 96), [[1, 96]], 0, 0)
-    iota(("w1", 0, 12), [[0, 2], [16, 6]], W, 0)
+    def weights(nm, col):
+        ts((nm, 0, 144), ("XP", 0, 144), ("wK", 0, 1) if col[0] == "wS" else K15, Op.is_equal, col, Op.mult)
+
+    def diag(nm, x):
+        ts(M(nm), M("XP"), 0.0, Op.is_equal, x, Op.mult)
 
     def consts_search():
-        ts(("E256", 0, 16), ("JR", 0, 16), KC, Op.is_equal, 256.0, Op.mult)
-        fill(("geo", 0, 16), 1.0 / 256)
-        fill(("geo", 16, 32), 0.0)
-        emit("v", lambda: g.vector.tensor_tensor_scan(ap(("geo", 32, 48)), ap(("geo", 0, 16)), ap(("geo", 16, 32)), -128.0,
-                                                      Op.mult, Op.add), [("geo", 0, 32)], [("geo", 32, 48)])
-        tt(("geo", 48, 60), ("geo", 32, 44), ("E256", 0, 12), Op.mult)
-        emit("v", lambda: g.vector.tensor_reduce(ap(WN), ap(("geo", 48, 60)), AxisListType.X, Op.add), [("geo", 48, 60)], [WN])
-        ts(full("LN"), full("BIG"), WN, Op.mult, 1.0 / 256, Op.mult)
-        ts(full("LV3"), full("BIG"), RC[3], Op.mult)
-        ts(M("NI"), M("ID"), -1.0, Op.mult)
+        iota(("pi", 0, 1), [[0, 1]], 0, 1, False)
+        iota(("XP", 0, 144), [[1, 144]], 0, -1)
+        iota(("JR", 0, 96), [[0, 6], [1, 16]], 0, 0)
+        fill(M("ONE"), 1.0)
         for j in range(16):
-            ts(LJ("LB", j), M("BD"), ("E256", j, j + 1), Op.mult)
-        ts(M("HI"), M("ID"), 0.5, Op.mult)
-        ts(T0, KC, 11.5, Op.is_gt, -100000.0, Op.mult)
-        ts(T1, NBI, 128.0, Op.subtract)
-        tt(LBI, T0, T1, Op.add)
+            pick(LJ(j), M("ONE"), [[-16, 8], [0, 16]], Op.is_equal, 0.0, -j, 1)
+        ts(("ki", 0, 1), ("pi", 0, 1), 15, Op.bitwise_and)
+        cp(KC, ("ki", 0, 1))
+        ts(K15, KC, -1.0, Op.mult, 15.0, Op.add)
+        ts(("wK", 0, 1), KC, -1.0, Op.mult, 15.0, Op.add)
+        ts(KA, KC, -7.5, Op.add)
+        ts(NBI, KC, -256.0, Op.mult)
+        ts(("E16", 0, 16), ("JR", 0, 16), KC, Op.is_equal)
+        act(M("AB"), M("XP"), Fn.Abs, bias=KA)
+        ts(M("R0"), M("AB"), 8.0, Op.is_lt, RC0, Op.mult)
+        weights("ZX", ("wS", 0, 1))
+        weights("ZY", ("wS", 1, 2))
+        weights("ZL", RC0)
+        ts(KLT, KC, 11.5, Op.is_lt)
+        act(WE, KC, Fn.Exp, bias=50 * LN2, scale=-10 * LN2, more=1.3)
+        tt(WS, WE, KLT, Op.mult)
+        weights("ZS", WS)
+        fill(("geo", 0, 4), 16.0)
+        scan(("geo", 8, 11), ("geo", 0, 3), ("E16", 12, 15), Op.add)
+        scan(("geo", 12, 15), ("geo", 0, 3), ("E16", 13, 16), Op.add)
+        ts(W2, ("geo", 9, 10), 16.0, Op.mult)
+        ts(WN, WH, -1.0, Op.mult)
+        weights("ZH", WH)
+        weights("ZN", WN)
+        weights("Z1", W1)
+        weights("Z2", W2)
+        for nm, x in (("ID", 1.0), ("NI", -1.0), ("I16", 16.0), ("N16", -16.0), ("ISY", KLT)):
+            diag(nm, x)
+        ts(B1, KC, -2048.0, Op.mult, -1760.0, Op.add)
+        ts(QB, KC, 256.0, Op.mult, 220.0, Op.add)
+        ts(RB, KC, 256.0, Op.mult, 256.0, Op.add)
+        ts(("LT", 0, 96), ("JR", 0, 96), KC, Op.is_gt, KLT, Op.mult)
+        fill(("HT", 0, 768), 0.0)
+        for c in range(2):
+            fill(("XB", 480 * c, 480 * c + 96), 0.0)
         fill(("mkT", W, MKW), 0.0)
 
     def consts_edits():
-        ts(KLT, KC, 11.5, Op.is_lt)
-        ts(M("ISY"), M("ID"), KLT, Op.mult)
+        iota(M("SRC"), [[0, 8], [1, 4], [1, 4]], 13, 0)
+        iota(("IT", 0, 96), [[1, 96]], 0, 0)
+        iota(("w1", 0, 12), [[0, 2], [16, 6]], W, 0)
+        ts(M("JP"), M("XP"), KC, Op.add)
+        ts(M("BD"), M("AB"), 8.0, Op.is_lt)
         ts(M("CAQ"), M("SRC"), KC, Op.is_equal)
         tt(M("CA"), M("CAQ"), M("BD"), Op.mult)
         ts(("ci", 0, 1), ("ki", 0, 1), 3, Op.bitwise_and)
-        ts(T2, KC, 11.5, Op.is_gt, 50.0, Op.mult)
+        ts(T2, KC, 11.5, Op.is_gt, 500.0, Op.mult)
         ts(T3, ("ci", 0, 1), 12.0, Op.add)
         tt(RCOL, T2, T3, Op.add)
         ts(M("RS"), M("JP"), RCOL, Op.is_equal)
         ts(("ci", 1, 2), ("ki", 0, 1), 2, Op.arith_shift_right)
-        ts(KK, ("ci", 1, 2), -256.0, Op.mult, 768.0, Op.add)
-        ts(T4, KC, 11.5, Op.is_lt, 50.0, Op.mult)
+        ts(KK, ("ci", 1, 2), -1.0, Op.mult, 3.0, Op.add)
+        ts(T4, KC, 11.5, Op.is_lt, 500.0, Op.mult)
         ts(T5, KC, 1.0, Op.add)
         tt(KP1, T4, T5, Op.add)
-        ts(M("DN"), M("JP"), KP1, Op.is_equal)
-        ts(R120, RC[0], 1.0 / 256, Op.mult)
-        ts(M("R12"), M("ID"), R120, Op.mult)
+        ts(M15, KC, 14.5, Op.is_lt)
+        ts(M("DN"), M("JP"), KP1, Op.is_equal, M15, Op.mult)
+        diag("R12", RC0)
         ts(("DU", 0, 12), ("w1", 0, 12), KC, Op.add)
         for J in range(6):
             ts(KJ[J], KC, 16.0 * J, Op.add)
@@ -367,6 +383,16 @@ def rank_program(g, core, T, topo):
         lo = c * NJ * n + k * NJ
         return (nm, lo, lo + NJ)
 
+    def pair(nm, c, k=0, n=1):
+        lo = 2 * (c * NJ * n + k * NJ)
+        return (nm, lo, lo + 2 * NJ)
+
+    def even(b):
+        return (b[0], b[1], b[2], 2)
+
+    def odd(b):
+        return (b[0], b[1] + 1, b[2], 2)
+
     def half(nm, c, h):
         lo = c * CH + h * NB
         return (nm, lo, lo + NB)
@@ -375,57 +401,61 @@ def rank_program(g, core, T, topo):
         return (nm, c * CH, c * CH + CH)
 
     def gb(c, h):
-        return "g%d%d" % (c, h)
+        return ("g%d%d" % (c, h), 0, NB)
+
+    def mo(r, c, s):
+        return sm("mo", 2 * r + c, s - 1, 4)
+
+    def first_length(r, c, src):
+        k = ("k%d" % c, 2 * NJ, 3 * NJ)
+        word("ZL", k, src, c * CH)
+        act(mo(r, c, 1), k, Fn.Copy, bias=MO)
+
+    def first_rope(c, src):
+        kb = ("k%d" % c, 0, 2 * NJ)
+        word("ZH", odd(kb), src, c * CH)
+        word("ZN", even(kb), src, c * CH, stop=False)
 
     def jmajor(c, src):
-        for h, bk in ((0, "h%d" % c), (1, "k%d" % c)):
-            seq = []
-            for x in range(8):
-                seq.append(((bk, x * NJ, x * NJ + NJ), M("ID"), (src, c * CH + 8 * h + x, c * CH + CH, 16), True, True))
-            mm(seq, [M("ID"), chunk(src, c)], [(bk, 0, NB)])
-            act(half("qj", c, h), (bk, 0, NB), Fn.Identity, bias=PB)
-
-    def lengths(c, src, rs):
-        for r in rs:
-            word("LV%d" % r, ("k%d" % c, r * NJ, r * NJ + NJ), src, c * CH, NJ)
-        lo, hi = rs[0] * NJ, rs[-1] * NJ + NJ
-        act(("Aw", c * 192 + lo, c * 192 + hi), ("k%d" % c, lo, hi), Fn.Copy)
-
-    def P1(c, s, src):
-        m = sm("Aw", c, s - 1, 4)
         for h in range(2):
-            seq = []
-            for x in range(8):
-                j = 8 * h + x
-                o = (gb(c, h), x * NJ, x * NJ + NJ)
-                if s == 1:
-                    seq.append((o, M("R0"), (src, c * CH + j, c * CH + CH, 16), True, True))
-                else:
-                    seq.append((o, LJ("LB", j), m, True, True))
-            mm(seq, [M("R0"), chunk(src, c)] if s == 1 else [full("LB"), m], [(gb(c, h), 0, NB)])
+            bk = gb(c, h)
+            mm([((bk[0], x * NJ, x * NJ + NJ), M("ID"), (src, c * CH + 8 * h + x, c * CH + CH, 16), True, True) for x in range(8)])
+            if h == 0:
+                act(half("qj", c, 0), bk, Fn.Copy)
+            else:
+                act(half("qv", c, 1), bk, Fn.Identity, bias=QB, scale=0.125)
 
-    def V1(c):
+    def from_length(r, c, s):
+        m = mo(r, c, s)
+        act(sm("m97", c, s % 2, 2), m, Fn.Copy, bias=-97.0 * MO, scale=97.0)
+        act(sm("Cw", c, s % 2, 2), m, Fn.Exp, bias=math.log(1.5) + (83 + 10 * MO) * LN2, scale=-10 * LN2)
+        act(sm("dead", c, s % 2, 2), m, Fn.Relu, bias=2.0 ** 80 * (MO + 0.5), scale=-2.0 ** 80)
+        act(sm("mt", c, s % 2, 2), m, Fn.Copy, bias=8192.0 * (2 - MO) + 131072.0 * s, scale=8192.0)
+
+    def mask(c):
+        m = odd(pair("Rb", c))
         for h in range(2):
-            tt(half("zp", c, h), half("qj", c, h), (gb(c, h), 0, NB), Op.min)
+            bk = gb(c, h)
+            mm([((bk[0], x * NJ, x * NJ + NJ), LJ(8 * h + x), m, True, True) for x in range(8)])
+        act(gb(c, 0), gb(c, 0), Fn.Relu, bias=B1, scale=8.0)
+        tt(half("zp", c, 1), half("qv", c, 1), gb(c, 1), Op.min)
+        tt(half("zz", c, 0), half("qj", c, 0), gb(c, 0), Op.min)
+        act(half("zz", c, 1), half("zp", c, 1), Fn.Relu, bias=B1, scale=8.0)
 
-    def A1(c):
-        for h in range(2):
-            act(half("zz", c, h), half("zp", c, h), Fn.Relu, bias=NBI)
+    def sums(c, strided):
+        hb = "h%d" % c
+        if strided:
+            word("ZX", (hb, 0, NJ), "zz", c * CH)
+            word("ZY", (hb, NJ, 2 * NJ), "zz", c * CH)
+            return
+        word("ZX", (hb, 0, NJ), "zz", c * CH, False, stop=False, js=range(8))
+        word("ZX", (hb, 0, NJ), "zz", c * CH, False, start=False, js=range(8, 16))
+        word("ZY", (hb, NJ, 2 * NJ), "zz", c * CH, False)
 
-    def A2(c, s):
-        m = sm("Aw", c, s - 1, 4)
-        act(sm("m97", c), m, Fn.Copy, scale=97.0)
-        act(sm("th", c), m, Fn.Silu, scale=-LN256)
-        act(sm("mt", c, s % 2, 2), m, Fn.Copy, bias=8192.0 + 65536.0 * s, scale=4096.0)
-
-    def P2(c):
-        word("LX", ("h%d" % c, 0, NJ), "zz", c * CH, NJ, strided=False)
-        word("LY", ("h%d" % c, NJ, 2 * NJ), "zz", c * CH, NJ, strided=False)
-
-    def V2(c):
+    def place_of(c, s):
         hb, o = "h%d" % c, c * 3 * NJ
         cp(("U", o, o + 2 * NJ), (hb, 0, 2 * NJ))
-        tt(sm("U", c, 2, 3), (hb, NJ, 2 * NJ), sm("m97", c), Op.add)
+        tt(sm("U", c, 2, 3), (hb, NJ, 2 * NJ), sm("m97", c, s % 2, 2), Op.add)
         ts(("UA", o, o + 3 * NJ), ("U", o, o + 3 * NJ), 4095, Op.bitwise_and)
         tt(sm("P", c), sm("UA", c, 0, 3), sm("UA", c, 1, 3), Op.mult)
         ts(sm("Wd", c), sm("UA", c, 2, 3), 32.0, Op.mult, -131072.0, Op.add)
@@ -436,126 +466,103 @@ def rank_program(g, core, T, topo):
     def win(off, w=W):
         return T.mkT[:, 0:w].indirect(ap(off))
 
-    def gathered(o, off, q, op):
-        emit("v", lambda: g.vector.tensor_tensor(ap(o), win(off), ap(q), op), [("mkT", 0, W), off, q], [o],
-             cost=0.08 + 1.5 * CYC * wide(o))
+    def gathered(o, off, q, op, nm="mkT", w=W):
+        return emit("v", lambda: g.vector.tensor_tensor(ap(o), T[nm][:, 0:w].indirect(ap(off)), ap(q), op), [(nm, 0, w), off, q],
+                    [o], cost=0.05 + GAT * CYC * wide(o))
 
-    def A3(c):
-        o, off = chunk("vv", c), sm("OFF", c)
-        emit("a", lambda: g.scalar.activation(ap(o), win(off), Fn.Copy), [("mkT", 0, W), off], [o],
-             cost=0.1 + 1.5 * CYC * wide(o))
+    def step(r, c, s, q0):
+        hb, kb = "h%d" % c, ("k%d" % c, 0, 2 * NJ)
+        S, hit, m = (hb, 2 * NJ, 3 * NJ), pair("HT", c, s - 1, 4), mo(r, c, s)
+        Rb = odd(pair("Rb", c))
+        place_of(c, s)
+        mm([(S, M("ID"), sm("Cw", c, s % 2, 2), True, False), (S, M("ID"), sm("dead", c, s % 2, 2), False, False)])
+        if s == 2:
+            mm([(odd(kb), M("I16"), sm("rest", c), True, True), (even(kb), M("N16"), sm("rest", c), True, False)])
+        if s == 3:
+            act(sm("m256", c), m, Fn.Copy, bias=-256.0 * MO, scale=256.0)
+            mm([(odd(kb), M("I16"), Rb, True, False), (odd(kb), M("N16"), sm("m256", c), False, True),
+                (even(kb), M("N16"), Rb, True, False), (even(kb), M("I16"), sm("m256", c), False, False)])
+        tt(even(pair("XB", c, s - 1, 5)), sm("H", c), sm("mt", c, s % 2, 2), Op.add)
+        gathered(chunk("nn", c), sm("OFF", c), chunk(q0, c), Op.subtract)
+        word("ZS", S, "nn", c * CH, start=False)
+        if s < 4:
+            word("Z1" if s == 1 else "Z2", even(kb), "nn", c * CH, start=False)
+        tt(odd(hit), S, sm("Cw", c, s % 2, 2), Op.is_equal)
+        if s < 4:
+            scan(pair("Rb", c), hit, kb, Op.add)
+            act(mo(r, c, s + 1), Rb, Fn.Copy, bias=MO - 0.42, scale=1.0 / 256)
+        if s == 1:
+            scan(pair("Rf", c), hit, kb, Op.add)
+            act(sm("m256", c), mo(r, c, 2), Fn.Copy, bias=-256.0 * MO, scale=256.0)
+            tt(sm("rest", c), odd(pair("Rf", c)), sm("m256", c), Op.subtract)
+        scan(pair("XB", c, s, 5), hit, pair("XB", c, s - 1, 5), Op.max)
 
-    def held(c, w):
-        return ("k%d" % c, NJ, 2 * NJ) if w == 0 else ("h%d" % c, (w - 1) * NJ, w * NJ)
+    def later_steps(r, q0):
+        for s in range(2, 5):
+            for c in range(2):
+                mask(c)
+                from_length(r, c, s)
+                sums(c, False)
+                step(r, c, s, q0)
 
-    def P4(c, s):
-        for w in range(4 - s):
-            word("LV%d" % w, held(c, w), "vv", c * CH, NJ, extra=(M("NI"), sm("Aw", c, s + w, 4)))
-
-    def V4(c, s):
-        hit, code = sm("hitS", c, s - 1, 4), sm("codeS", c, s - 1, 4)
-        tt(code, sm("H", c), sm("mt", c, s % 2, 2), Op.add)
-        tt(hit, ("k%d" % c, 0, NJ), sm("th", c), Op.is_gt)
-        for w in range(4 - s):
-            t = ("tm", c * 144 + w * NJ, c * 144 + w * NJ + NJ)
-            tt(t, held(c, w), hit, Op.mult)
-            tt(sm("Aw", c, s + w, 4), sm("Aw", c, s + w, 4), t, Op.add)
-        tt(sm("B" if s == 1 else "ch", c), code, hit, Op.mult)
-        if s > 1:
-            tt(sm("B", c), sm("B", c), sm("ch", c), Op.max)
-
-    def La(c, src):
-        ts(sm("Li", c), sm("B", c), 12, Op.arith_shift_right, 15, Op.bitwise_and)
-        ts(sm("Hb", c), sm("B", c), 4095, Op.bitwise_and)
-        cp(sm("Lb", c), sm("Li", c))
+    def learn(c, q0, dest, after):
+        B = odd(pair("XB", c, 4, 5))
+        cp(sm("Bi", c), B)
+        ts(sm("OL", c), B, 1.0 / 8192, Op.mult)
+        ts(sm("Hb", c), sm("Bi", c), 4095, Op.bitwise_and)
         cp(sm("OB", c), sm("Hb", c))
         for h in range(2):
-            r = ("Lb", c * NJ + 24 * h, c * NJ + 24 * h + 24)
-            bk = (gb(c, h), 0, NB)
-            mm([((gb(c, h), j, NB, 16), LJ("LB", j), r, True, True) for j in range(16)], [full("LB"), r], [bk])
-            act(bk, bk, Fn.Sign, bias=LBI)
-            gathered(half("dd", c, h), ("OB", c * NJ + 24 * h, c * NJ + 24 * h + 24), half(src, c, h), Op.subtract)
+            p = 2 * c + h
+            gathered(half("dd", c, h), ("OB", 24 * p, 24 * p + 24), half(q0, c, h), Op.subtract)
+            gathered(half(dest(p), c, h), ("OL", 24 * p, 24 * p + 24), half("dd", c, h), Op.mult, "LT", 96)
+            after(p)
 
-    def Lb(c, h, src, to):
-        bk, d, sd, q = (gb(c, h), 0, NB), half("dd", c, h), half("sd", c, h), half(src, c, h)
-        tt(sd, d, bk, Op.mult)
-        mm([(bk, M("ID"), q, True, False), (bk, M("HI"), d, False, False), (bk, M("HI"), sd, False, True)],
-           [M("ID"), M("HI"), q, d, sd], [bk])
-        act(half(to, c, h), bk, Fn.Copy)
+    sends = [[], []]
 
-    def search(src):
-        for s in range(1, 5):
-            for c in range(2):
-                if s == 1:
-                    jmajor(c, src)
-                P1(c, s, src)
-                if s == 1:
-                    lengths(c, src, [0])
-                A2(c, s)
-                V1(c)
-                A1(c)
-                P2(c)
-                if s == 1:
-                    lengths(c, src, [1, 2, 3])
-                V2(c)
-                gathered(chunk("nn", c), sm("OFF", c), chunk(src, c), Op.not_equal)
-                if s < 4:
-                    A3(c)
-                word("LN", ("k%d" % c, 0, NJ), "nn", c * CH, NJ)
-                P4(c, s)
-                V4(c, s)
-
-    def close(src, dest, after):
-        for c in range(2):
-            La(c, src)
-            for h in range(2):
-                Lb(c, h, src, dest(2 * c + h))
-                after(2 * c + h)
-
-    omask = off_chip_mask(core, cores, topo)
-    sends = []
-
-    def send(p):
-        s = goes[p]
+    def send(k, p, after=()):
+        s = held[p]
         if s == rank:
             return
-        b = ("qA", NB * p, NB * p + NB)
+        b = (("qN", "dS")[k], NB * p, NB * p + NB)
         rel = relay_of(core, cores[s], cores, topo)
         to = cores[s] if rel is None else rel
-        m = omask & topo.mask(core, to)
+        m = topo.mask(core, to)
         rid, pid = topo.addr(to, core)
-        x = NB * held_order(s)[1].index(rank)
-        dst, sem = (T.land[:], "rin") if rel is not None else (T.qB[:, x:x + NB], "arr%d" % rank)
-        sends.append(emit("g", lambda: g.remote_dma(dst, ap(b), T.sem[sem], T.sem.sent, pid, rid, m), [b], [], None, 0.3,
-                          ("sent", count(m))))
+        x = NB * held_order(s, cores, topo).index(rank)
+        if rel is None:
+            dst, sem = T[LANDS[k]][:, x:x + NB], "arr%d%d" % (k, rank)
+        else:
+            dst, sem = T["land%d" % k][:], "rin%d" % k
+        sends[k].append(emit("g", lambda: g.remote_dma(dst, ap(b), T.sem[sem], T.sem.sent, pid, rid, m), [b], [], None, 0.3,
+                             ("sent", count(m)), after))
 
-    def arrivals():
-        for p in range(4):
-            s = came[p]
-            if s != rank:
-                rel = relay_of(cores[s], core, cores, topo)
-                n = count(topo.mask(cores[s] if rel is None else rel, core))
-                emit("x%d" % s, None, [], [("qB", NB * p, NB * p + NB)], None, 4.0 if rel is None else 8.0, ("arr%d" % s, n),
-                     sends[:1] if p < 2 else sends)
+    def arrivals(k):
+        for p in range(3):
+            s = held[p]
+            rel = relay_of(cores[s], core, cores, topo)
+            n = count(topo.mask(cores[s] if rel is None else rel, core))
+            emit("x%d%d" % (k, s), None, [], [(LANDS[k], NB * p, NB * p + NB)], None, 3.5 if rel is None else 6.5,
+                 ("arr%d%d" % (k, s), n), sends[k][:max(p, 1) + 1] if k else sends[k])
 
-    def edits(src):
-        e = goes.index(0)
-        w0, h0 = 192 * (e // 2), 24 * (e % 2)
-        qe, de, Bb = (src, NB * e, NB * e + 96), ("dd", NB * e, NB * e + 96), ("B", 24 * e, 24 * e + 6)
+    def edits():
+        e = held.index(0)
+        c, h0 = e // 2, 24 * (e % 2)
+        qe, de = ("q0", NB * e, NB * e + 96), ("dd", NB * e, NB * e + 96)
+        x4 = pair("XB", c, 4, 5)[1] + 2 * h0 + 1
         fk = [("fc", NJ * k + h0, NJ * k + h0 + 6) for k in range(4)]
-        ts(("al", 0, 192), ("Aw", w0, w0 + 192), 0.0, Op.is_gt)
-        tt(("ms", 0, 192), ("al", 0, 192), ("hitS", w0, w0 + 192), Op.subtract)
-        tt(("fc", 0, 192), ("codeS", w0, w0 + 192), ("ms", 0, 192), Op.mult)
+        ts(("al", 0, 192), ("mo", 192 * c, 192 * c + 192), MO + 0.5, Op.is_gt)
+        tt(("ms", 0, 192), ("al", 0, 192), ("HT", 384 * c + 1, 384 * c + 384, 2), Op.subtract)
+        tt(("fc", 0, 192), ("XB", 480 * c, 480 * c + 384, 2), ("ms", 0, 192), Op.mult)
         tt(("f1", 0, 6), fk[0], fk[1], Op.max)
         tt(("f1", 8, 14), fk[2], fk[3], Op.max)
-        F = ("FB", 0, 6)
+        F, Bb = ("FB", 0, 6), ("FB", 6, 12)
         tt(F, ("f1", 0, 6), ("f1", 8, 14), Op.max)
-        cp(("FB", 6, 12), Bb)
+        cp(Bb, ("XB", x4, x4 + 11, 2))
         tt(("ed", 0, 6), F, Bb, Op.is_gt)
         ts(("ed", 8, 14), Bb, 0.0, Op.is_gt)
         ts(("cl", 0, 12), ("FB", 0, 12), 4095, Op.bitwise_and)
-        ts(("si", 0, 6), F, 12, Op.arith_shift_right, 15, Op.bitwise_and)
-        ts(("si", 8, 14), Bb, 16, Op.arith_shift_right)
+        ts(("si", 0, 6), F, 13, Op.arith_shift_right, 15, Op.bitwise_and)
+        ts(("si", 8, 14), Bb, 17, Op.arith_shift_right)
         for o in (0, 6):
             tt(("ed2", o, o + 6), ("ed", 0, 6), ("ed", 8, 14), Op.mult)
         ts(("nk", 0, 12), ("ed2", 0, 12), -8192.0, Op.mult, 8192.0, Op.add)
@@ -563,35 +570,31 @@ def rank_program(g, core, T, topo):
         ts(("key1", 0, 12), ("key", 0, 12), 1.0, Op.add)
         ts(("kh", 0, 12), ("key", 0, 12), 6, Op.arith_shift_right)
         ts(("kh", 12, 24), ("key", 0, 12), 63, Op.bitwise_and)
-        ts(("khb", 0, 12), ("kh", 0, 12), 0.25, Op.mult)
-        ts(("khb", 16, 28), ("kh", 12, 24), 1.0 / 256, Op.mult)
+        ts(("khb", 0, 12), ("kh", 0, 12), 64.0, Op.mult)
+        cp(("khb", 16, 28), ("kh", 12, 24))
         ts(("sb", 0, 6), ("si", 0, 6), -2.0, Op.add)
         cp(("sb", 8, 14), ("si", 8, 14))
         seq = []
         for j in range(16):
-            o = ("h0", j, 192, 16)
-            seq += [(o, LJ("LB", j), ("khb", 0, 12), True, False), (o, LJ("LB", j), ("khb", 16, 28), False, True)]
-        mm(seq, [full("LB"), ("khb", 0, 12), ("khb", 16, 28)], [("h0", 0, 192)])
-        mm([(("k0", j, 96, 16), LJ("LB", j), ("sb", 8, 14), True, True) for j in range(16)],
-           [full("LB"), ("sb", 8, 14)], [("k0", 0, 96)])
-        mm([(("k1", j, 96, 16), LJ("LB", j), ("sb", 0, 6), True, True) for j in range(16)],
-           [full("LB"), ("sb", 0, 6)], [("k1", 0, 96)])
-        mm([(("h1", 0, 96), M("CA"), de, True, False), (("h1", 0, 96), M("CA"), qe, False, True)],
-           [M("CA"), de, qe], [("h1", 0, 96)])
+            o = ("k0", j, 192, 16)
+            seq += [(o, LJ(j), ("khb", 0, 12), True, False), (o, LJ(j), ("khb", 16, 28), False, True)]
+        mm(seq)
+        mm([(("k1", j, 96, 16), LJ(j), ("sb", 8, 14), True, True) for j in range(16)]
+           + [(("k1", 96 + j, 192, 16), LJ(j), ("sb", 0, 6), True, True) for j in range(16)]
+           + [(("k1", 192, 288), M("CA"), de, True, True)])
         for x in range(12):
             J = x % 6
             act(("LK", 96 * x, 96 * x + 96), ("LM", 96 * J, 96 * J + 96), Fn.Copy, bias=-1.0, scale=("key1", x, x + 1))
-        act(("mf", 0, 96), ("k1", 0, 96), Fn.Copy)
-        ts(("mk1", 0, 96), ("k0", 0, 96), KK, Op.is_equal)
-        tt(("cm", 0, 96), ("h1", 0, 96), ("mk1", 0, 96), Op.mult)
-        mm([(("k0", 0, 96), M("ISY"), qe, True, False), (("k0", 0, 96), M("RS"), ("cm", 0, 96), False, True)],
-           [M("ISY"), M("RS"), qe, ("cm", 0, 96)], [("k0", 0, 96)])
+        act(("mf", 0, 96), ("k1", 96, 192), Fn.Copy)
+        ts(("mk1", 0, 96), ("k1", 0, 96), KK, Op.is_equal)
+        tt(("cm", 0, 96), ("k1", 192, 288), ("mk1", 0, 96), Op.mult)
+        mm([(("k1", 0, 96), M("ISY"), qe, True, False), (("k1", 0, 96), M("RS"), ("cm", 0, 96), False, True)])
         for x in range(12):
             w = x // 6
             eq = ("EQ", 96 * x, 96 * x + 96)
-            tt(eq, ("LK", 96 * x, 96 * x + 96), ("h0", 96 * w, 96 * w + 96), Op.is_equal)
+            tt(eq, ("LK", 96 * x, 96 * x + 96), ("k0", 96 * w, 96 * w + 96), Op.is_equal)
             act(eq, eq, Fn.Copy, accum=("CNT", x, x + 1))
-        cp(("Eb", 0, 96), ("k0", 0, 96))
+        cp(("Eb", 0, 96), ("k1", 0, 96))
         ts(("w1", 12, 24), ("CNT", 0, 12), 0.0, Op.is_equal)
         tt(("w1", 24, 36), ("cl", 0, 12), ("DU", 0, 12), Op.subtract)
         tt(("w1", 36, 48), ("w1", 12, 24), ("ed2", 0, 12), Op.mult)
@@ -601,32 +604,68 @@ def rank_program(g, core, T, topo):
         oF, oB, full_w = ("OE", 0, 6), ("OE", 6, 12), ("mkT", 0, MKW)
         emit("v", lambda: g.vector.tensor_copy(win(oF, MKW), ap(("Eb", 0, 96))), [oF, ("Eb", 0, 96)], [full_w], cost=0.35)
         emit("v", lambda: g.vector.tensor_copy(ap(("vb", 0, 96)), win(oB, MKW)), [oB, full_w], [("vb", 0, 96)], cost=0.2)
-        mm([(("h1", 0, 96), M("ISY"), ("vb", 0, 96), True, False), (("h1", 0, 96), M("DN"), ("vb", 0, 96), False, False),
-            (("h1", 0, 96), M("R12"), ("mf", 0, 96), False, True)],
-           [M("ISY"), M("DN"), M("R12"), ("vb", 0, 96), ("mf", 0, 96)], [("h1", 0, 96)])
-        cp(("Sb", 0, 96), ("h1", 0, 96))
+        mm([(("k1", 0, 96), M("ISY"), ("vb", 0, 96), True, False), (("k1", 0, 96), M("DN"), ("vb", 0, 96), False, False),
+            (("k1", 0, 96), M("R12"), ("mf", 0, 96), False, True)])
+        cp(("Sb", 0, 96), ("k1", 0, 96))
         emit("v", lambda: g.vector.tensor_copy(win(oB, MKW), ap(("Sb", 0, 96))), [oB, ("Sb", 0, 96)], [full_w], cost=0.35)
 
     consts_search()
-    search("qN")
-    close("qN", lambda p: "qB" if goes[p] == rank else "qA", send)
+    for p in range(3):
+        send(0, p, tab)
+    arrivals(0)
+    for c in range(2):
+        for h in range(2):
+            mm([(gb(c, h), M("R0"), half("qN", c, h), True, True)])
+            act(gb(c, h), gb(c, h), Fn.Relu, bias=NBI, scale=256.0)
+            tt(half("zz", c, h), half("qN", c, h), gb(c, h), Op.min)
+        first_length(0, c, "qN")
+        from_length(0, c, 1)
+        sums(c, True)
+        for h in range(2):
+            act(half("q0", c, h), half("qN", c, h), Fn.Copy, scale=KLT)
+        first_rope(c, "qN")
+        jmajor(c, "qN")
+        step(0, c, 1, "q0")
+    later_steps(0, "q0")
+    for c in range(2):
+        learn(c, "q0", lambda p: "dR" if held[p] == rank else "dS", lambda p: send(1, p))
+    for c in range(2):
+        for h in range(2):
+            mm([(gb(c, h), M("R0"), half("qO", c, h), True, True)])
+            act(half("rr", c, h), gb(c, h), Fn.Relu, bias=RB, scale=-256.0)
+            mm([(gb(c, h), M("ID"), half("qO", c, h), True, False), (gb(c, h), M("NI"), half("rr", c, h), False, False)])
+        first_length(1, c, "qO")
+        from_length(1, c, 1)
     consts_edits()
-    edits("qN")
-    arrivals()
-    search("qB")
+    edits()
+    arrivals(1)
+    for c in range(2):
+        for h in range(2):
+            mm([(gb(c, h), M("ID"), half("dR", c, h), False, True)])
+            act(half("zz", c, h), gb(c, h), Fn.Relu)
+        sums(c, True)
+        for h in range(2):
+            mm([(gb(c, h), M("ISY"), half("qO", c, h), True, False), (gb(c, h), M("ID"), half("dR", c, h), False, True)])
+            act(half("q1", c, h), gb(c, h), Fn.Copy)
+        first_rope(c, "qO")
+        jmajor(c, "q1")
+        step(1, c, 1, "q1")
+    later_steps(1, "q1")
 
     def out(p):
-        b, x = ("qF", NB * p, NB * p + NB), NB * came[p]
+        c, h = p // 2, p % 2
+        b, x = half("qF", c, h), NB * held[p]
+        mm([(gb(c, h), M("ID"), half("dF", c, h), False, True)])
+        act(b, gb(c, h), Fn.Copy)
         emit("s", lambda: g.sync.dma_start(T.yq[:, x:x + NB], ap(b)), [b], [], "dy%d" % p, 2.5)
 
     for c in range(2):
-        ts(sm("y1", c), sm("B", c), 0.0, Op.is_gt)
-        ts(sm("y0", c), sm("B", c), 4095, Op.bitwise_and)
-        ts(sm("y2", c), sm("y0", c), 1.0, Op.add)
-        tt(sm("y3", c), sm("y1", c), sm("y2", c), Op.mult)
-        ts(sm("yS", c), sm("y3", c), -1.0, Op.add)
+        for h in range(2):
+            mm([(gb(c, h), M("ID"), half("qO", c, h), True, False), (gb(c, h), M("ID"), half("dR", c, h), False, False)])
+        learn(c, "q1", lambda p: "dF", out)
+        act(sm("Bm", c), odd(pair("XB", c, 4, 5)), Fn.Copy, bias=-1.0)
+        tt(sm("yS", c), sm("Hb", c), sm("Bm", c), Op.min)
         for p in (2 * c, 2 * c + 1):
-            b, x = ("yS", 24 * p, 24 * p + 24), 24 * came[p]
+            b, x = ("yS", 24 * p, 24 * p + 24), 24 * held[p]
             emit("s", lambda b=b, x=x: g.sync.dma_start(T.yb[:, x:x + 24], ap(b)), [b], [], "db%d" % p, 2.5)
-    close("qB", lambda p: "qF", out)
     issue(place())

@@ -7,10 +7,11 @@ MKW = W + 128
 LN2 = math.log(2.0)
 MO = 136.0
 CYC, PEC, WAKE, SLACK = 0.00083, 0.00042, 0.17, 0.04
-GAT = 1.5
+GAT, AHEAD, TMK, TFAR, TNEAR = 1.5, 0.4, 7.0, 4.5, 2.5
+SCAN3, ONEGROUP, WAYS = True, True, ("av", "va")
 
 _words = ["XP", "ZX", "ZY", "ZS", "ZL", "ZH", "ZN", "Z1", "Z2"]
-_mats = ["AB", "ONE", "ID", "NI", "I16", "N16", "R0", "ISY", "SRC", "CAQ", "BD", "CA", "JP", "RS", "DN", "R12"]
+_mats = ["AB", "ONE", "ID", "NI", "I16", "N16", "I256", "ISY", "SRC", "CAQ", "BD", "CA", "JP", "RS", "DN", "R12"]
 SCRATCH = {"mkT": ("sbuf", [128, MKW], "bfloat16"), "LB": ("sbuf", [128, 2048], "bfloat16")}
 for _n in ("qN", "q0", "q1", "qO", "dR", "dS", "dF", "qF", "qj", "zz", "nn", "dd", "rr"):
     SCRATCH[_n] = ("sbuf", [128, K], "bfloat16")
@@ -28,11 +29,10 @@ def _add(dtype, **widths):
 
 
 _add("bfloat16", wK=2, wS=2, land0=NB, land1=NB, JR=96, LT=96, mo=768, Rb=192, rest=96, m256=96, Cw=192, dead=192, khb=32, sb=16,
-     cm=96, Eb=96, vb=96, mf=96, Sb=96)
-_add("int32", pi=1, ki=1, ci=4, U=288, UA=288, P=96, Wd=96, S=96, H=96, Bi=96, Hb=96, fc=192, f1=32, FB=12, cl=12, key=12,
-     kh=24, si=16)
-_add("float32", col=40, E16=16, geo=32, IT=96, LM=576, DU=12, HT=768, XB=960, Rf=192, m97=192, mt=192, Bm=96, yS=96,
-     al=192, ms=192, ed=32, ed2=12, nk=12, key1=12, LK=1152, EQ=1152, CNT=12, w1=64, mk1=96)
+     cm=96, Eb=96, vb=96, mf=96, Sb=96, HT=768, IT=192, J16=16)
+_add("int32", pi=1, ki=1, ci=4, U=288, UA=288, X0=288, X1=288, P=96, Wd=96, S=96, H=96, Bi=96, Hb=96, FB=12, cl=12, kh=24, si=12)
+_add("float32", col=40, E16=16, geo=48, XB=960, Rf=192, m97=192, mt=192, Bm=96, yS=96, al=192, ms=144, fc=144, f1=8, XF=12,
+     XG=24, HM=40, WD=24, WO=24, TO=24, ed=24, key=12, EQ=1152, MN=12, w1=12, mk1=96)
 _add("uint16", OFF=96, OB=96, OL=96, OE=12)
 BANKS = ("g00", "g01", "g10", "g11", "h0", "h1", "k0", "k1")
 for _n in BANKS:
@@ -101,7 +101,7 @@ def rank_program(g, core, T, topo):
         waits, order = set(after), set(behind)
         for kind, lst in (("r", reads), ("w", writes)):
             for b in lst:
-                nm, lo, hi = b[0], b[1], b[2]
+                nm, lo, hi, step = (b + (1,))[:4]
                 r = rec.setdefault(nm, [])
                 if nm in BANKS:
                     for x in r:
@@ -114,11 +114,13 @@ def rank_program(g, core, T, topo):
                     r[:] = [x for x in r if x[2] == q or x[3] == i]
                 else:
                     for x in r:
-                        if x[3] != i and x[0] < hi and lo < x[1] and (kind == "w" or x[4] == "w"):
+                        if (x[3] != i and x[0] < hi and lo < x[1] and (kind == "w" or x[4] == "w")
+                                and not (x[5] == step and (x[0] - lo) % step)):
                             waits.add(x[3])
                     if kind == "w":
-                        r[:] = [x for x in r if not (lo <= x[0] and x[1] <= hi)]
-                r.append((lo, hi, q, i, kind))
+                        r[:] = [x for x in r if not (lo <= x[0] and x[1] <= hi
+                                                     and (step == 1 or (x[5] == step and (x[0] - lo) % step == 0)))]
+                r.append((lo, hi, q, i, kind, step))
         ops.append((q, fn, sem, cost, waits, order - waits, ev))
         return i
 
@@ -137,11 +139,38 @@ def rank_program(g, core, T, topo):
         ready = [i for i in range(n) if need[i] == 0]
         free = {}
         seq = []
+
+        def coming(q, until):
+            when = {i: max(free.get(ops[i][0], 0.0), at[i]) for i in ready}
+            left, todo, found = {}, [i for i in ready if when[i] < until], []
+            while todo:
+                i = todo.pop()
+                if ops[i][0] == q:
+                    found.append((when[i], i))
+                    continue
+                for j in succ[i]:
+                    when[j] = max(when.get(j, at[j]), when[i] + ops[i][3] + WAKE if i in ops[j][4] else when[i])
+                    left[j] = left.get(j, need[j]) - 1
+                    if left[j] == 0 and when[j] < until:
+                        todo.append(j)
+            return found
+
         while ready:
             st = [max(free.get(ops[i][0], 0.0), at[i]) for i in ready]
             t = min(st)
             q = ops[ready[st.index(t)]][0]
-            i = -max((prio[i], -i) for i, x in zip(ready, st) if ops[i][0] == q and x <= t + SLACK)[1]
+            now = sorted(((-prio[i], i) for i, x in zip(ready, st) if ops[i][0] == q and x <= t + SLACK))
+            later = [(w, k) for w, k in coming(q, t + 1.1) if w > t + SLACK]
+            i = None
+            for x in now:
+                c, p = ops[x[1]][3], prio[x[1]]
+                if ops[x[1]][2] is not None or not any(
+                        w < t + c and max(w + prio[k], w + ops[k][3] + p) + AHEAD < t + c + prio[k] for w, k in later):
+                    i = x[1]
+                    break
+            if i is None:
+                free[q] = min(later)[0]
+                continue
             t = max(free.get(q, 0.0), at[i])
             ready.remove(i)
             seq.append(i)
@@ -281,28 +310,33 @@ def rank_program(g, core, T, topo):
         loads.append(emit("s", lambda: g.sync.dma_start(ap(b), src), [], [b], sem, t, behind=loads[-1:]))
         return loads[-1]
 
-    emit("a", lambda: g.scalar.dma_start(ap(("wS", 0, 2)), T.wt[:]), [], [("wS", 0, 2)], "dw", 2.0)
+    emit("a", lambda: g.scalar.dma_start(ap(("wS", 0, 2)), T.wt[:]), [], [("wS", 0, 2)], "dw", 1.0)
     for p in range(4):
-        load(("qN", NB * p, NB * p + NB), T.qs[:, NB * held[p]:NB * held[p] + NB], "dq%d" % p, 2.4 + 0.4 * p)
-    tab = [load(("mkT", x, x + W // 2), T.mk[:, x:x + W // 2], "dm%d" % (2 * x // W), 7.0) for x in (0, W // 2)]
-    load(("qO", 3 * NB, K), T.qs[:, NB * rank:NB * rank + NB], "dq4", 7.5)
+        load(("qN", NB * p, NB * p + NB), T.qs[:, NB * held[p]:NB * held[p] + NB], "dq%d" % p, 1.4 + 0.4 * p)
+    tab = [load(("mkT", x, x + W // 2), T.mk[:, x:x + W // 2], "dm%d" % (2 * x // W), TMK) for x in (0, W // 2)]
+    load(("qO", 3 * NB, K), T.qs[:, NB * rank:NB * rank + NB], "dq4", TMK + 0.5)
 
     def C(i):
         return ("col", i, i + 1)
-    KC, K15, KA, KLT, NBI, B1, QB, RB, WS, WE, W2, WN, KP1, RCOL, KK = [C(i) for i in range(15)]
-    KJ = [C(16 + J) for J in range(6)]
+    KC, K15, KA, KLT, NBI, B1, QB, RB, WS, R8, W2, WN, KP1, RCOL, KK, Y64 = [C(i) for i in range(16)]
     T2, T3, T4, T5, M15 = [C(24 + i) for i in range(5)]
     RC0, W1, WH = ("E16", 12, 13), ("geo", 10, 11), ("geo", 14, 15)
 
-    def iota(out, pattern, base, cm, flag=True):
+    def iota(out, pattern, base, cm, flag=True, behind=()):
         c = 0.13 + 2 * wide(out) * CYC
-        if flag:
-            return emit("g", lambda: g.iota(ap(out), pattern, base, cm, allow_small_or_imprecise_dtypes=True), [], [out], cost=c)
-        return emit("g", lambda: g.iota(ap(out), pattern, base, cm), [], [out], cost=c)
+        kw = {"allow_small_or_imprecise_dtypes": True} if flag else {}
+        made.append(emit("g", lambda: g.iota(ap(out), pattern, base, cm, **kw), [], [out], cost=c, behind=behind))
+        return made[-1]
+
+    made = []
+
+    def least(out, a, op):
+        return emit("v", lambda: g.vector.tensor_reduce(ap(out), ap(a), AxisListType.X, op), [a], [out],
+                    cost=max(64, wide(a)) * CYC + 0.03)
 
     def pick(out, a, pattern, op, x, base, cm):
-        return emit("g", lambda: g.affine_select(ap(out), ap(a), pattern, op, x, base, cm), [a], [out],
-                    cost=0.17 + 2 * wide(out) * CYC)
+        made.append(emit("g", lambda: g.affine_select(ap(out), ap(a), pattern, op, x, base, cm), [a], [out],
+                         cost=0.17 + 2 * wide(out) * CYC))
 
     def weights(nm, col):
         ts((nm, 0, 144), ("XP", 0, 144), ("wK", 0, 1) if col[0] == "wS" else K15, Op.is_equal, col, Op.mult)
@@ -311,27 +345,34 @@ def rank_program(g, core, T, topo):
         ts(M(nm), M("XP"), 0.0, Op.is_equal, x, Op.mult)
 
     def consts_search():
-        iota(("pi", 0, 1), [[0, 1]], 0, 1, False)
+        first = iota(("J16", 0, 16), [[1, 16]], 0, 0)
+        act(("geo", 16, 32), ("J16", 0, 16), Fn.Exp, bias=50 * LN2, scale=-10 * LN2, more=1.3)
+        iota(("pi", 0, 1), [[0, 1]], 0, 1, False, [first])
         iota(("XP", 0, 144), [[1, 144]], 0, -1)
         iota(("JR", 0, 96), [[0, 6], [1, 16]], 0, 0)
         fill(M("ONE"), 1.0)
         for j in range(16):
             pick(LJ(j), M("ONE"), [[-16, 8], [0, 16]], Op.is_equal, 0.0, -j, 1)
-        ts(("ki", 0, 1), ("pi", 0, 1), 15, Op.bitwise_and)
-        cp(KC, ("ki", 0, 1))
-        ts(K15, KC, -1.0, Op.mult, 15.0, Op.add)
-        ts(("wK", 0, 1), KC, -1.0, Op.mult, 15.0, Op.add)
-        ts(KA, KC, -7.5, Op.add)
-        ts(NBI, KC, -256.0, Op.mult)
-        ts(("E16", 0, 16), ("JR", 0, 16), KC, Op.is_equal)
-        act(M("AB"), M("XP"), Fn.Abs, bias=KA)
-        ts(M("R0"), M("AB"), 8.0, Op.is_lt, RC0, Op.mult)
+        ki = ("ki", 0, 1)
+        ts(ki, ("pi", 0, 1), 15, Op.bitwise_and)
+        cp(KC, ki)
+        ts(K15, ki, -1.0, Op.mult, 15.0, Op.add)
+        ts(("wK", 0, 1), ki, -1.0, Op.mult, 15.0, Op.add)
+        ts(NBI, ki, -256.0, Op.mult)
+        ts(("E16", 0, 16), ("J16", 0, 16), KC, Op.is_equal)
         weights("ZX", ("wS", 0, 1))
-        weights("ZY", ("wS", 1, 2))
+        if SCAN3:
+            ts(Y64, ("wS", 1, 2), 64.0, Op.mult)
+            weights("ZY", Y64)
+            for c in range(2):
+                for nm, k, x in (("X0", 0, 0), ("X0", 1, 1), ("X1", 1, -32)):
+                    fill((nm, 144 * c + k, 144 * c + 144, 3), x)
+        else:
+            weights("ZY", ("wS", 1, 2))
         weights("ZL", RC0)
-        ts(KLT, KC, 11.5, Op.is_lt)
-        act(WE, KC, Fn.Exp, bias=50 * LN2, scale=-10 * LN2, more=1.3)
-        tt(WS, WE, KLT, Op.mult)
+        ts(KLT, ki, 11.5, Op.is_lt)
+        tt(("geo", 32, 44), ("geo", 16, 28), ("E16", 0, 12), Op.mult)
+        least(WS, ("geo", 32, 44), Op.add)
         weights("ZS", WS)
         fill(("geo", 0, 4), 16.0)
         scan(("geo", 8, 11), ("geo", 0, 3), ("E16", 12, 15), Op.add)
@@ -344,19 +385,22 @@ def rank_program(g, core, T, topo):
         weights("Z2", W2)
         for nm, x in (("ID", 1.0), ("NI", -1.0), ("I16", 16.0), ("N16", -16.0), ("ISY", KLT)):
             diag(nm, x)
-        ts(B1, KC, -2048.0, Op.mult, -1760.0, Op.add)
-        ts(QB, KC, 256.0, Op.mult, 220.0, Op.add)
-        ts(RB, KC, 256.0, Op.mult, 256.0, Op.add)
+        act(B1, KC, Fn.Copy, bias=-1760.0, scale=-2048.0)
+        act(QB, KC, Fn.Copy, bias=220.0, scale=256.0)
+        act(RB, KC, Fn.Copy, bias=256.0, scale=256.0)
+        act(R8, KC, Fn.Copy, bias=2048.0, scale=2048.0)
         ts(("LT", 0, 96), ("JR", 0, 96), KC, Op.is_gt, KLT, Op.mult)
-        fill(("HT", 0, 768), 0.0)
         for c in range(2):
-            fill(("XB", 480 * c, 480 * c + 96), 0.0)
+            fill(("HT", 384 * c, 384 * c + 384, 2), 0.0)
+            fill(("XB", 480 * c + 1, 480 * c + 96, 2), 0.0)
         fill(("mkT", W, MKW), 0.0)
 
     def consts_edits():
         iota(M("SRC"), [[0, 8], [1, 4], [1, 4]], 13, 0)
-        iota(("IT", 0, 96), [[1, 96]], 0, 0)
+        iota(("IT", 0, 192), [[0, 2], [1, 96]], 0, 0)
         iota(("w1", 0, 12), [[0, 2], [16, 6]], W, 0)
+        act(KA, KC, Fn.Copy, bias=-7.5)
+        act(M("AB"), M("XP"), Fn.Abs, bias=KA)
         ts(M("JP"), M("XP"), KC, Op.add)
         ts(M("BD"), M("AB"), 8.0, Op.is_lt)
         ts(M("CAQ"), M("SRC"), KC, Op.is_equal)
@@ -374,10 +418,10 @@ def rank_program(g, core, T, topo):
         ts(M15, KC, 14.5, Op.is_lt)
         ts(M("DN"), M("JP"), KP1, Op.is_equal, M15, Op.mult)
         diag("R12", RC0)
-        ts(("DU", 0, 12), ("w1", 0, 12), KC, Op.add)
-        for J in range(6):
-            ts(KJ[J], KC, 16.0 * J, Op.add)
-            ts(("LM", 96 * J, 96 * J + 96), ("IT", 0, 96), KJ[J], Op.is_lt)
+        diag("I256", 1.0 / 256)
+        ts(("WD", 1, 24, 2), ("w1", 0, 12), KC, Op.add)
+        ts(("TO", 0, 6), ("WD", 1, 12, 2), 1.0 / 256, Op.mult, 8192.0 - W / 256, Op.add)
+        fill(("HM", 0, 40), 0.0)
 
     def sm(nm, c, k=0, n=1):
         lo = c * NJ * n + k * NJ
@@ -420,14 +464,15 @@ def rank_program(g, core, T, topo):
         for h in range(2):
             bk = gb(c, h)
             mm([((bk[0], x * NJ, x * NJ + NJ), M("ID"), (src, c * CH + 8 * h + x, c * CH + CH, 16), True, True) for x in range(8)])
-            if h == 0:
-                act(half("qj", c, 0), bk, Fn.Copy)
+            if WAYS[h] != "va":
+                act(half("qj", c, h), bk, Fn.Copy)
             else:
-                act(half("qv", c, 1), bk, Fn.Identity, bias=QB, scale=0.125)
+                act(half("qv", c, h), bk, Fn.Identity, bias=QB, scale=0.125)
 
     def from_length(r, c, s):
         m = mo(r, c, s)
-        act(sm("m97", c, s % 2, 2), m, Fn.Copy, bias=-97.0 * MO, scale=97.0)
+        x = 3104.0 if SCAN3 else 97.0
+        act(sm("m97", c, s % 2, 2), m, Fn.Copy, bias=-x * MO, scale=x)
         act(sm("Cw", c, s % 2, 2), m, Fn.Exp, bias=math.log(1.5) + (83 + 10 * MO) * LN2, scale=-10 * LN2)
         act(sm("dead", c, s % 2, 2), m, Fn.Relu, bias=2.0 ** 80 * (MO + 0.5), scale=-2.0 ** 80)
         act(sm("mt", c, s % 2, 2), m, Fn.Copy, bias=8192.0 * (2 - MO) + 131072.0 * s, scale=8192.0)
@@ -436,11 +481,26 @@ def rank_program(g, core, T, topo):
         m = odd(pair("Rb", c))
         for h in range(2):
             bk = gb(c, h)
-            mm([((bk[0], x * NJ, x * NJ + NJ), LJ(8 * h + x), m, True, True) for x in range(8)])
-        act(gb(c, 0), gb(c, 0), Fn.Relu, bias=B1, scale=8.0)
-        tt(half("zp", c, 1), half("qv", c, 1), gb(c, 1), Op.min)
-        tt(half("zz", c, 0), half("qj", c, 0), gb(c, 0), Op.min)
-        act(half("zz", c, 1), half("zp", c, 1), Fn.Relu, bias=B1, scale=8.0)
+            if WAYS[h] == "aa":
+                mm([((bk[0], x * NJ, x * NJ + NJ), LJ(8 * h + x), m, x == 0, False) for x in range(8)])
+            else:
+                mm([((bk[0], x * NJ, x * NJ + NJ), LJ(8 * h + x), m, True, True) for x in range(8)])
+        for h in range(2):
+            bk, z = gb(c, h), half("zz", c, h)
+            if WAYS[h] == "av":
+                act(bk, bk, Fn.Relu, bias=B1, scale=8.0)
+                tt(z, half("qj", c, h), bk, Op.min)
+            elif WAYS[h] == "va":
+                tt(half("zp", c, h), half("qv", c, h), bk, Op.min)
+                act(z, half("zp", c, h), Fn.Relu, bias=B1, scale=8.0)
+            elif WAYS[h] == "aa":
+                act(bk, bk, Fn.Relu, bias=R8, scale=-8.0)
+                mm([(bk, M("NI"), half("qj", c, h), False, True)])
+                act(z, bk, Fn.Relu, scale=-1.0)
+            else:
+                act(half("rr", c, h), bk, Fn.Relu, bias=R8, scale=-8.0)
+                mm([(bk, M("ID"), half("qj", c, h), True, False), (bk, M("NI"), half("rr", c, h), False, True)])
+                act(z, bk, Fn.Relu)
 
     def sums(c, strided):
         hb = "h%d" % c
@@ -448,14 +508,28 @@ def rank_program(g, core, T, topo):
             word("ZX", (hb, 0, NJ), "zz", c * CH)
             word("ZY", (hb, NJ, 2 * NJ), "zz", c * CH)
             return
-        word("ZX", (hb, 0, NJ), "zz", c * CH, False, stop=False, js=range(8))
-        word("ZX", (hb, 0, NJ), "zz", c * CH, False, start=False, js=range(8, 16))
-        word("ZY", (hb, NJ, 2 * NJ), "zz", c * CH, False)
+        if not ONEGROUP:
+            word("ZX", (hb, 0, NJ), "zz", c * CH, False, stop=False, js=range(8))
+            word("ZX", (hb, 0, NJ), "zz", c * CH, False, start=False, js=range(8, 16))
+            word("ZY", (hb, NJ, 2 * NJ), "zz", c * CH, False)
+            return
+        for h in range(2):
+            js = range(8 * h, 8 * h + 8)
+            word("ZX", (hb, 0, NJ), "zz", c * CH, False, h == 0, False, js)
+            word("ZY", (hb, NJ, 2 * NJ), "zz", c * CH, False, False, h == 1, js)
 
     def place_of(c, s):
         hb, o = "h%d" % c, c * 3 * NJ
         cp(("U", o, o + 2 * NJ), (hb, 0, 2 * NJ))
         tt(sm("U", c, 2, 3), (hb, NJ, 2 * NJ), sm("m97", c, s % 2, 2), Op.add)
+        if SCAN3:
+            ts(("X1", o, o + 3 * NJ, 3), sm("U", c, 0, 3), 4095, Op.bitwise_and)
+            ts(("X0", o + 2, o + 3 * NJ, 3), sm("U", c, 1, 3), 6, Op.arith_shift_right, 4095, Op.bitwise_and)
+            ts(("X1", o + 2, o + 3 * NJ, 3), sm("U", c, 2, 3), 131071, Op.bitwise_and)
+            scan(("UA", o, o + 3 * NJ), ("X0", o, o + 3 * NJ), ("X1", o, o + 3 * NJ), Op.add)
+            ts(sm("H", c), ("UA", o + 2, o + 3 * NJ, 3), 5, Op.arith_shift_right, 4095, Op.bitwise_and)
+            cp(sm("OFF", c), sm("H", c))
+            return
         ts(("UA", o, o + 3 * NJ), ("U", o, o + 3 * NJ), 4095, Op.bitwise_and)
         tt(sm("P", c), sm("UA", c, 0, 3), sm("UA", c, 1, 3), Op.mult)
         ts(sm("Wd", c), sm("UA", c, 2, 3), 32.0, Op.mult, -131072.0, Op.add)
@@ -519,7 +593,7 @@ def rank_program(g, core, T, topo):
 
     sends = [[], []]
 
-    def send(k, p, after=()):
+    def send(k, p, after=(), behind=()):
         s = held[p]
         if s == rank:
             return
@@ -534,73 +608,70 @@ def rank_program(g, core, T, topo):
         else:
             dst, sem = T["land%d" % k][:], "rin%d" % k
         sends[k].append(emit("g", lambda: g.remote_dma(dst, ap(b), T.sem[sem], T.sem.sent, pid, rid, m), [b], [], None, 0.3,
-                             ("sent", count(m)), after))
+                             ("sent", count(m)), after, behind))
 
     def arrivals(k):
         for p in range(3):
             s = held[p]
             rel = relay_of(cores[s], core, cores, topo)
             n = count(topo.mask(cores[s] if rel is None else rel, core))
-            emit("x%d%d" % (k, s), None, [], [(LANDS[k], NB * p, NB * p + NB)], None, 3.5 if rel is None else 6.5,
+            emit("x%d%d" % (k, s), None, [], [(LANDS[k], NB * p, NB * p + NB)], None, (TNEAR if rel is None else TFAR) + 3 - 3 * k,
                  ("arr%d%d" % (k, s), n), sends[k][:max(p, 1) + 1] if k else sends[k])
 
     def edits():
         e = held.index(0)
         c, h0 = e // 2, 24 * (e % 2)
         qe, de = ("q0", NB * e, NB * e + 96), ("dd", NB * e, NB * e + 96)
-        x4 = pair("XB", c, 4, 5)[1] + 2 * h0 + 1
-        fk = [("fc", NJ * k + h0, NJ * k + h0 + 6) for k in range(4)]
-        ts(("al", 0, 192), ("mo", 192 * c, 192 * c + 192), MO + 0.5, Op.is_gt)
-        tt(("ms", 0, 192), ("al", 0, 192), ("HT", 384 * c + 1, 384 * c + 384, 2), Op.subtract)
-        tt(("fc", 0, 192), ("XB", 480 * c, 480 * c + 384, 2), ("ms", 0, 192), Op.mult)
+        def six(b):
+            return (b[0], b[1] + 2 * h0, b[1] + 2 * h0 + 12)
+
+        fk = [("fc", NJ * k + h0, NJ * k + h0 + 6) for k in range(3)]
+        act(("al", 0, 144), ("mo", 192 * c, 192 * c + 144), Fn.Sign, bias=-MO)
+        act(("al", 144, 150), ("mo", 192 * c + 144 + h0, 192 * c + 150 + h0), Fn.Sign, bias=-MO)
+        tt(("ms", 0, 144), ("al", 0, 144), ("HT", 384 * c + 1, 384 * c + 288, 2), Op.subtract)
+        tt(("fc", 0, 144), ("XB", 480 * c, 480 * c + 288, 2), ("ms", 0, 144), Op.mult)
         tt(("f1", 0, 6), fk[0], fk[1], Op.max)
-        tt(("f1", 8, 14), fk[2], fk[3], Op.max)
-        F, Bb = ("FB", 0, 6), ("FB", 6, 12)
-        tt(F, ("f1", 0, 6), ("f1", 8, 14), Op.max)
-        cp(Bb, ("XB", x4, x4 + 11, 2))
+        tt(("XF", 1, 12, 2), ("f1", 0, 6), fk[2], Op.max)
+        cp(("XF", 0, 12, 2), even(six(pair("XB", c, 3, 5))))
+        hit = six(pair("HT", c, 3, 4))
+        tt(("HM", 1, 12, 2), ("al", 144, 150), odd(hit), Op.subtract)
+        scan(("XG", 0, 12), ("HM", 0, 12), ("XF", 0, 12), Op.max)
+        scan(("XG", 12, 24), hit, six(pair("XB", c, 3, 5)), Op.max)
+        F, Bb, ned = ("XG", 1, 12, 2), ("XG", 13, 24, 2), ("ed", 16, 22)
+        cp(("FB", 0, 12), ("XG", 1, 24, 2))
         tt(("ed", 0, 6), F, Bb, Op.is_gt)
-        ts(("ed", 8, 14), Bb, 0.0, Op.is_gt)
+        ts(("ed", 8, 14), Bb, 0.0, Op.is_gt, -8192.0, Op.mult)
+        tt(ned, ("ed", 0, 6), ("ed", 8, 14), Op.mult)
         ts(("cl", 0, 12), ("FB", 0, 12), 4095, Op.bitwise_and)
-        ts(("si", 0, 6), F, 13, Op.arith_shift_right, 15, Op.bitwise_and)
-        ts(("si", 8, 14), Bb, 17, Op.arith_shift_right)
-        for o in (0, 6):
-            tt(("ed2", o, o + 6), ("ed", 0, 6), ("ed", 8, 14), Op.mult)
-        ts(("nk", 0, 12), ("ed2", 0, 12), -8192.0, Op.mult, 8192.0, Op.add)
-        tt(("key", 0, 12), ("cl", 0, 12), ("nk", 0, 12), Op.add)
-        ts(("key1", 0, 12), ("key", 0, 12), 1.0, Op.add)
-        ts(("kh", 0, 12), ("key", 0, 12), 6, Op.arith_shift_right)
-        ts(("kh", 12, 24), ("key", 0, 12), 63, Op.bitwise_and)
-        ts(("khb", 0, 12), ("kh", 0, 12), 64.0, Op.mult)
+        ts(("kh", 0, 12), ("FB", 0, 12), 4032, Op.bitwise_and)
+        ts(("kh", 12, 24), ("FB", 0, 12), 63, Op.bitwise_and)
+        ts(("si", 0, 6), ("FB", 6, 12), 17, Op.arith_shift_right)
+        ts(("si", 6, 12), ("FB", 0, 6), 13, Op.arith_shift_right, 15, Op.bitwise_and)
+        cp(("sb", 0, 12), ("si", 0, 12))
         cp(("khb", 16, 28), ("kh", 12, 24))
-        ts(("sb", 0, 6), ("si", 0, 6), -2.0, Op.add)
-        cp(("sb", 8, 14), ("si", 8, 14))
-        seq = []
-        for j in range(16):
-            o = ("k0", j, 192, 16)
-            seq += [(o, LJ(j), ("khb", 0, 12), True, False), (o, LJ(j), ("khb", 16, 28), False, True)]
-        mm(seq)
-        mm([(("k1", j, 96, 16), LJ(j), ("sb", 8, 14), True, True) for j in range(16)]
-           + [(("k1", 96 + j, 192, 16), LJ(j), ("sb", 0, 6), True, True) for j in range(16)]
-           + [(("k1", 192, 288), M("CA"), de, True, True)])
-        for x in range(12):
-            J = x % 6
-            act(("LK", 96 * x, 96 * x + 96), ("LM", 96 * J, 96 * J + 96), Fn.Copy, bias=-1.0, scale=("key1", x, x + 1))
-        act(("mf", 0, 96), ("k1", 96, 192), Fn.Copy)
+        for o in (0, 6):
+            tt(("khb", o, o + 6), ("kh", o, o + 6), ned, Op.add)
+            tt(("key", o, o + 6), ("cl", o, o + 6), ned, Op.add)
+            tt(("TO", 8 + o, 14 + o), ("TO", 0, 6), ned, Op.add)
+        tt(("WD", 0, 24, 2), ("cl", 0, 12), ("WD", 1, 24, 2), Op.subtract)
+        mm([(("k0", 0, 192), M("I256"), ("IT", 0, 192), True, False)])
+        mm([(("k0", j, 192, 16), LJ(j), ("khb", 16, 28), False, False) for j in range(16)])
+        mm([(("k0", j, 192, 16), LJ(j), ("khb", 0, 12), False, j == 15) for j in range(16)])
+        mm([(("k1", j, 192, 16), LJ(j), ("sb", 0, 12), True, True) for j in range(16)])
+        mm([(("k1", 192, 288), M("CA"), de, True, True)])
+        act(("mf", 0, 96), ("k1", 96, 192), Fn.Copy, bias=-2.0)
         ts(("mk1", 0, 96), ("k1", 0, 96), KK, Op.is_equal)
         tt(("cm", 0, 96), ("k1", 192, 288), ("mk1", 0, 96), Op.mult)
         mm([(("k1", 0, 96), M("ISY"), qe, True, False), (("k1", 0, 96), M("RS"), ("cm", 0, 96), False, True)])
         for x in range(12):
             w = x // 6
             eq = ("EQ", 96 * x, 96 * x + 96)
-            tt(eq, ("LK", 96 * x, 96 * x + 96), ("k0", 96 * w, 96 * w + 96), Op.is_equal)
-            act(eq, eq, Fn.Copy, accum=("CNT", x, x + 1))
+            act(eq, ("k0", 96 * w, 96 * w + 96), Fn.Abs, bias=("key", x, x + 1), scale=-1.0)
+            least(("MN", x, x + 1), eq, Op.min)
         cp(("Eb", 0, 96), ("k1", 0, 96))
-        ts(("w1", 12, 24), ("CNT", 0, 12), 0.0, Op.is_equal)
-        tt(("w1", 24, 36), ("cl", 0, 12), ("DU", 0, 12), Op.subtract)
-        tt(("w1", 36, 48), ("w1", 12, 24), ("ed2", 0, 12), Op.mult)
-        tt(("w1", 48, 60), ("w1", 24, 36), ("w1", 36, 48), Op.mult)
-        tt(("w1", 12, 24), ("w1", 48, 60), ("DU", 0, 12), Op.add)
-        cp(("OE", 0, 12), ("w1", 12, 24))
+        tt(("HM", 17, 40, 2), ("MN", 0, 12), ("TO", 8, 20), Op.is_equal)
+        scan(("WO", 0, 24), ("HM", 16, 40), ("WD", 0, 24), Op.add)
+        cp(("OE", 0, 12), ("WO", 1, 24, 2))
         oF, oB, full_w = ("OE", 0, 6), ("OE", 6, 12), ("mkT", 0, MKW)
         emit("v", lambda: g.vector.tensor_copy(win(oF, MKW), ap(("Eb", 0, 96))), [oF, ("Eb", 0, 96)], [full_w], cost=0.35)
         emit("v", lambda: g.vector.tensor_copy(ap(("vb", 0, 96)), win(oB, MKW)), [oB, full_w], [("vb", 0, 96)], cost=0.2)
@@ -610,12 +681,13 @@ def rank_program(g, core, T, topo):
         emit("v", lambda: g.vector.tensor_copy(win(oB, MKW), ap(("Sb", 0, 96))), [oB, ("Sb", 0, 96)], [full_w], cost=0.35)
 
     consts_search()
+    consts_edits()
     for p in range(3):
-        send(0, p, tab)
+        send(0, p, tab, made)
     arrivals(0)
     for c in range(2):
         for h in range(2):
-            mm([(gb(c, h), M("R0"), half("qN", c, h), True, True)])
+            mm([(gb(c, h), LJ(12), half("qN", c, h), True, True)])
             act(gb(c, h), gb(c, h), Fn.Relu, bias=NBI, scale=256.0)
             tt(half("zz", c, h), half("qN", c, h), gb(c, h), Op.min)
         first_length(0, c, "qN")
@@ -631,12 +703,11 @@ def rank_program(g, core, T, topo):
         learn(c, "q0", lambda p: "dR" if held[p] == rank else "dS", lambda p: send(1, p))
     for c in range(2):
         for h in range(2):
-            mm([(gb(c, h), M("R0"), half("qO", c, h), True, True)])
+            mm([(gb(c, h), LJ(12), half("qO", c, h), True, True)])
             act(half("rr", c, h), gb(c, h), Fn.Relu, bias=RB, scale=-256.0)
             mm([(gb(c, h), M("ID"), half("qO", c, h), True, False), (gb(c, h), M("NI"), half("rr", c, h), False, False)])
         first_length(1, c, "qO")
         from_length(1, c, 1)
-    consts_edits()
     edits()
     arrivals(1)
     for c in range(2):

@@ -6,13 +6,15 @@ CH, NJ = 768, 48
 MKW = W + 128
 LN2 = math.log(2.0)
 MO = 136.0
-CYC, PEC, WAKE, SLACK = 0.00083, 0.00042, 0.17, 0.04
-GAT, AHEAD, TMK, TFAR, TNEAR = 1.5, 0.4, 7.0, 4.5, 2.5
-SCAN3, ONEGROUP, WAYS = True, True, ("av", "va")
+CYC, PEC, WAKE, SLACK = 0.00083, 0.00042, 0.14, 0.04
+GAT, TMK, TFAR, TNEAR = 1.5, 7.0, 3.5, 2.2
+LEADS, AHEADS, JIT, JA = (2.0, 2.5, 3.0, 3.5, 4.0), (0.2, 0.3, 0.4, 0.6), (0,), 0.3
+WAYS = ("av", "va")
 
-_words = ["XP", "ZX", "ZY", "ZS", "ZL", "ZH", "ZN", "Z1", "Z2"]
+_words = ["XP", "Z64", "ZX", "ZY", "ZS", "ZL", "ZH", "ZN", "Z1", "Z2"]
 _mats = ["AB", "ONE", "ID", "NI", "I16", "N16", "I256", "ISY", "SRC", "CAQ", "BD", "CA", "JP", "RS", "DN", "R12"]
-SCRATCH = {"mkT": ("sbuf", [128, MKW], "bfloat16"), "LB": ("sbuf", [128, 2048], "bfloat16")}
+SCRATCH = {"mkT": ("sbuf", [128, W], "bfloat16"), "mkE": ("sbuf", [128, MKW], "bfloat16"),
+           "LB": ("sbuf", [128, 2048], "bfloat16")}
 for _n in ("qN", "q0", "q1", "qO", "dR", "dS", "dF", "qF", "qj", "zz", "nn", "dd", "rr"):
     SCRATCH[_n] = ("sbuf", [128, K], "bfloat16")
 for _n in ("qv", "zp"):
@@ -28,16 +30,17 @@ def _add(dtype, **widths):
         SCRATCH[n] = ("sbuf", [128, w], dtype)
 
 
-_add("bfloat16", wK=2, wS=2, land0=NB, land1=NB, JR=96, LT=96, mo=768, Rb=192, rest=96, m256=96, Cw=192, dead=192, khb=32, sb=16,
+_add("bfloat16", wS=2, land0=NB, land1=NB, JR=96, LT=96, mo=768, Rb=192, rest=96, m256=96, Cw=192, dead=192, khb=32, sb=16,
      cm=96, Eb=96, vb=96, mf=96, Sb=96, HT=768, IT=192, J16=16)
-_add("int32", pi=1, ki=1, ci=4, U=288, UA=288, X0=288, X1=288, P=96, Wd=96, S=96, H=96, Bi=96, Hb=96, FB=12, cl=12, kh=24, si=12)
-_add("float32", col=40, E16=16, geo=48, XB=960, Rf=192, m97=192, mt=192, Bm=96, yS=96, al=192, ms=144, fc=144, f1=8, XF=12,
-     XG=24, HM=40, WD=24, WO=24, TO=24, ed=24, key=12, EQ=1152, MN=12, w1=12, mk1=96)
+_add("int32", pi=1, ki=1, ci=4, U=304, UA=288, X=592, H=96, Hb=96, cl=12, kh=24, si=12,
+     XB=960, XF=12, XG=24)
+_add("float32", col=40, E16=16, geo=48, Rf=192, m97=192, mt=192, Bm=96, yS=96, al=192, ms=144, fc=144, f1=8,
+     HM=40, WD=24, WO=24, TO=24, ed=24, key=12, EQ=1152, MN=12, w1=12, mk1=96)
 _add("uint16", OFF=96, OB=96, OL=96, OE=12)
 BANKS = ("g00", "g01", "g10", "g11", "h0", "h1", "k0", "k1")
 for _n in BANKS:
     SCRATCH[_n] = ("psum", [128, 512], "float32")
-SEMAPHORES = ["sV", "sA", "sP", "sG", "dw", "dq0", "dq1", "dq2", "dq3", "dq4", "dm0", "dm1", "dy0", "dy1", "dy2", "dy3",
+SEMAPHORES = ["sV", "sA", "sP", "sG", "dw", "dq0", "dq1", "dq2", "dq3", "dq4", "dm0", "dm1", "dm2", "dy0", "dy1", "dy2", "dy3",
               "db0", "db1", "db2", "db3", "sent", "rin0", "rin1", "rls"]
 SEMAPHORES += ["arr%d%d" % (_k, _r) for _k in range(2) for _r in range(4)]
 
@@ -58,17 +61,25 @@ def relay_of(src, dst, cores, topo):
     return None
 
 
-def held_order(rank, cores, topo):
-    me = cores[rank]
-    far = [s for s in range(len(cores)) if s != rank and not topo.may_write(me, cores[s])]
-    near = [s for s in range(len(cores)) if s != rank and topo.may_write(me, cores[s])]
-    return far + near + [rank]
+def way(a, b, cores, topo):
+    return 0 if a == b else 1 if topo.may_write(cores[a], cores[b]) else 2
+
+
+def goes_order(rank, cores, topo):
+    n = len(cores)
+    rest = sorted(range(1, n), key=lambda s: ((way(rank, s, cores, topo) + 1) % 3, (s - rank) % n))
+    return [0] + rest
+
+
+def came_order(rank, cores, topo):
+    return sorted(range(len(cores)), key=lambda s: (goes_order(s, cores, topo).index(rank) // 2, way(s, rank, cores, topo)))
 
 
 def count(mask):
     return bin(mask).count("1")
 
 
+TABLE = ("mkT", "mkE")
 LANDS = ("qO", "dR")
 
 
@@ -83,7 +94,7 @@ def rank_program(g, core, T, topo):
                 r = T.rank_of(a)
                 m_out = topo.mask(core, b)
                 rid, pid = topo.addr(b, core)
-                p = NB * held_order(T.rank_of(b), cores, topo).index(r)
+                p = NB * came_order(T.rank_of(b), cores, topo).index(r)
                 for k in range(2):
                     g.wait_ge(T.sem["rin%d" % k], count(topo.mask(a, core)))
                     g.remote_dma(T[LANDS[k]][:, p:p + NB], T["land%d" % k][:], T.sem["arr%d%d" % (k, r)], T.sem.rls, pid, rid,
@@ -95,6 +106,7 @@ def rank_program(g, core, T, topo):
     SEM = {"v": "sV", "a": "sA", "p": "sP", "g": "sG"}
     ops = []
     rec = {}
+    lead = {}
 
     def emit(q, fn, reads, writes, sem=None, cost=0.1, ev=None, after=(), behind=()):
         i = len(ops)
@@ -124,7 +136,20 @@ def rank_program(g, core, T, topo):
         ops.append((q, fn, sem, cost, waits, order - waits, ev))
         return i
 
-    def place():
+    def length(seq, f):
+        end, start, free = {}, {}, {}
+        for i in seq:
+            q, c = ops[i][0], ops[i][3] * (f if ops[i][2] is None and ops[i][6] is None else 1.0)
+            t = max([free.get(q, 0.0)] + [end[d] + WAKE for d in ops[i][4]] + [start[d] for d in ops[i][5]])
+            start[i], end[i] = t, t + c
+            free[q] = t + 0.05 if ops[i][2] is not None else t + c
+        return max(end.values())
+
+    def best_order():
+        tried = [place(x, y, z) for x in LEADS for y in AHEADS for z in JIT]
+        return min(tried, key=lambda seq: length(seq, 1.0) + length(seq, 1.4) / 1.4)
+
+    def place(run, AHEAD, jit):
         n = len(ops)
         succ = [[] for _ in ops]
         need = [0] * n
@@ -134,7 +159,10 @@ def rank_program(g, core, T, topo):
                 need[i] += 1
         prio = [0.0] * n
         for i in reversed(range(n)):
-            prio[i] = ops[i][3] + max([prio[j] + (WAKE if i in ops[j][4] else 0.0) for j in succ[i]] + [0.0])
+            prio[i] = ops[i][3] + max([prio[j] + (WAKE if i in ops[j][4] else 0.0) for j in succ[i]]
+                                      + [run * lead.get(i, (0, 0))[0] + lead.get(i, (0, 0))[1]])
+        if jit:
+            prio = [p + JA * ((i * 7919 * jit + i * i * 31 * jit) % 1000) / 1000 for i, p in enumerate(prio)]
         at = [0.0] * n
         ready = [i for i in range(n) if need[i] == 0]
         free = {}
@@ -303,18 +331,19 @@ def rank_program(g, core, T, topo):
             seq.append((out, (nm, 15 - j, 143 - j), r, start and j == js[0], stop and j == js[-1]))
         return mm(seq)
 
-    held = held_order(rank, cores, topo)
+    goes, came = goes_order(rank, cores, topo), came_order(rank, cores, topo)
+    own = NB * came.index(rank)
     loads = []
 
-    def load(b, src, sem, t):
-        loads.append(emit("s", lambda: g.sync.dma_start(ap(b), src), [], [b], sem, t, behind=loads[-1:]))
+    def load(b, src, sem, t, after=()):
+        loads.append(emit("s", lambda: g.sync.dma_start(ap(b), src), [], [b], sem, t, None, after, loads[-1:]))
         return loads[-1]
 
     emit("a", lambda: g.scalar.dma_start(ap(("wS", 0, 2)), T.wt[:]), [], [("wS", 0, 2)], "dw", 1.0)
     for p in range(4):
-        load(("qN", NB * p, NB * p + NB), T.qs[:, NB * held[p]:NB * held[p] + NB], "dq%d" % p, 1.4 + 0.4 * p)
+        load(("qN", NB * p, NB * p + NB), T.qs[:, NB * goes[p]:NB * goes[p] + NB], "dq%d" % p, 1.4 + 0.4 * p)
     tab = [load(("mkT", x, x + W // 2), T.mk[:, x:x + W // 2], "dm%d" % (2 * x // W), TMK) for x in (0, W // 2)]
-    load(("qO", 3 * NB, K), T.qs[:, NB * rank:NB * rank + NB], "dq4", TMK + 0.5)
+    load(("qO", own, own + NB), T.qs[:, NB * rank:NB * rank + NB], "dq4", TMK + 0.5)
 
     def C(i):
         return ("col", i, i + 1)
@@ -339,7 +368,7 @@ def rank_program(g, core, T, topo):
                          cost=0.17 + 2 * wide(out) * CYC))
 
     def weights(nm, col):
-        ts((nm, 0, 144), ("XP", 0, 144), ("wK", 0, 1) if col[0] == "wS" else K15, Op.is_equal, col, Op.mult)
+        ts((nm, 0, 144), ("XP", 0, 144), K15, Op.is_equal, col, Op.mult)
 
     def diag(nm, x):
         ts(M(nm), M("XP"), 0.0, Op.is_equal, x, Op.mult)
@@ -357,18 +386,15 @@ def rank_program(g, core, T, topo):
         ts(ki, ("pi", 0, 1), 15, Op.bitwise_and)
         cp(KC, ki)
         ts(K15, ki, -1.0, Op.mult, 15.0, Op.add)
-        ts(("wK", 0, 1), ki, -1.0, Op.mult, 15.0, Op.add)
         ts(NBI, ki, -256.0, Op.mult)
         ts(("E16", 0, 16), ("J16", 0, 16), KC, Op.is_equal)
-        weights("ZX", ("wS", 0, 1))
-        if SCAN3:
-            ts(Y64, ("wS", 1, 2), 64.0, Op.mult)
-            weights("ZY", Y64)
-            for c in range(2):
-                for nm, k, x in (("X0", 0, 0), ("X0", 1, 1), ("X1", 1, -32)):
-                    fill((nm, 144 * c + k, 144 * c + 144, 3), x)
-        else:
-            weights("ZY", ("wS", 1, 2))
+        ts(("Z64", 0, 144), ("XP", 0, 144), K15, Op.is_equal, 64.0, Op.mult)
+        for k, nm in enumerate(("ZX", "ZY")):
+            ts((nm, 0, 144), ("Z64", 0, 144), ("wS", k, k + 1), Op.mult)
+        for c in range(2):
+            for k, x in ((145, 0), (146, 1), (1, -32)):
+                fill(("X", 296 * c + k, 296 * c + k + 143, 3), x)
+            fill(("h%d" % c, NJ, NJ + 1), 0.0)
         weights("ZL", RC0)
         ts(KLT, ki, 11.5, Op.is_lt)
         tt(("geo", 32, 44), ("geo", 16, 28), ("E16", 0, 12), Op.mult)
@@ -392,8 +418,8 @@ def rank_program(g, core, T, topo):
         ts(("LT", 0, 96), ("JR", 0, 96), KC, Op.is_gt, KLT, Op.mult)
         for c in range(2):
             fill(("HT", 384 * c, 384 * c + 384, 2), 0.0)
-            fill(("XB", 480 * c + 1, 480 * c + 96, 2), 0.0)
-        fill(("mkT", W, MKW), 0.0)
+            fill(("XB", 480 * c + 1, 480 * c + 96, 2), 0)
+        fill(("mkE", W, MKW), 0.0)
 
     def consts_edits():
         iota(M("SRC"), [[0, 8], [1, 4], [1, 4]], 13, 0)
@@ -471,8 +497,7 @@ def rank_program(g, core, T, topo):
 
     def from_length(r, c, s):
         m = mo(r, c, s)
-        x = 3104.0 if SCAN3 else 97.0
-        act(sm("m97", c, s % 2, 2), m, Fn.Copy, bias=-x * MO, scale=x)
+        act(sm("m97", c, s % 2, 2), m, Fn.Copy, bias=-3104.0 * MO, scale=3104.0)
         act(sm("Cw", c, s % 2, 2), m, Fn.Exp, bias=math.log(1.5) + (83 + 10 * MO) * LN2, scale=-10 * LN2)
         act(sm("dead", c, s % 2, 2), m, Fn.Relu, bias=2.0 ** 80 * (MO + 0.5), scale=-2.0 ** 80)
         act(sm("mt", c, s % 2, 2), m, Fn.Copy, bias=8192.0 * (2 - MO) + 131072.0 * s, scale=8192.0)
@@ -504,49 +529,36 @@ def rank_program(g, core, T, topo):
 
     def sums(c, strided):
         hb = "h%d" % c
+        u1, u2 = (hb, 0, NJ), (hb, NJ + 1, 2 * NJ + 1)
         if strided:
-            word("ZX", (hb, 0, NJ), "zz", c * CH)
-            word("ZY", (hb, NJ, 2 * NJ), "zz", c * CH)
-            return
-        if not ONEGROUP:
-            word("ZX", (hb, 0, NJ), "zz", c * CH, False, stop=False, js=range(8))
-            word("ZX", (hb, 0, NJ), "zz", c * CH, False, start=False, js=range(8, 16))
-            word("ZY", (hb, NJ, 2 * NJ), "zz", c * CH, False)
+            word("ZX", u1, "zz", c * CH)
+            word("ZY", u2, "zz", c * CH)
             return
         for h in range(2):
             js = range(8 * h, 8 * h + 8)
-            word("ZX", (hb, 0, NJ), "zz", c * CH, False, h == 0, False, js)
-            word("ZY", (hb, NJ, 2 * NJ), "zz", c * CH, False, False, h == 1, js)
+            word("ZX", u1, "zz", c * CH, False, h == 0, False, js)
+            word("ZY", u2, "zz", c * CH, False, False, h == 1, js)
 
     def place_of(c, s):
-        hb, o = "h%d" % c, c * 3 * NJ
-        cp(("U", o, o + 2 * NJ), (hb, 0, 2 * NJ))
-        tt(sm("U", c, 2, 3), (hb, NJ, 2 * NJ), sm("m97", c, s % 2, 2), Op.add)
-        if SCAN3:
-            ts(("X1", o, o + 3 * NJ, 3), sm("U", c, 0, 3), 4095, Op.bitwise_and)
-            ts(("X0", o + 2, o + 3 * NJ, 3), sm("U", c, 1, 3), 6, Op.arith_shift_right, 4095, Op.bitwise_and)
-            ts(("X1", o + 2, o + 3 * NJ, 3), sm("U", c, 2, 3), 131071, Op.bitwise_and)
-            scan(("UA", o, o + 3 * NJ), ("X0", o, o + 3 * NJ), ("X1", o, o + 3 * NJ), Op.add)
-            ts(sm("H", c), ("UA", o + 2, o + 3 * NJ, 3), 5, Op.arith_shift_right, 4095, Op.bitwise_and)
-            cp(sm("OFF", c), sm("H", c))
-            return
-        ts(("UA", o, o + 3 * NJ), ("U", o, o + 3 * NJ), 4095, Op.bitwise_and)
-        tt(sm("P", c), sm("UA", c, 0, 3), sm("UA", c, 1, 3), Op.mult)
-        ts(sm("Wd", c), sm("UA", c, 2, 3), 32.0, Op.mult, -131072.0, Op.add)
-        tt(sm("S", c), sm("P", c), sm("Wd", c), Op.add)
-        ts(sm("H", c), sm("S", c), 5, Op.arith_shift_right, 4095, Op.bitwise_and)
+        hb, o, u, x = "h%d" % c, c * 3 * NJ, c * 152, c * 296
+        cp(("U", u, u + 2 * NJ + 1), (hb, 0, 2 * NJ + 1))
+        tt(("U", u + 100, u + 100 + NJ), (hb, NJ + 1, 2 * NJ + 1), sm("m97", c, s % 2, 2), Op.add)
+        ts(("X", x, x + 291, 3), ("U", u, u + 2 * NJ + 1), 6, Op.arith_shift_right, 4095, Op.bitwise_and)
+        ts(("X", x + 2, x + 144, 3), ("U", u + 100, u + 100 + NJ), 131071, Op.bitwise_and)
+        scan(("UA", o, o + 3 * NJ), ("X", x + 145, x + 289), ("X", x, x + 144), Op.add)
+        ts(sm("H", c), ("UA", o + 2, o + 3 * NJ, 3), 5, Op.arith_shift_right, 4095, Op.bitwise_and)
         cp(sm("OFF", c), sm("H", c))
 
     def win(off, w=W):
-        return T.mkT[:, 0:w].indirect(ap(off))
+        return T.mkE[:, 0:w].indirect(ap(off))
 
-    def gathered(o, off, q, op, nm="mkT", w=W):
+    def gathered(o, off, q, op, nm, w=W):
         return emit("v", lambda: g.vector.tensor_tensor(ap(o), T[nm][:, 0:w].indirect(ap(off)), ap(q), op), [(nm, 0, w), off, q],
                     [o], cost=0.05 + GAT * CYC * wide(o))
 
     def step(r, c, s, q0):
         hb, kb = "h%d" % c, ("k%d" % c, 0, 2 * NJ)
-        S, hit, m = (hb, 2 * NJ, 3 * NJ), pair("HT", c, s - 1, 4), mo(r, c, s)
+        S, hit, m = (hb, 100, 100 + NJ), pair("HT", c, s - 1, 4), mo(r, c, s)
         Rb = odd(pair("Rb", c))
         place_of(c, s)
         mm([(S, M("ID"), sm("Cw", c, s % 2, 2), True, False), (S, M("ID"), sm("dead", c, s % 2, 2), False, False)])
@@ -557,7 +569,7 @@ def rank_program(g, core, T, topo):
             mm([(odd(kb), M("I16"), Rb, True, False), (odd(kb), M("N16"), sm("m256", c), False, True),
                 (even(kb), M("N16"), Rb, True, False), (even(kb), M("I16"), sm("m256", c), False, False)])
         tt(even(pair("XB", c, s - 1, 5)), sm("H", c), sm("mt", c, s % 2, 2), Op.add)
-        gathered(chunk("nn", c), sm("OFF", c), chunk(q0, c), Op.subtract)
+        gathered(chunk("nn", c), sm("OFF", c), chunk(q0, c), Op.subtract, TABLE[r])
         word("ZS", S, "nn", c * CH, start=False)
         if s < 4:
             word("Z1" if s == 1 else "Z2", even(kb), "nn", c * CH, start=False)
@@ -579,30 +591,29 @@ def rank_program(g, core, T, topo):
                 sums(c, False)
                 step(r, c, s, q0)
 
-    def learn(c, q0, dest, after):
+    def learn(r, c, q0, dest, after):
         B = odd(pair("XB", c, 4, 5))
-        cp(sm("Bi", c), B)
+        ts(sm("Hb", c), B, 4095, Op.bitwise_and)
         ts(sm("OL", c), B, 1.0 / 8192, Op.mult)
-        ts(sm("Hb", c), sm("Bi", c), 4095, Op.bitwise_and)
         cp(sm("OB", c), sm("Hb", c))
         for h in range(2):
             p = 2 * c + h
-            gathered(half("dd", c, h), ("OB", 24 * p, 24 * p + 24), half(q0, c, h), Op.subtract)
-            gathered(half(dest(p), c, h), ("OL", 24 * p, 24 * p + 24), half("dd", c, h), Op.mult, "LT", 96)
-            after(p)
+            gathered(half("dd", c, h), ("OB", 24 * p, 24 * p + 24), half(q0, c, h), Op.subtract, TABLE[r])
+            after(p, gathered(dest(p), ("OL", 24 * p, 24 * p + 24), half("dd", c, h), Op.mult, "LT", 96))
 
     sends = [[], []]
 
     def send(k, p, after=(), behind=()):
-        s = held[p]
+        s = goes[p]
         if s == rank:
+            sends[k] += after[:k]
             return
         b = (("qN", "dS")[k], NB * p, NB * p + NB)
         rel = relay_of(core, cores[s], cores, topo)
         to = cores[s] if rel is None else rel
         m = topo.mask(core, to)
         rid, pid = topo.addr(to, core)
-        x = NB * held_order(s, cores, topo).index(rank)
+        x = NB * came_order(s, cores, topo).index(rank)
         if rel is None:
             dst, sem = T[LANDS[k]][:, x:x + NB], "arr%d%d" % (k, rank)
         else:
@@ -611,15 +622,18 @@ def rank_program(g, core, T, topo):
                              ("sent", count(m)), after, behind))
 
     def arrivals(k):
-        for p in range(3):
-            s = held[p]
+        for p in range(4):
+            s = came[p]
+            if s == rank:
+                continue
+            there = goes_order(s, cores, topo).index(rank)
             rel = relay_of(cores[s], core, cores, topo)
             n = count(topo.mask(cores[s] if rel is None else rel, core))
             emit("x%d%d" % (k, s), None, [], [(LANDS[k], NB * p, NB * p + NB)], None, (TNEAR if rel is None else TFAR) + 3 - 3 * k,
-                 ("arr%d%d" % (k, s), n), sends[k][:max(p, 1) + 1] if k else sends[k])
+                 ("arr%d%d" % (k, s), n), sends[k][:2 * (max(there, p) // 2) + 2] if k else sends[k])
 
     def edits():
-        e = held.index(0)
+        e = goes.index(0)
         c, h0 = e // 2, 24 * (e % 2)
         qe, de = ("q0", NB * e, NB * e + 96), ("dd", NB * e, NB * e + 96)
         def six(b):
@@ -638,15 +652,15 @@ def rank_program(g, core, T, topo):
         scan(("XG", 0, 12), ("HM", 0, 12), ("XF", 0, 12), Op.max)
         scan(("XG", 12, 24), hit, six(pair("XB", c, 3, 5)), Op.max)
         F, Bb, ned = ("XG", 1, 12, 2), ("XG", 13, 24, 2), ("ed", 16, 22)
-        cp(("FB", 0, 12), ("XG", 1, 24, 2))
+        FB = ("XG", 1, 24, 2)
         tt(("ed", 0, 6), F, Bb, Op.is_gt)
         ts(("ed", 8, 14), Bb, 0.0, Op.is_gt, -8192.0, Op.mult)
         tt(ned, ("ed", 0, 6), ("ed", 8, 14), Op.mult)
-        ts(("cl", 0, 12), ("FB", 0, 12), 4095, Op.bitwise_and)
-        ts(("kh", 0, 12), ("FB", 0, 12), 4032, Op.bitwise_and)
-        ts(("kh", 12, 24), ("FB", 0, 12), 63, Op.bitwise_and)
-        ts(("si", 0, 6), ("FB", 6, 12), 17, Op.arith_shift_right)
-        ts(("si", 6, 12), ("FB", 0, 6), 13, Op.arith_shift_right, 15, Op.bitwise_and)
+        ts(("cl", 0, 12), FB, 4095, Op.bitwise_and)
+        ts(("kh", 0, 12), FB, 4032, Op.bitwise_and)
+        ts(("kh", 12, 24), FB, 63, Op.bitwise_and)
+        ts(("si", 0, 6), Bb, 17, Op.arith_shift_right)
+        ts(("si", 6, 12), F, 13, Op.arith_shift_right, 15, Op.bitwise_and)
         cp(("sb", 0, 12), ("si", 0, 12))
         cp(("khb", 16, 28), ("kh", 12, 24))
         for o in (0, 6):
@@ -672,7 +686,7 @@ def rank_program(g, core, T, topo):
         tt(("HM", 17, 40, 2), ("MN", 0, 12), ("TO", 8, 20), Op.is_equal)
         scan(("WO", 0, 24), ("HM", 16, 40), ("WD", 0, 24), Op.add)
         cp(("OE", 0, 12), ("WO", 1, 24, 2))
-        oF, oB, full_w = ("OE", 0, 6), ("OE", 6, 12), ("mkT", 0, MKW)
+        oF, oB, full_w = ("OE", 0, 6), ("OE", 6, 12), ("mkE", 0, MKW)
         emit("v", lambda: g.vector.tensor_copy(win(oF, MKW), ap(("Eb", 0, 96))), [oF, ("Eb", 0, 96)], [full_w], cost=0.35)
         emit("v", lambda: g.vector.tensor_copy(ap(("vb", 0, 96)), win(oB, MKW)), [oB, full_w], [("vb", 0, 96)], cost=0.2)
         mm([(("k1", 0, 96), M("ISY"), ("vb", 0, 96), True, False), (("k1", 0, 96), M("DN"), ("vb", 0, 96), False, False),
@@ -682,9 +696,10 @@ def rank_program(g, core, T, topo):
 
     consts_search()
     consts_edits()
-    for p in range(3):
+    for p in range(4):
         send(0, p, tab, made)
     arrivals(0)
+    load(("mkE", 0, W), T.mk[:], "dm2", 6.0, [len(ops) - 3, len(ops) - 2, len(ops) - 1])
     for c in range(2):
         for h in range(2):
             mm([(gb(c, h), LJ(12), half("qN", c, h), True, True)])
@@ -700,7 +715,8 @@ def rank_program(g, core, T, topo):
         step(0, c, 1, "q0")
     later_steps(0, "q0")
     for c in range(2):
-        learn(c, "q0", lambda p: "dR" if held[p] == rank else "dS", lambda p: send(1, p))
+        learn(0, c, "q0", lambda p: ("dR", own, own + NB) if goes[p] == rank else ("dS", NB * p, NB * p + NB),
+              lambda p, i: send(1, p, [i]))
     for c in range(2):
         for h in range(2):
             mm([(gb(c, h), LJ(12), half("qO", c, h), True, True)])
@@ -723,20 +739,20 @@ def rank_program(g, core, T, topo):
         step(1, c, 1, "q1")
     later_steps(1, "q1")
 
-    def out(p):
+    def out(p, i):
         c, h = p // 2, p % 2
-        b, x = half("qF", c, h), NB * held[p]
+        b, x = half("qF", c, h), NB * came[p]
         mm([(gb(c, h), M("ID"), half("dF", c, h), False, True)])
         act(b, gb(c, h), Fn.Copy)
-        emit("s", lambda: g.sync.dma_start(T.yq[:, x:x + NB], ap(b)), [b], [], "dy%d" % p, 2.5)
+        lead[emit("s", lambda: g.sync.dma_start(T.yq[:, x:x + NB], ap(b)), [b], [], "dy%d" % p, 1.5)] = (1 - c, 0.6 - 0.6 * h)
 
     for c in range(2):
         for h in range(2):
             mm([(gb(c, h), M("ID"), half("qO", c, h), True, False), (gb(c, h), M("ID"), half("dR", c, h), False, False)])
-        learn(c, "q1", lambda p: "dF", out)
-        act(sm("Bm", c), odd(pair("XB", c, 4, 5)), Fn.Copy, bias=-1.0)
+        learn(1, c, "q1", lambda p: ("dF", NB * p, NB * p + NB), out)
+        ts(sm("Bm", c), odd(pair("XB", c, 4, 5)), -1.0, Op.add)
         tt(sm("yS", c), sm("Hb", c), sm("Bm", c), Op.min)
         for p in (2 * c, 2 * c + 1):
-            b, x = ("yS", 24 * p, 24 * p + 24), 24 * held[p]
-            emit("s", lambda b=b, x=x: g.sync.dma_start(T.yb[:, x:x + 24], ap(b)), [b], [], "db%d" % p, 2.5)
-    issue(place())
+            b, x = ("yS", 24 * p, 24 * p + 24), 24 * came[p]
+            emit("s", lambda b=b, x=x: g.sync.dma_start(T.yb[:, x:x + 24], ap(b)), [b], [], "db%d" % p, 1.2)
+    issue(best_order())

@@ -1,4 +1,5 @@
 import math
+import numpy as np
 from concourse.mybir import AluOpType as Op, ActivationFunctionType as Fn, AxisListType
 
 W, K, NB = 4096, 1536, 384
@@ -7,15 +8,15 @@ MKW = W + 128
 LN2 = math.log(2.0)
 MO = 136.0
 CYC, PEC, WAKE, SLACK = 0.00083, 0.00042, 0.14, 0.04
-GAT, TMK, TFAR, TNEAR = 1.5, 7.0, 3.5, 2.2
-LEADS, AHEADS, JIT, JA = (2.0, 2.5, 3.0, 3.5, 4.0), (0.2, 0.3, 0.4, 0.6), (0,), 0.3
-WAYS = ("av", "va")
+GAT, TMK, TFAR, TNEAR, PROP = 1.5, 7.0, 3.6, 1.8, 0.7
+LEADS, AHEADS, TRIES, JA, JF = (2.5, 3.5), (0.4, 0.6, 0.8), 0, 0.5, 0.05
+WAYS, BY_SCALAR, APART, SPLIT, ADD_V = ("av", "va"), ((1, 3), (1, 3)), False, False, (3,)
 
 _words = ["XP", "Z64", "ZX", "ZY", "ZS", "ZL", "ZH", "ZN", "Z1", "Z2"]
 _mats = ["AB", "ONE", "ID", "NI", "I16", "N16", "I256", "ISY", "SRC", "CAQ", "BD", "CA", "JP", "RS", "DN", "R12"]
 SCRATCH = {"mkT": ("sbuf", [128, W], "bfloat16"), "mkE": ("sbuf", [128, MKW], "bfloat16"),
            "LB": ("sbuf", [128, 2048], "bfloat16")}
-for _n in ("qN", "q0", "q1", "qO", "dR", "dS", "dF", "qF", "qj", "zz", "nn", "dd", "rr"):
+for _n in ("qN", "q0", "q1", "qO", "dR", "dS", "dF", "qF", "qj", "zz", "nn", "dd", "rr", "r1"):
     SCRATCH[_n] = ("sbuf", [128, K], "bfloat16")
 for _n in ("qv", "zp"):
     SCRATCH[_n] = ("sbuf", [128, K], "float32")
@@ -30,12 +31,12 @@ def _add(dtype, **widths):
         SCRATCH[n] = ("sbuf", [128, w], dtype)
 
 
-_add("bfloat16", wS=2, land0=NB, land1=NB, JR=96, LT=96, mo=768, Rb=192, rest=96, m256=96, Cw=192, dead=192, khb=32, sb=16,
-     cm=96, Eb=96, vb=96, mf=96, Sb=96, HT=768, IT=192, J16=16)
+_add("bfloat16", wS=2, land0=NB, land1=NB, JR=96, LT=96, mo=768, Rb=192, rope=192, rest=96, m256=96, Cw=192, dead=192, khb=32, sb=16,
+     cm=96, Eb=96, vb=96, mf=96, Sb=96, HT=768, IT=192, J16=16, EQ=1152, MN=1152, NEW=NB)
 _add("int32", pi=1, ki=1, ci=4, U=304, UA=288, X=592, H=96, Hb=96, cl=12, kh=24, si=12,
      XB=960, XF=12, XG=24)
 _add("float32", col=40, E16=16, geo=48, Rf=192, m97=192, mt=192, Bm=96, yS=96, al=192, ms=144, fc=144, f1=8,
-     HM=40, WD=24, WO=24, TO=24, ed=24, key=12, EQ=1152, MN=12, w1=12, mk1=96)
+     HM=40, WD=24, WO=24, TO=12, ed=32, key=12, w1=12, mk1=96)
 _add("uint16", OFF=96, OB=96, OL=96, OE=12)
 BANKS = ("g00", "g01", "g10", "g11", "h0", "h1", "k0", "k1")
 for _n in BANKS:
@@ -101,7 +102,122 @@ def rank_program(g, core, T, topo):
                                  m_out)
                 g.wait_ge(T.sem.rls, 2 * count(m_out))
         return
+    if not ORDER:
+        ORDER.extend(orders([calls(g, r, T, topo) for r in range(len(cores))]))
+    calls(g, rank, T, topo)[4](ORDER[rank])
 
+
+ORDER = []
+
+
+def orders(ranks):
+    ops, lead, base = [], {}, [0]
+    for x in ranks:
+        base.append(base[-1] + len(x[0]))
+    for r, (own, ahead, sent, come, issue) in enumerate(ranks):
+        far = {i: base[s] + ranks[s][2][k, r] for (k, s), i in come.items()}
+        for i, (q, fn, sem, cost, waits, order, ev) in enumerate(own):
+            ops.append(((r, q), sem is not None, sem is None and ev is None, cost,
+                        set(base[r] + d for d in waits) | ({far[i]} if i in far else set()), set(base[r] + d for d in order)))
+        lead.update({base[r] + i: x for i, x in ahead.items()})
+    n = len(ops)
+    succ = [[] for _ in ops]
+    for i in range(n):
+        for d in ops[i][4] | ops[i][5]:
+            succ[d].append(i)
+    need = [len(x[4] | x[5]) for x in ops]
+    first = [i for i in range(n) if need[i] == 0]
+    for i in first:
+        for j in succ[i]:
+            need[j] -= 1
+            if need[j] == 0:
+                first.append(j)
+
+    def length(seq, f):
+        end, start, free = {}, {}, {}
+        for i in seq:
+            q, c = ops[i][0], ops[i][3] * (f if ops[i][2] else 1.0)
+            t = max([free.get(q, 0.0)] + [end[d] + WAKE for d in ops[i][4]] + [start[d] for d in ops[i][5]])
+            start[i], end[i] = t, t + c
+            free[q] = t + 0.05 if ops[i][1] else t + c
+        return max(end.values())
+
+    def place(run, ahead, bias):
+        need = [len(x[4] | x[5]) for x in ops]
+        prio = [0.0] * n
+        for i in reversed(first):
+            prio[i] = ops[i][3] + max([prio[j] + (WAKE if i in ops[j][4] else 0.0) for j in succ[i]]
+                                      + [run * lead.get(i, (0, 0))[0] + lead.get(i, (0, 0))[1]])
+        prio = [p + x for p, x in zip(prio, bias)]
+        at = [0.0] * n
+        ready = [[i for i in range(base[r], base[r + 1]) if need[i] == 0] for r in range(len(ranks))]
+        free = {}
+        seq = []
+
+        def coming(q, until):
+            when = {i: max(free.get(ops[i][0], 0.0), at[i]) for i in ready[q[0]]}
+            left, todo, found = {}, [i for i in when if when[i] < until], []
+            while todo:
+                i = todo.pop()
+                if ops[i][0] == q:
+                    found.append((when[i], i))
+                    continue
+                for j in succ[i]:
+                    when[j] = max(when.get(j, at[j]), when[i] + ops[i][3] + WAKE if i in ops[j][4] else when[i])
+                    left[j] = left.get(j, need[j]) - 1
+                    if left[j] == 0 and when[j] < until:
+                        todo.append(j)
+            return found
+
+        while len(seq) < n:
+            t, i = min((max(free.get(ops[i][0], 0.0), at[i]), i) for x in ready for i in x)
+            q = ops[i][0]
+            now = sorted((-prio[i], i) for i in ready[q[0]] if ops[i][0] == q and at[i] <= t + SLACK)
+            later = [(w, k) for w, k in coming(q, t + max(ops[x[1]][3] for x in now)) if w > t + SLACK] if ops[i][2] else []
+            i = None
+            for x in now:
+                c, p = ops[x[1]][3], prio[x[1]]
+                if ops[x[1]][1] or not any(
+                        w < t + c and max(w + prio[k], w + ops[k][3] + p) + ahead * (PROP * c + 1 - PROP) < t + c + prio[k] for w, k in later):
+                    i = x[1]
+                    break
+            if i is None:
+                free[q] = min(later)[0]
+                continue
+            t = max(free.get(q, 0.0), at[i])
+            ready[q[0]].remove(i)
+            seq.append(i)
+            end = t + ops[i][3]
+            free[q] = t + 0.05 if ops[i][1] else end
+            for j in succ[i]:
+                at[j] = max(at[j], end + WAKE if i in ops[j][4] else t)
+                need[j] -= 1
+                if need[j] == 0:
+                    ready[ops[j][0][0]].append(j)
+        return seq
+
+    def both(seq):
+        return length(seq, 1.0) + length(seq, 1.4) / 1.4
+
+    bias = [0.0] * n
+    best = min((both(place(x, y, bias)), x, y) for x in LEADS for y in AHEADS)
+    t, rnd = best[0], np.random.default_rng(1)
+    for k in range(TRIES):
+        new = [float(b + JA * x * (y < JF)) for b, x, y in zip(bias, rnd.normal(size=n), rnd.random(n))]
+        x = both(place(best[1], best[2], new))
+        if x <= t:
+            t, bias = x, new
+    seq = place(best[1], best[2], bias)
+    NOTE[:] = [best, length(seq, 1.0)]
+    return [[i - base[r] for i in seq if ops[i][0][0] == r] for r in range(len(ranks))]
+
+
+NOTE = []
+
+
+def calls(g, rank, T, topo):
+    cores = list(T.cores)
+    core = cores[rank]
     Q = {"v": g.vector, "a": g.scalar, "p": g.tensor, "g": g, "s": g.sync}
     SEM = {"v": "sV", "a": "sA", "p": "sP", "g": "sG"}
     ops = []
@@ -135,81 +251,6 @@ def rank_program(g, core, T, topo):
                 r.append((lo, hi, q, i, kind, step))
         ops.append((q, fn, sem, cost, waits, order - waits, ev))
         return i
-
-    def length(seq, f):
-        end, start, free = {}, {}, {}
-        for i in seq:
-            q, c = ops[i][0], ops[i][3] * (f if ops[i][2] is None and ops[i][6] is None else 1.0)
-            t = max([free.get(q, 0.0)] + [end[d] + WAKE for d in ops[i][4]] + [start[d] for d in ops[i][5]])
-            start[i], end[i] = t, t + c
-            free[q] = t + 0.05 if ops[i][2] is not None else t + c
-        return max(end.values())
-
-    def best_order():
-        tried = [place(x, y, z) for x in LEADS for y in AHEADS for z in JIT]
-        return min(tried, key=lambda seq: length(seq, 1.0) + length(seq, 1.4) / 1.4)
-
-    def place(run, AHEAD, jit):
-        n = len(ops)
-        succ = [[] for _ in ops]
-        need = [0] * n
-        for i in range(n):
-            for d in ops[i][4] | ops[i][5]:
-                succ[d].append(i)
-                need[i] += 1
-        prio = [0.0] * n
-        for i in reversed(range(n)):
-            prio[i] = ops[i][3] + max([prio[j] + (WAKE if i in ops[j][4] else 0.0) for j in succ[i]]
-                                      + [run * lead.get(i, (0, 0))[0] + lead.get(i, (0, 0))[1]])
-        if jit:
-            prio = [p + JA * ((i * 7919 * jit + i * i * 31 * jit) % 1000) / 1000 for i, p in enumerate(prio)]
-        at = [0.0] * n
-        ready = [i for i in range(n) if need[i] == 0]
-        free = {}
-        seq = []
-
-        def coming(q, until):
-            when = {i: max(free.get(ops[i][0], 0.0), at[i]) for i in ready}
-            left, todo, found = {}, [i for i in ready if when[i] < until], []
-            while todo:
-                i = todo.pop()
-                if ops[i][0] == q:
-                    found.append((when[i], i))
-                    continue
-                for j in succ[i]:
-                    when[j] = max(when.get(j, at[j]), when[i] + ops[i][3] + WAKE if i in ops[j][4] else when[i])
-                    left[j] = left.get(j, need[j]) - 1
-                    if left[j] == 0 and when[j] < until:
-                        todo.append(j)
-            return found
-
-        while ready:
-            st = [max(free.get(ops[i][0], 0.0), at[i]) for i in ready]
-            t = min(st)
-            q = ops[ready[st.index(t)]][0]
-            now = sorted(((-prio[i], i) for i, x in zip(ready, st) if ops[i][0] == q and x <= t + SLACK))
-            later = [(w, k) for w, k in coming(q, t + 1.1) if w > t + SLACK]
-            i = None
-            for x in now:
-                c, p = ops[x[1]][3], prio[x[1]]
-                if ops[x[1]][2] is not None or not any(
-                        w < t + c and max(w + prio[k], w + ops[k][3] + p) + AHEAD < t + c + prio[k] for w, k in later):
-                    i = x[1]
-                    break
-            if i is None:
-                free[q] = min(later)[0]
-                continue
-            t = max(free.get(q, 0.0), at[i])
-            ready.remove(i)
-            seq.append(i)
-            end = t + ops[i][3]
-            free[q] = t + 0.05 if ops[i][2] is not None else end
-            for j in succ[i]:
-                at[j] = max(at[j], end + WAKE if i in ops[j][4] else t)
-                need[j] -= 1
-                if need[j] == 0:
-                    ready.append(j)
-        return seq
 
     def issue(seq):
         cnt = {"v": 0, "a": 0, "p": 0, "g": 0}
@@ -402,18 +443,17 @@ def rank_program(g, core, T, topo):
         weights("ZS", WS)
         fill(("geo", 0, 4), 16.0)
         scan(("geo", 8, 11), ("geo", 0, 3), ("E16", 12, 15), Op.add)
-        scan(("geo", 12, 15), ("geo", 0, 3), ("E16", 13, 16), Op.add)
-        ts(W2, ("geo", 9, 10), 16.0, Op.mult)
-        ts(WN, WH, -1.0, Op.mult)
-        weights("ZH", WH)
-        weights("ZN", WN)
+        scan(("geo", 13, 15), ("geo", 0, 2), ("E16", 14, 16), Op.add)
+        act(W2, ("geo", 9, 10), Fn.Copy, scale=16.0)
+        act(WN, ("E16", 13, 14), Fn.Copy, scale=256.0)
+        weights("ZH", WN)
+        weights("ZN", WH)
         weights("Z1", W1)
         weights("Z2", W2)
         for nm, x in (("ID", 1.0), ("NI", -1.0), ("I16", 16.0), ("N16", -16.0), ("ISY", KLT)):
             diag(nm, x)
         act(B1, KC, Fn.Copy, bias=-1760.0, scale=-2048.0)
         act(QB, KC, Fn.Copy, bias=220.0, scale=256.0)
-        act(RB, KC, Fn.Copy, bias=256.0, scale=256.0)
         act(R8, KC, Fn.Copy, bias=2048.0, scale=2048.0)
         ts(("LT", 0, 96), ("JR", 0, 96), KC, Op.is_gt, KLT, Op.mult)
         for c in range(2):
@@ -446,8 +486,10 @@ def rank_program(g, core, T, topo):
         diag("R12", RC0)
         diag("I256", 1.0 / 256)
         ts(("WD", 1, 24, 2), ("w1", 0, 12), KC, Op.add)
-        ts(("TO", 0, 6), ("WD", 1, 12, 2), 1.0 / 256, Op.mult, 8192.0 - W / 256, Op.add)
+        act(("TO", 0, 12), ("WD", 1, 24, 2), Fn.Copy, bias=-W / 256, scale=1.0 / 256)
         fill(("HM", 0, 40), 0.0)
+        fill(("NEW", 0, NB), 0.0)
+        fill(("NEW", 0, NB, 96), 16384.0)
 
     def sm(nm, c, k=0, n=1):
         lo = c * NJ * n + k * NJ
@@ -482,9 +524,9 @@ def rank_program(g, core, T, topo):
         act(mo(r, c, 1), k, Fn.Copy, bias=MO)
 
     def first_rope(c, src):
-        kb = ("k%d" % c, 0, 2 * NJ)
-        word("ZH", odd(kb), src, c * CH)
-        word("ZN", even(kb), src, c * CH, stop=False)
+        for k, nm in enumerate(("ZH", "ZN")):
+            word(nm, ("k%d" % c, (3 + k) * NJ, (4 + k) * NJ), src, c * CH)
+        act(pair("rope", c), ("k%d" % c, 3 * NJ, 5 * NJ), Fn.Copy)
 
     def jmajor(c, src):
         for h in range(2):
@@ -502,21 +544,22 @@ def rank_program(g, core, T, topo):
         act(sm("dead", c, s % 2, 2), m, Fn.Relu, bias=2.0 ** 80 * (MO + 0.5), scale=-2.0 ** 80)
         act(sm("mt", c, s % 2, 2), m, Fn.Copy, bias=8192.0 * (2 - MO) + 131072.0 * s, scale=8192.0)
 
-    def mask(c):
+    def mask(r, c, s):
         m = odd(pair("Rb", c))
+        mins[r, c, s] = []
         for h in range(2):
             bk = gb(c, h)
             if WAYS[h] == "aa":
-                mm([((bk[0], x * NJ, x * NJ + NJ), LJ(8 * h + x), m, x == 0, False) for x in range(8)])
+                mm([((bk[0], x * NJ, x * NJ + NJ), LJ(8 * h + x), m, x == 0, x == 7) for x in range(8)])
             else:
                 mm([((bk[0], x * NJ, x * NJ + NJ), LJ(8 * h + x), m, True, True) for x in range(8)])
         for h in range(2):
             bk, z = gb(c, h), half("zz", c, h)
             if WAYS[h] == "av":
                 act(bk, bk, Fn.Relu, bias=B1, scale=8.0)
-                tt(z, half("qj", c, h), bk, Op.min)
+                mins[r, c, s].append(tt(z, half("qj", c, h), bk, Op.min))
             elif WAYS[h] == "va":
-                tt(half("zp", c, h), half("qv", c, h), bk, Op.min)
+                mins[r, c, s].append(tt(half("zp", c, h), half("qv", c, h), bk, Op.min))
                 act(z, half("zp", c, h), Fn.Relu, bias=B1, scale=8.0)
             elif WAYS[h] == "aa":
                 act(bk, bk, Fn.Relu, bias=R8, scale=-8.0)
@@ -552,9 +595,15 @@ def rank_program(g, core, T, topo):
     def win(off, w=W):
         return T.mkE[:, 0:w].indirect(ap(off))
 
-    def gathered(o, off, q, op, nm, w=W):
+    def gathered(o, off, q, op, nm, w=W, behind=()):
         return emit("v", lambda: g.vector.tensor_tensor(ap(o), T[nm][:, 0:w].indirect(ap(off)), ap(q), op), [(nm, 0, w), off, q],
-                    [o], cost=0.05 + GAT * CYC * wide(o))
+                    [o], cost=0.05 + GAT * CYC * wide(o), behind=behind)
+
+    def picked(o, off, nm, w=W):
+        return emit("a", lambda: g.scalar.activation(ap(o), T[nm][:, 0:w].indirect(ap(off)), Fn.Copy), [(nm, 0, w), off], [o],
+                    cost=0.065 + GAT * CYC * wide(o))
+
+    mins = {}
 
     def step(r, c, s, q0):
         hb, kb = "h%d" % c, ("k%d" % c, 0, 2 * NJ)
@@ -562,6 +611,10 @@ def rank_program(g, core, T, topo):
         Rb = odd(pair("Rb", c))
         place_of(c, s)
         mm([(S, M("ID"), sm("Cw", c, s % 2, 2), True, False), (S, M("ID"), sm("dead", c, s % 2, 2), False, False)])
+        if s == 1:
+            hi, lo = sm("rope", c, 0, 2), sm("rope", c, 1, 2)
+            mm([(odd(kb), M("ID"), hi, True, False), (odd(kb), M("ID"), lo, False, True),
+                (even(kb), M("NI"), hi, True, False), (even(kb), M("NI"), lo, False, False)])
         if s == 2:
             mm([(odd(kb), M("I16"), sm("rest", c), True, True), (even(kb), M("N16"), sm("rest", c), True, False)])
         if s == 3:
@@ -569,7 +622,13 @@ def rank_program(g, core, T, topo):
             mm([(odd(kb), M("I16"), Rb, True, False), (odd(kb), M("N16"), sm("m256", c), False, True),
                 (even(kb), M("N16"), Rb, True, False), (even(kb), M("I16"), sm("m256", c), False, False)])
         tt(even(pair("XB", c, s - 1, 5)), sm("H", c), sm("mt", c, s % 2, 2), Op.add)
-        gathered(chunk("nn", c), sm("OFF", c), chunk(q0, c), Op.subtract, TABLE[r])
+        other = mins.get((r, 1 - c, s + c), []) if APART else []
+        if SPLIT:
+            for h in range(2):
+                p = 2 * c + h
+                gathered(half("nn", c, h), ("OFF", 24 * p, 24 * p + 24), half(q0, c, h), Op.subtract, TABLE[r], behind=other)
+        else:
+            gathered(chunk("nn", c), sm("OFF", c), chunk(q0, c), Op.subtract, TABLE[r], behind=other)
         word("ZS", S, "nn", c * CH, start=False)
         if s < 4:
             word("Z1" if s == 1 else "Z2", even(kb), "nn", c * CH, start=False)
@@ -584,12 +643,14 @@ def rank_program(g, core, T, topo):
         scan(pair("XB", c, s, 5), hit, pair("XB", c, s - 1, 5), Op.max)
 
     def later_steps(r, q0):
-        for s in range(2, 5):
-            for c in range(2):
-                mask(c)
+        for k in range(1, 8):
+            c, s = k % 2, k // 2 + 1
+            if k < 7:
+                mask(r, 1 - c, (k + 1) // 2 + 1)
+            if s > 1:
                 from_length(r, c, s)
                 sums(c, False)
-                step(r, c, s, q0)
+            step(r, c, s, q0)
 
     def learn(r, c, q0, dest, after):
         B = odd(pair("XB", c, 4, 5))
@@ -598,15 +659,23 @@ def rank_program(g, core, T, topo):
         cp(sm("OB", c), sm("Hb", c))
         for h in range(2):
             p = 2 * c + h
-            gathered(half("dd", c, h), ("OB", 24 * p, 24 * p + 24), half(q0, c, h), Op.subtract, TABLE[r])
-            after(p, gathered(dest(p), ("OL", 24 * p, 24 * p + 24), half("dd", c, h), Op.mult, "LT", 96))
+            ob, ol, d = ("OB", 24 * p, 24 * p + 24), ("OL", 24 * p, 24 * p + 24), half("dd", c, h)
+            if p not in BY_SCALAR[r]:
+                gathered(d, ob, half(q0, c, h), Op.subtract, TABLE[r])
+                after(p, gathered(dest(p), ol, d, Op.mult, "LT", 96))
+                continue
+            bk = (("k%d", "h%d")[h] % c, 0, NB)
+            picked(half("rr", c, h), ol, "LT", 96)
+            picked(d, ob, TABLE[r])
+            mm([(bk, M("NI"), half(q0, c, h), True, False)])
+            mm([(bk, M("ID"), d, False, True)])
+            after(p, tt(dest(p), bk, half("rr", c, h), Op.mult))
 
-    sends = [[], []]
+    sent, come = {}, {}
 
     def send(k, p, after=(), behind=()):
         s = goes[p]
         if s == rank:
-            sends[k] += after[:k]
             return
         b = (("qN", "dS")[k], NB * p, NB * p + NB)
         rel = relay_of(core, cores[s], cores, topo)
@@ -618,19 +687,20 @@ def rank_program(g, core, T, topo):
             dst, sem = T[LANDS[k]][:, x:x + NB], "arr%d%d" % (k, rank)
         else:
             dst, sem = T["land%d" % k][:], "rin%d" % k
-        sends[k].append(emit("g", lambda: g.remote_dma(dst, ap(b), T.sem[sem], T.sem.sent, pid, rid, m), [b], [], None, 0.3,
-                             ("sent", count(m)), after, behind))
+        sent[k, s] = emit("g", lambda: g.remote_dma(dst, ap(b), T.sem[sem], T.sem.sent, pid, rid, m), [b], [], None, 0.3,
+                          ("sent", count(m)), after, behind)
 
     def arrivals(k):
         for p in range(4):
             s = came[p]
             if s == rank:
                 continue
-            there = goes_order(s, cores, topo).index(rank)
             rel = relay_of(cores[s], core, cores, topo)
             n = count(topo.mask(cores[s] if rel is None else rel, core))
-            emit("x%d%d" % (k, s), None, [], [(LANDS[k], NB * p, NB * p + NB)], None, (TNEAR if rel is None else TFAR) + 3 - 3 * k,
-                 ("arr%d%d" % (k, s), n), sends[k][:2 * (max(there, p) // 2) + 2] if k else sends[k])
+            come[k, s] = emit("x%d%d" % (k, s), None, [], [(LANDS[k], NB * p, NB * p + NB)], None,
+                              (TNEAR if rel is None else TFAR) + 4 - 4 * k, ("arr%d%d" % (k, s), n))
+
+    EB = "g11"
 
     def edits():
         e = goes.index(0)
@@ -656,6 +726,8 @@ def rank_program(g, core, T, topo):
         tt(("ed", 0, 6), F, Bb, Op.is_gt)
         ts(("ed", 8, 14), Bb, 0.0, Op.is_gt, -8192.0, Op.mult)
         tt(ned, ("ed", 0, 6), ("ed", 8, 14), Op.mult)
+        far = ("ed", 24, 30)
+        act(far, ned, Fn.Copy, bias=16384.0, scale=3.0)
         ts(("cl", 0, 12), FB, 4095, Op.bitwise_and)
         ts(("kh", 0, 12), FB, 4032, Op.bitwise_and)
         ts(("kh", 12, 24), FB, 63, Op.bitwise_and)
@@ -665,33 +737,36 @@ def rank_program(g, core, T, topo):
         cp(("khb", 16, 28), ("kh", 12, 24))
         for o in (0, 6):
             tt(("khb", o, o + 6), ("kh", o, o + 6), ned, Op.add)
-            tt(("key", o, o + 6), ("cl", o, o + 6), ned, Op.add)
-            tt(("TO", 8 + o, 14 + o), ("TO", 0, 6), ned, Op.add)
+            tt(("key", o, o + 6), ("cl", o, o + 6), far, Op.add)
         tt(("WD", 0, 24, 2), ("cl", 0, 12), ("WD", 1, 24, 2), Op.subtract)
         mm([(("k0", 0, 192), M("I256"), ("IT", 0, 192), True, False)])
         mm([(("k0", j, 192, 16), LJ(j), ("khb", 16, 28), False, False) for j in range(16)])
         mm([(("k0", j, 192, 16), LJ(j), ("khb", 0, 12), False, j == 15) for j in range(16)])
-        mm([(("k1", j, 192, 16), LJ(j), ("sb", 0, 12), True, True) for j in range(16)])
-        mm([(("k1", 192, 288), M("CA"), de, True, True)])
-        act(("mf", 0, 96), ("k1", 96, 192), Fn.Copy, bias=-2.0)
-        ts(("mk1", 0, 96), ("k1", 0, 96), KK, Op.is_equal)
-        tt(("cm", 0, 96), ("k1", 192, 288), ("mk1", 0, 96), Op.mult)
-        mm([(("k1", 0, 96), M("ISY"), qe, True, False), (("k1", 0, 96), M("RS"), ("cm", 0, 96), False, True)])
+        mm([((EB, j, 192, 16), LJ(j), ("sb", 0, 12), True, True) for j in range(16)])
+        mm([((EB, 192, 288), M("CA"), de, True, True)])
+        act(("mf", 0, 96), (EB, 96, 192), Fn.Copy, bias=-2.0)
+        ts(("mk1", 0, 96), (EB, 0, 96), KK, Op.is_equal)
+        tt(("cm", 0, 96), (EB, 192, 288), ("mk1", 0, 96), Op.mult)
+        mm([((EB, 0, 96), M("ISY"), qe, True, False), ((EB, 0, 96), M("RS"), ("cm", 0, 96), False, True)])
         for x in range(12):
             w = x // 6
             eq = ("EQ", 96 * x, 96 * x + 96)
             act(eq, ("k0", 96 * w, 96 * w + 96), Fn.Abs, bias=("key", x, x + 1), scale=-1.0)
-            least(("MN", x, x + 1), eq, Op.min)
-        cp(("Eb", 0, 96), ("k1", 0, 96))
-        tt(("HM", 17, 40, 2), ("MN", 0, 12), ("TO", 8, 20), Op.is_equal)
+            if x % 4 == 3:
+                a, o = ("EQ", 96 * x - 288, 96 * x + 96), ("MN", 96 * x - 288, 96 * x + 96)
+                emit("v", lambda a=a, o=o: g.vector.tensor_tensor_scan(ap(o), ap(("NEW", 0, NB)), ap(a), 0.0, Op.add, Op.min),
+                     [a, ("NEW", 0, NB)], [o], cost=cost(o, [a]))
+        act(("Eb", 0, 96), (EB, 0, 96), Fn.Copy)
+        tt(("HM", 17, 40, 2), ("MN", 95, 1152, 96), ("TO", 0, 12), Op.is_equal)
         scan(("WO", 0, 24), ("HM", 16, 40), ("WD", 0, 24), Op.add)
         cp(("OE", 0, 12), ("WO", 1, 24, 2))
         oF, oB, full_w = ("OE", 0, 6), ("OE", 6, 12), ("mkE", 0, MKW)
         emit("v", lambda: g.vector.tensor_copy(win(oF, MKW), ap(("Eb", 0, 96))), [oF, ("Eb", 0, 96)], [full_w], cost=0.35)
         emit("v", lambda: g.vector.tensor_copy(ap(("vb", 0, 96)), win(oB, MKW)), [oB, full_w], [("vb", 0, 96)], cost=0.2)
-        mm([(("k1", 0, 96), M("ISY"), ("vb", 0, 96), True, False), (("k1", 0, 96), M("DN"), ("vb", 0, 96), False, False),
-            (("k1", 0, 96), M("R12"), ("mf", 0, 96), False, True)])
-        cp(("Sb", 0, 96), ("k1", 0, 96))
+        o = ("k0", 0, 96)
+        mm([(o, M("R12"), ("mf", 0, 96), True, False)])
+        mm([(o, M("ISY"), ("vb", 0, 96), False, False), (o, M("DN"), ("vb", 0, 96), False, True)])
+        act(("Sb", 0, 96), o, Fn.Copy)
         emit("v", lambda: g.vector.tensor_copy(win(oB, MKW), ap(("Sb", 0, 96))), [oB, ("Sb", 0, 96)], [full_w], cost=0.35)
 
     consts_search()
@@ -712,47 +787,48 @@ def rank_program(g, core, T, topo):
             act(half("q0", c, h), half("qN", c, h), Fn.Copy, scale=KLT)
         first_rope(c, "qN")
         jmajor(c, "qN")
-        step(0, c, 1, "q0")
+    step(0, 0, 1, "q0")
     later_steps(0, "q0")
-    for c in range(2):
-        learn(0, c, "q0", lambda p: ("dR", own, own + NB) if goes[p] == rank else ("dS", NB * p, NB * p + NB),
-              lambda p, i: send(1, p, [i]))
     for c in range(2):
         for h in range(2):
             mm([(gb(c, h), LJ(12), half("qO", c, h), True, True)])
-            act(half("rr", c, h), gb(c, h), Fn.Relu, bias=RB, scale=-256.0)
-            mm([(gb(c, h), M("ID"), half("qO", c, h), True, False), (gb(c, h), M("NI"), half("rr", c, h), False, False)])
+            act(half("r1", c, h), gb(c, h), Fn.Relu, bias=NBI, scale=256.0)
         first_length(1, c, "qO")
+        first_rope(c, "qO")
         from_length(1, c, 1)
+    for c in range(2):
+        learn(0, c, "q0", lambda p: ("dR", own, own + NB) if goes[p] == rank else ("dS", NB * p, NB * p + NB),
+              lambda p, i: send(1, p, [i]))
     edits()
     arrivals(1)
     for c in range(2):
         for h in range(2):
+            mm([(gb(c, h), M("ISY"), half("qO", c, h), True, False)])
             mm([(gb(c, h), M("ID"), half("dR", c, h), False, True)])
-            act(half("zz", c, h), gb(c, h), Fn.Relu)
-        sums(c, True)
-        for h in range(2):
-            mm([(gb(c, h), M("ISY"), half("qO", c, h), True, False), (gb(c, h), M("ID"), half("dR", c, h), False, True)])
+            tt(half("zz", c, h), gb(c, h), half("r1", c, h), Op.min)
             act(half("q1", c, h), gb(c, h), Fn.Copy)
-        first_rope(c, "qO")
+        sums(c, True)
         jmajor(c, "q1")
-        step(1, c, 1, "q1")
+    step(1, 0, 1, "q1")
     later_steps(1, "q1")
 
     def out(p, i):
         c, h = p // 2, p % 2
         b, x = half("qF", c, h), NB * came[p]
-        mm([(gb(c, h), M("ID"), half("dF", c, h), False, True)])
-        act(b, gb(c, h), Fn.Copy)
+        if p in ADD_V:
+            tt(b, gb(c, h), half("dF", c, h), Op.add)
+        else:
+            mm([(gb(c, h), M("ID"), half("dF", c, h), False, True)])
+            act(b, gb(c, h), Fn.Copy)
         lead[emit("s", lambda: g.sync.dma_start(T.yq[:, x:x + NB], ap(b)), [b], [], "dy%d" % p, 1.5)] = (1 - c, 0.6 - 0.6 * h)
 
     for c in range(2):
         for h in range(2):
-            mm([(gb(c, h), M("ID"), half("qO", c, h), True, False), (gb(c, h), M("ID"), half("dR", c, h), False, False)])
+            mm([(gb(c, h), M("ID"), half("qO", c, h), True, False), (gb(c, h), M("ID"), half("dR", c, h), False,
+                                                                    2 * c + h in ADD_V)])
         learn(1, c, "q1", lambda p: ("dF", NB * p, NB * p + NB), out)
         ts(sm("Bm", c), odd(pair("XB", c, 4, 5)), -1.0, Op.add)
-        tt(sm("yS", c), sm("Hb", c), sm("Bm", c), Op.min)
         for p in (2 * c, 2 * c + 1):
-            b, x = ("yS", 24 * p, 24 * p + 24), 24 * came[p]
-            emit("s", lambda b=b, x=x: g.sync.dma_start(T.yb[:, x:x + 24], ap(b)), [b], [], "db%d" % p, 1.2)
-    issue(best_order())
+            tt(("yS", 24 * came[p], 24 * came[p] + 24), ("Hb", 24 * p, 24 * p + 24), ("Bm", 24 * p, 24 * p + 24), Op.min)
+    emit("s", lambda: g.sync.dma_start(T.yb[:], T.yS[:]), [("yS", 0, 96)], [], "db0", 1.2)
+    return ops, lead, sent, come, issue

@@ -2,26 +2,29 @@ import math
 import numpy as np
 from concourse.mybir import AluOpType as Op, ActivationFunctionType as Fn, AxisListType
 
-W, K, NB = 4096, 1536, 384
-CH, NJ = 768, 48
+W, K, NB, NU = 4096, 1536, 384, 128
+CH, NT, NC = 512, 32, 3
 MKW = W + 128
 LN2 = math.log(2.0)
-MO = 136.0
-CYC, PEC, WAKE, SLACK = 0.00083, 0.00042, 0.14, 0.04
-GAT, TMK, TFAR, TNEAR, PROP = 1.5, 7.0, 3.6, 1.8, 0.7
-LEADS, AHEADS, TRIES, JA, JF = (2.5, 3.5), (0.4, 0.6, 0.8), 0, 0.5, 0.05
-WAYS, BY_SCALAR, APART, SPLIT, ADD_V = ("av", "va"), ((1, 3), (1, 3)), False, False, (3,)
+MAGIC = 1.5 * 2.0 ** 23
+NONE = -136.0 * 8192 - 2048
+TILT = 0.000435
+CYC, PEC, WAKE, ISSUE = 0.00083, 0.00042, 0.19, 0.05
+GAT, TMK, TFAR, TNEAR, APART, TSEND, TFIRST = 1.5, 6.0, 4.0, 2.0, 1.9, 0.5, 3.0
+FIXV, FIXA, GW = 0.035, 0.055, 32
+AHEAD = (3.2, 2.0, 0.0)
+LEAD, SLOW, FACTORS = 1.0, 1.05, ((1.0, 0.2, 1.0), (1.0, 0.16, 1.2), (1.35, 0.16, 1.35))
+TRIES, SPAN, SHIFT, SHARE = 1200, 15.0, 0.4, 0.06
+BY_SCALAR = ((0, 1, 3), (1, 3, 5))
+ADD_V = (4, 5)
 
-_words = ["XP", "Z64", "ZX", "ZY", "ZS", "ZL", "ZH", "ZN", "Z1", "Z2"]
-_mats = ["AB", "ONE", "ID", "NI", "I16", "N16", "I256", "ISY", "SRC", "CAQ", "BD", "CA", "JP", "RS", "DN", "R12"]
+_mats = ["XP", "ID", "NI", "I97", "I8K", "I256", "ISY", "N8K", "CA", "DN", "R12", "T2K", "CST", "ZM", "half", "I13", "hf2"]
 SCRATCH = {"mkT": ("sbuf", [128, W], "bfloat16"), "mkE": ("sbuf", [128, MKW], "bfloat16"),
-           "LB": ("sbuf", [128, 2048], "bfloat16")}
-for _n in ("qN", "q0", "q1", "qO", "dR", "dS", "dF", "qF", "qj", "zz", "nn", "dd", "rr", "r1"):
+           "LB": ("sbuf", [128, 512], "bfloat16"), "HW": ("sbuf", [128, 32 * 4 + 3, 4], "float16"),
+           "HV": ("sbuf", [128, 32 * 7 + 3, 4], "bfloat16"),
+           "khb": ("sbuf", [128, 48], "float16")}
+for _n in ("qN", "q0", "qO", "qP", "q1", "dR", "dS", "dF", "qF", "zz", "nn", "dd", "rr"):
     SCRATCH[_n] = ("sbuf", [128, K], "bfloat16")
-for _n in ("qv", "zp"):
-    SCRATCH[_n] = ("sbuf", [128, K], "float32")
-for _n in _words:
-    SCRATCH[_n] = ("sbuf", [128, 144], "bfloat16")
 for _n in _mats:
     SCRATCH[_n] = ("sbuf", [128, 128], "bfloat16")
 
@@ -31,19 +34,19 @@ def _add(dtype, **widths):
         SCRATCH[n] = ("sbuf", [128, w], dtype)
 
 
-_add("bfloat16", wS=2, land0=NB, land1=NB, JR=96, LT=96, mo=768, Rb=192, rope=192, rest=96, m256=96, Cw=192, dead=192, khb=32, sb=16,
-     cm=96, Eb=96, vb=96, mf=96, Sb=96, HT=768, IT=192, J16=16, EQ=1152, MN=1152, NEW=NB)
-_add("int32", pi=1, ki=1, ci=4, U=304, UA=288, X=592, H=96, Hb=96, cl=12, kh=24, si=12,
-     XB=960, XF=12, XG=24)
-_add("float32", col=40, E16=16, geo=48, Rf=192, m97=192, mt=192, Bm=96, yS=96, al=192, ms=144, fc=144, f1=8,
-     HM=40, WD=24, WO=24, TO=12, ed=32, key=12, w1=12, mk1=96)
-_add("uint16", OFF=96, OB=96, OL=96, OE=12)
-BANKS = ("g00", "g01", "g10", "g11", "h0", "h1", "k0", "k1")
+_add("bfloat16", wS=2, land0=NB, land1=NB, JR=96, LT=96, ONE=128, IO=36, MK=36, W0=106, W1=288, W2=288, WS=40, MB=480, SPM=384, MG=96,
+     MKG=36, M12=36, PM=384, OF=96, qK=1152, f0=768, sl=1728, ET=768, Cw=192, Cx=192, dead=64, none=96, MS=984, NM=160, sb=48, cm=96, Eb=96, vb=96, mf=96, Sb=96, IT=192,
+     J16=16, EQ=1152, MN=1152, NEW=NB)
+_add("int32", pi=1, ki=2, ci=4, X=288, H=96)
+_add("float32", col=48, D0=288, yS=96, HM=40, WD=24, WO=24, TO=12, ed=96, key=12, w1=12, w2=12, mk1=96, BT=480, FT=160)
+_add("uint16", OFF=96, OB=192, OE=12)
+BANKS = ("Z0", "Z1", "Z2", "B0", "B1", "B2", "SP", "SQ")
 for _n in BANKS:
     SCRATCH[_n] = ("psum", [128, 512], "float32")
-SEMAPHORES = ["sV", "sA", "sP", "sG", "dw", "dq0", "dq1", "dq2", "dq3", "dq4", "dm0", "dm1", "dm2", "dy0", "dy1", "dy2", "dy3",
-              "db0", "db1", "db2", "db3", "sent", "rin0", "rin1", "rls"]
-SEMAPHORES += ["arr%d%d" % (_k, _r) for _k in range(2) for _r in range(4)]
+SEMAPHORES = ["sV", "sA", "sP", "sG", "dw", "dm0", "dm1", "dm2", "db", "sent", "rls"]
+SEMAPHORES += ["d%s%d" % (_k, _i) for _k in "qoy" for _i in range(12)]
+SEMAPHORES += ["rin%d%d" % (_k, _u) for _k in range(2) for _u in range(3)]
+SEMAPHORES += ["arr%d%d%d" % (_k, _r, _u) for _k in range(2) for _r in range(4) for _u in range(3)]
 
 
 def relay_of(src, dst, cores, topo):
@@ -68,12 +71,37 @@ def way(a, b, cores, topo):
 
 def goes_order(rank, cores, topo):
     n = len(cores)
-    rest = sorted(range(1, n), key=lambda s: ((way(rank, s, cores, topo) + 1) % 3, (s - rank) % n))
-    return [0] + rest
+    blocks = sorted(range(n), key=lambda s: (-way(rank, s, cores, topo), s ^ rank))
+    return [(0, 0)] + [(s, u) for s in blocks for u in range(3) if (s, u) != (0, 0)]
 
 
 def came_order(rank, cores, topo):
-    return sorted(range(len(cores)), key=lambda s: (goes_order(s, cores, topo).index(rank) // 2, way(s, rank, cores, topo)))
+    def when(x):
+        at = goes_order(x[0], cores, topo).index((rank, x[1])) // 4
+        return (APART * at + (0.0, TNEAR, TFAR)[way(x[0], rank, cores, topo)], x[0] ^ rank, x[1])
+    return sorted([(s, u) for s in range(len(cores)) for u in range(3)], key=when)
+
+
+def runs(order, cut):
+    out = []
+    for i, x in enumerate(order):
+        if i % cut and order[i - 1] == (x[0], x[1] - 1):
+            out[-1][1] += 1
+        else:
+            out.append([i, 1])
+    return out
+
+
+def pieces(k, a, b, cores, topo):
+    src, dst = goes_order(a, cores, topo), came_order(b, cores, topo)
+    out = []
+    for u in range(3):
+        i, j = src.index((b, u)), dst.index((a, u))
+        if out and (i, j) == (out[-1][1] + out[-1][3], out[-1][2] + out[-1][3]) and not (k and i % 4 == 0):
+            out[-1][3] += 1
+        else:
+            out.append([u, i, j, 1])
+    return out
 
 
 def count(mask):
@@ -92,15 +120,17 @@ def rank_program(g, core, T, topo):
             for b in cores:
                 if a == b or relay_of(a, b, cores, topo) != core:
                     continue
-                r = T.rank_of(a)
+                ra, rb = T.rank_of(a), T.rank_of(b)
                 m_out = topo.mask(core, b)
                 rid, pid = topo.addr(b, core)
-                p = NB * came_order(T.rank_of(b), cores, topo).index(r)
+                n = 0
                 for k in range(2):
-                    g.wait_ge(T.sem["rin%d" % k], count(topo.mask(a, core)))
-                    g.remote_dma(T[LANDS[k]][:, p:p + NB], T["land%d" % k][:], T.sem["arr%d%d" % (k, r)], T.sem.rls, pid, rid,
-                                 m_out)
-                g.wait_ge(T.sem.rls, 2 * count(m_out))
+                    for u, i, j, w in sorted(pieces(k, ra, rb, cores, topo), key=lambda x: x[1]):
+                        g.wait_ge(T.sem["rin%d%d" % (k, u)], count(topo.mask(a, core)))
+                        g.remote_dma(T[LANDS[k]][:, NU * j:NU * (j + w)], T["land%d" % k][:, NU * u:NU * (u + w)],
+                                     T.sem["arr%d%d%d" % (k, ra, u)], T.sem.rls, pid, rid, m_out)
+                        n += count(m_out)
+                g.wait_ge(T.sem.rls, n)
         return
     if not ORDER:
         ORDER.extend(orders([calls(g, r, T, topo) for r in range(len(cores))]))
@@ -114,102 +144,99 @@ def orders(ranks):
     ops, lead, base = [], {}, [0]
     for x in ranks:
         base.append(base[-1] + len(x[0]))
-    for r, (own, ahead, sent, come, issue) in enumerate(ranks):
-        far = {i: base[s] + ranks[s][2][k, r] for (k, s), i in come.items()}
+    for r, (own, ahead, sent, come, issue, names) in enumerate(ranks):
+        far = {i: base[s] + ranks[s][2][k, r, u] for (k, s, u), i in come.items()}
         for i, (q, fn, sem, cost, waits, order, ev) in enumerate(own):
             ops.append(((r, q), sem is not None, sem is None and ev is None, cost,
                         set(base[r] + d for d in waits) | ({far[i]} if i in far else set()), set(base[r] + d for d in order)))
         lead.update({base[r] + i: x for i, x in ahead.items()})
     n = len(ops)
+    names = {}
+    name = [names.setdefault(x, len(names)) for y in ranks for x in y[5]]
+    cost = [x[3] * (SLOW if x[2] and x[0][1] == "p" else 1.0) for x in ops]
+    hold = [ISSUE if x[1] else c for x, c in zip(ops, cost)]
+    pred = [[(d, cost[d] + WAKE) for d in x[4]] + [(d, hold[d] if ops[d][0] == x[0] else 0.0) for d in x[5]] for x in ops]
     succ = [[] for _ in ops]
     for i in range(n):
-        for d in ops[i][4] | ops[i][5]:
-            succ[d].append(i)
-    need = [len(x[4] | x[5]) for x in ops]
+        for d, lag in pred[i]:
+            succ[d].append((i, lag))
+
+    def listed(key, before):
+        key = list(key)
+        for i in (first if before is pred else first[::-1]):
+            for d, lag in before[i]:
+                if key[d] >= key[i]:
+                    key[i] = key[d] + 1e-7
+        return sorted(range(n), key=lambda i: key[i])
+
+    def length(seq, f, wake=WAKE, pf=None):
+        end, start, free = [0.0] * n, [0.0] * n, {}
+        for i in seq:
+            q, dma, comp, c, waits, order = ops[i]
+            t = free.get(q, 0.0)
+            for d in waits:
+                t = max(t, end[d] + wake)
+            for d in order:
+                t = max(t, start[d])
+            start[i], end[i] = t, t + (c * (pf if pf and q[1] == "p" else f) if comp else c)
+            free[q] = t + ISSUE if dma else end[i]
+        ends = [max(end[base[r]:base[r + 1]]) for r in range(len(ranks))]
+        return (max(ends) + sum(ends) / len(ends)) / 2
+
+    def sweep(key, back):
+        before = succ if back else pred
+        at, slots = [0.0] * n, {}
+        for i in listed(key, before):
+            t = cost[i] + LEAD * lead.get(i, 0) if back else 0.0
+            for j, lag in before[i]:
+                t = max(t, at[j] + lag)
+            h = hold[i]
+            if back:
+                t -= h
+            s = slots.setdefault(ops[i][0], [])
+            lo, hi = 0, len(s)
+            while lo < hi:
+                k = (lo + hi) // 2
+                if s[k][1] <= t + 1e-9:
+                    lo = k + 1
+                else:
+                    hi = k
+            while lo < len(s) and s[lo][0] < t + h - 1e-9:
+                t = s[lo][1]
+                lo += 1
+            s.insert(lo, (t, t + h))
+            at[i] = t + h if back else t
+        return at
+
+    def tight(at, most=1e9):
+        at = sweep([-x for x in sweep([-(a + h) for a, h in zip(at, hold)], True)], False)
+        seq = listed(at, pred)
+        t = [length(seq, *FACTORS[0])]
+        if t[0] > most:
+            return 1e9, at, seq, t[0]
+        t += [length(seq, f, w, pf) / f for f, w, pf in FACTORS[1:]]
+        return sum(t) / len(t), at, seq, t[0]
+
+    need = [len(x) for x in pred]
     first = [i for i in range(n) if need[i] == 0]
     for i in first:
-        for j in succ[i]:
+        for j, lag in succ[i]:
             need[j] -= 1
             if need[j] == 0:
                 first.append(j)
-
-    def length(seq, f):
-        end, start, free = {}, {}, {}
-        for i in seq:
-            q, c = ops[i][0], ops[i][3] * (f if ops[i][2] else 1.0)
-            t = max([free.get(q, 0.0)] + [end[d] + WAKE for d in ops[i][4]] + [start[d] for d in ops[i][5]])
-            start[i], end[i] = t, t + c
-            free[q] = t + 0.05 if ops[i][1] else t + c
-        return max(end.values())
-
-    def place(run, ahead, bias):
-        need = [len(x[4] | x[5]) for x in ops]
-        prio = [0.0] * n
-        for i in reversed(first):
-            prio[i] = ops[i][3] + max([prio[j] + (WAKE if i in ops[j][4] else 0.0) for j in succ[i]]
-                                      + [run * lead.get(i, (0, 0))[0] + lead.get(i, (0, 0))[1]])
-        prio = [p + x for p, x in zip(prio, bias)]
-        at = [0.0] * n
-        ready = [[i for i in range(base[r], base[r + 1]) if need[i] == 0] for r in range(len(ranks))]
-        free = {}
-        seq = []
-
-        def coming(q, until):
-            when = {i: max(free.get(ops[i][0], 0.0), at[i]) for i in ready[q[0]]}
-            left, todo, found = {}, [i for i in when if when[i] < until], []
-            while todo:
-                i = todo.pop()
-                if ops[i][0] == q:
-                    found.append((when[i], i))
-                    continue
-                for j in succ[i]:
-                    when[j] = max(when.get(j, at[j]), when[i] + ops[i][3] + WAKE if i in ops[j][4] else when[i])
-                    left[j] = left.get(j, need[j]) - 1
-                    if left[j] == 0 and when[j] < until:
-                        todo.append(j)
-            return found
-
-        while len(seq) < n:
-            t, i = min((max(free.get(ops[i][0], 0.0), at[i]), i) for x in ready for i in x)
-            q = ops[i][0]
-            now = sorted((-prio[i], i) for i in ready[q[0]] if ops[i][0] == q and at[i] <= t + SLACK)
-            later = [(w, k) for w, k in coming(q, t + max(ops[x[1]][3] for x in now)) if w > t + SLACK] if ops[i][2] else []
-            i = None
-            for x in now:
-                c, p = ops[x[1]][3], prio[x[1]]
-                if ops[x[1]][1] or not any(
-                        w < t + c and max(w + prio[k], w + ops[k][3] + p) + ahead * (PROP * c + 1 - PROP) < t + c + prio[k] for w, k in later):
-                    i = x[1]
-                    break
-            if i is None:
-                free[q] = min(later)[0]
-                continue
-            t = max(free.get(q, 0.0), at[i])
-            ready[q[0]].remove(i)
-            seq.append(i)
-            end = t + ops[i][3]
-            free[q] = t + 0.05 if ops[i][1] else end
-            for j in succ[i]:
-                at[j] = max(at[j], end + WAKE if i in ops[j][4] else t)
-                need[j] -= 1
-                if need[j] == 0:
-                    ready[ops[j][0][0]].append(j)
-        return seq
-
-    def both(seq):
-        return length(seq, 1.0) + length(seq, 1.4) / 1.4
-
-    bias = [0.0] * n
-    best = min((both(place(x, y, bias)), x, y) for x in LEADS for y in AHEADS)
-    t, rnd = best[0], np.random.default_rng(1)
+    tail = [0.0] * n
+    for i in reversed(first):
+        tail[i] = max([cost[i] + LEAD * lead.get(i, 0)] + [tail[j] + lag for j, lag in succ[i]])
+    best = tight(sweep([-x for x in tail], False))
+    rnd = np.random.default_rng(1)
     for k in range(TRIES):
-        new = [float(b + JA * x * (y < JF)) for b, x, y in zip(bias, rnd.normal(size=n), rnd.random(n))]
-        x = both(place(best[1], best[2], new))
-        if x <= t:
-            t, bias = x, new
-    seq = place(best[1], best[2], bias)
-    NOTE[:] = [best, length(seq, 1.0)]
-    return [[i - base[r] for i in seq if ops[i][0][0] == r] for r in range(len(ranks))]
+        lo = float(rnd.random()) * best[0] - SPAN / 2
+        move = (rnd.normal(size=len(names)) * SHIFT * (rnd.random(len(names)) < SHARE)).tolist()
+        new = tight([a + move[name[i]] if lo < a < lo + SPAN else a for i, a in enumerate(best[1])], best[3] + 0.2)
+        if new[0] <= best[0]:
+            best = new
+    NOTE[:] = [best[0], length(best[2], 1.0), length(best[2], 1.4)]
+    return [[i - base[r] for i in best[2] if ops[i][0][0] == r] for r in range(len(ranks))]
 
 
 NOTE = []
@@ -220,7 +247,7 @@ def calls(g, rank, T, topo):
     core = cores[rank]
     Q = {"v": g.vector, "a": g.scalar, "p": g.tensor, "g": g, "s": g.sync}
     SEM = {"v": "sV", "a": "sA", "p": "sP", "g": "sG"}
-    ops = []
+    ops, names, seen = [], [], {}
     rec = {}
     lead = {}
 
@@ -230,6 +257,10 @@ def calls(g, rank, T, topo):
         for kind, lst in (("r", reads), ("w", writes)):
             for b in lst:
                 nm, lo, hi, step = (b + (1,))[:4]
+                if nm in ("HW", "HV"):
+                    step = 1
+                if isap(b[-1]):
+                    nm += "32"
                 r = rec.setdefault(nm, [])
                 if nm in BANKS:
                     for x in r:
@@ -249,6 +280,9 @@ def calls(g, rank, T, topo):
                         r[:] = [x for x in r if not (lo <= x[0] and x[1] <= hi
                                                      and (step == 1 or (x[5] == step and (x[0] - lo) % step == 0)))]
                 r.append((lo, hi, q, i, kind, step))
+        x = (q,) + tuple((writes + reads)[0][:3])
+        seen[x] = seen.get(x, 0) + 1
+        names.append(x + (seen[x],))
         ops.append((q, fn, sem, cost, waits, order - waits, ev))
         return i
 
@@ -298,20 +332,23 @@ def calls(g, rank, T, topo):
         await_all("g", list(total.items()))
 
     def wide(b):
-        return (b[2] - b[1] + (b[3] - 1 if len(b) > 3 else 0)) // (b[3] if len(b) > 3 else 1)
+        step = b[3] if len(b) > 3 else 1
+        return (b[2] - b[1] + step - 1) // step * (4 if b[0] in ("HW", "HV") and step > 1 else 1)
 
     def cost(out, ins, two=False):
         n = wide(out)
         if two:
             n *= 1 if any(b[0] in BANKS for b in ins) else 2
-        elif all(SCRATCH[b[0]][2] in ("bfloat16", "uint16") for b in [out] + ins):
+        elif all(SCRATCH[b[0]][2] in ("bfloat16", "uint16", "float16") for b in [out] + ins):
             n /= 2
-        return max(64, n) * CYC + 0.03
+        return max(64, n) * CYC + FIXV
 
     def ap(b):
-        if len(b) > 3:
-            return T[b[0]][:, b[1]:b[2]:b[3]]
-        return T[b[0]][:, b[1]:b[2]]
+        nm, lo, hi, step, rows = (b + (1, 128)[len(b) - 3:])[:5]
+        if nm in ("HW", "HV"):
+            return T[nm][:, lo // 4:hi // 4:max(step // 4, 1), :]
+        p, q = rows if isap(rows) else (0, rows)
+        return T[nm][p:q, lo:hi:step]
 
     def isap(x):
         return isinstance(x, tuple)
@@ -333,22 +370,19 @@ def calls(g, rank, T, topo):
     def fill(out, x):
         return emit("v", lambda: g.vector.memset(ap(out), x), [], [out], cost=cost(out, []))
 
-    def scan(out, d0, d1, op1):
-        return emit("v", lambda: g.vector.tensor_tensor_scan(ap(out), ap(d0), ap(d1), 0.0, Op.mult, op1), [d0, d1], [out],
+    def scan(out, d0, d1, op1, op0=Op.mult):
+        return emit("v", lambda: g.vector.tensor_tensor_scan(ap(out), ap(d0), ap(d1), 0.0, op0, op1), [d0, d1], [out],
                     cost=cost(out, [d0, d1]))
 
-    def act(out, a, fn, bias=0.0, scale=1.0, accum=None, more=0.0):
+    def act(out, a, fn, bias=0.0, scale=1.0, more=0.0, behind=()):
         rd = [a] + [s for s in (bias, scale) if isap(s)]
         kw = {}
         if isap(bias) or bias != 0.0:
             kw["bias"] = ap(bias) if isap(bias) else bias
         if isap(scale) or scale != 1.0:
             kw["scale"] = ap(scale) if isap(scale) else scale
-        wr = [out]
-        if accum is not None:
-            kw["accum_out"] = ap(accum)
-            wr = [out, accum]
-        return emit("a", lambda: g.scalar.activation(ap(out), ap(a), fn, **kw), rd, wr, cost=wide(out) * CYC + 0.05 + more)
+        return emit("a", lambda: g.scalar.activation(ap(out), ap(a), fn, **kw), rd, [out],
+                    cost=max(64, wide(out)) * CYC + FIXA + more, behind=behind)
 
     def mm(seq):
         def go():
@@ -357,40 +391,41 @@ def calls(g, rank, T, topo):
                 ins = g.tensor.matmul(ap(o), ap(l), ap(r), st, sp)
             return ins
         reads = sorted(set(x[1][:3] for x in seq) | set(x[2][:3] for x in seq))
-        return emit("p", go, reads, [seq[0][0]], cost=sum(max(64, wide(x[0])) for x in seq) * PEC + 0.03)
+        reads += [y[:3] + (1, (32, 33)) for x in seq for y in x[1:3] if len(y) == 5 and y[4] == 33]
+        return emit("p", go, reads, [seq[0][0]], cost=sum(max(min(64, wide(x[1])), wide(x[0])) for x in seq) * PEC + 0.03)
 
     def LJ(j):
         return ("LB", 128 * j, 128 * j + 128)
 
-    def M(nm):
-        return (nm, 0, 128)
+    def M(nm, rows=128):
+        return (nm, 0, 128, 1, rows)
 
-    def word(nm, out, src, base, strided=True, start=True, stop=True, js=range(16)):
-        seq = []
-        for j in js:
-            r = (src, base + j, base + CH, 16) if strided else (src, base + NJ * j, base + NJ * (j + 1))
-            seq.append((out, (nm, 15 - j, 143 - j), r, start and j == js[0], stop and j == js[-1]))
-        return mm(seq)
+    def units(nm, i, n=1):
+        return (nm, NU * i, NU * (i + n))
 
     goes, came = goes_order(rank, cores, topo), came_order(rank, cores, topo)
-    own = NB * came.index(rank)
     loads = []
 
     def load(b, src, sem, t, after=()):
         loads.append(emit("s", lambda: g.sync.dma_start(ap(b), src), [], [b], sem, t, None, after, loads[-1:]))
         return loads[-1]
 
+    def hbm(t, x, n):
+        return t[:, NB * x[0] + NU * x[1]:NB * x[0] + NU * (x[1] + n)]
+
     emit("a", lambda: g.scalar.dma_start(ap(("wS", 0, 2)), T.wt[:]), [], [("wS", 0, 2)], "dw", 1.0)
-    for p in range(4):
-        load(("qN", NB * p, NB * p + NB), T.qs[:, NB * goes[p]:NB * goes[p] + NB], "dq%d" % p, 1.4 + 0.4 * p)
+    for i, n in runs(goes, 4):
+        load(units("qN", i, n), hbm(T.qs, goes[i], n), "dq%d" % i, 1.4 + 0.15 * (i + n))
     tab = [load(("mkT", x, x + W // 2), T.mk[:, x:x + W // 2], "dm%d" % (2 * x // W), TMK) for x in (0, W // 2)]
-    load(("qO", own, own + NB), T.qs[:, NB * rank:NB * rank + NB], "dq4", TMK + 0.5)
+    for u, i, j, n in pieces(0, rank, rank, cores, topo):
+        load(units("qO", j, n), hbm(T.qs, (rank, u), n), "do%d" % u, TMK + 0.5)
 
     def C(i):
         return ("col", i, i + 1)
-    KC, K15, KA, KLT, NBI, B1, QB, RB, WS, R8, W2, WN, KP1, RCOL, KK, Y64 = [C(i) for i in range(16)]
-    T2, T3, T4, T5, M15 = [C(24 + i) for i in range(5)]
-    RC0, W1, WH = ("E16", 12, 13), ("geo", 10, 11), ("geo", 14, 15)
+    KC, KA, KLT, KGE, KP1, RCOL, KK, G4, G8, GE, GS, OFS, OF32, N32, P97 = [C(i) for i in range(15)]
+    T1, T2, T3, T4, T5, M15, T6, T7 = [C(16 + i) for i in range(8)]
+    RC0 = ("E16", 12, 13)
+    made = []
 
     def iota(out, pattern, base, cm, flag=True, behind=()):
         c = 0.13 + 2 * wide(out) * CYC
@@ -398,364 +433,347 @@ def calls(g, rank, T, topo):
         made.append(emit("g", lambda: g.iota(ap(out), pattern, base, cm, **kw), [], [out], cost=c, behind=behind))
         return made[-1]
 
-    made = []
-
-    def least(out, a, op):
-        return emit("v", lambda: g.vector.tensor_reduce(ap(out), ap(a), AxisListType.X, op), [a], [out],
-                    cost=max(64, wide(a)) * CYC + 0.03)
-
     def pick(out, a, pattern, op, x, base, cm):
         made.append(emit("g", lambda: g.affine_select(ap(out), ap(a), pattern, op, x, base, cm), [a], [out],
                          cost=0.17 + 2 * wide(out) * CYC))
 
-    def weights(nm, col):
-        ts((nm, 0, 144), ("XP", 0, 144), K15, Op.is_equal, col, Op.mult)
-
     def diag(nm, x):
         ts(M(nm), M("XP"), 0.0, Op.is_equal, x, Op.mult)
 
+    def zero(out):
+        iota(out, [[0, wide(out)]], 0, 0)
+
+    def PM(b):
+        return ("PM", 128 * b, 128 * b + 128)
+
     def consts_search():
-        first = iota(("J16", 0, 16), [[1, 16]], 0, 0)
-        act(("geo", 16, 32), ("J16", 0, 16), Fn.Exp, bias=50 * LN2, scale=-10 * LN2, more=1.3)
-        iota(("pi", 0, 1), [[0, 1]], 0, 1, False, [first])
-        iota(("XP", 0, 144), [[1, 144]], 0, -1)
-        iota(("JR", 0, 96), [[0, 6], [1, 16]], 0, 0)
-        fill(M("ONE"), 1.0)
-        for j in range(16):
-            pick(LJ(j), M("ONE"), [[-16, 8], [0, 16]], Op.is_equal, 0.0, -j, 1)
-        ki = ("ki", 0, 1)
+        first = iota(("pi", 0, 1), [[0, 1]], 0, 1, False)
+        iota(M("XP"), [[1, 128]], 0, -1, True, [first])
+        iota(("IO", 0, 36), [[1, 36]], 0, 0)
+        fill(("ONE", 0, 128), 1.0)
+        ki, kg = ("ki", 0, 1), ("ki", 1, 2)
         ts(ki, ("pi", 0, 1), 15, Op.bitwise_and)
+        ts(kg, ("pi", 0, 1), 4, Op.arith_shift_right)
         cp(KC, ki)
-        ts(K15, ki, -1.0, Op.mult, 15.0, Op.add)
-        ts(NBI, ki, -256.0, Op.mult)
-        ts(("E16", 0, 16), ("J16", 0, 16), KC, Op.is_equal)
-        ts(("Z64", 0, 144), ("XP", 0, 144), K15, Op.is_equal, 64.0, Op.mult)
-        for k, nm in enumerate(("ZX", "ZY")):
-            ts((nm, 0, 144), ("Z64", 0, 144), ("wS", k, k + 1), Op.mult)
-        for c in range(2):
-            for k, x in ((145, 0), (146, 1), (1, -32)):
-                fill(("X", 296 * c + k, 296 * c + k + 143, 3), x)
-            fill(("h%d" % c, NJ, NJ + 1), 0.0)
-        weights("ZL", RC0)
+        fill(("MG", 0, 96), 1.5 * 2.0 ** 35)
+        x = act(M("half"), M("ONE"), Fn.Exp, scale=-LN2, more=1.3)
+        act(T1, KC, Fn.Exp, bias=-57 * LN2, scale=10 * LN2, behind=[x])
+        act(T6, KC, Fn.Exp, bias=50 * LN2, scale=-10 * LN2, behind=[x])
         ts(KLT, ki, 11.5, Op.is_lt)
-        tt(("geo", 32, 44), ("geo", 16, 28), ("E16", 0, 12), Op.mult)
-        least(WS, ("geo", 32, 44), Op.add)
-        weights("ZS", WS)
-        fill(("geo", 0, 4), 16.0)
-        scan(("geo", 8, 11), ("geo", 0, 3), ("E16", 12, 15), Op.add)
-        scan(("geo", 13, 15), ("geo", 0, 2), ("E16", 14, 16), Op.add)
-        act(W2, ("geo", 9, 10), Fn.Copy, scale=16.0)
-        act(WN, ("E16", 13, 14), Fn.Copy, scale=256.0)
-        weights("ZH", WN)
-        weights("ZN", WH)
-        weights("Z1", W1)
-        weights("Z2", W2)
-        for nm, x in (("ID", 1.0), ("NI", -1.0), ("I16", 16.0), ("N16", -16.0), ("ISY", KLT)):
+        ts(G4, kg, 4.0, Op.mult, 3.0, Op.add)
+        ts(("MK", 0, 36), ("IO", 0, 36), G4, Op.is_equal)
+        for nm, x in (("ID", 1.0), ("ISY", KLT), ("NI", -1.0), ("I97", 3104.0)):
             diag(nm, x)
-        act(B1, KC, Fn.Copy, bias=-1760.0, scale=-2048.0)
-        act(QB, KC, Fn.Copy, bias=220.0, scale=256.0)
-        act(R8, KC, Fn.Copy, bias=2048.0, scale=2048.0)
-        ts(("LT", 0, 96), ("JR", 0, 96), KC, Op.is_gt, KLT, Op.mult)
-        for c in range(2):
-            fill(("HT", 384 * c, 384 * c + 384, 2), 0.0)
-            fill(("XB", 480 * c + 1, 480 * c + 96, 2), 0)
-        fill(("mkE", W, MKW), 0.0)
+        pick(("WS", 8, 40), ("ONE", 0, 32), [[-1, 4], [-16, 8]], Op.is_equal, 0.0, -12, 1)
+        pick(("M12", 0, 36), ("ONE", 0, 36), [[-16, 9], [1000, 4]], Op.is_equal, 0.0, -3012, 1)
+        for b in range(3):
+            pick(PM(b), M("ONE"), [[-16, 8], [1000, 4], [-1, 4]], Op.is_equal, 0.0, -3000 - 4 * b, 1)
+        ts(("MKG", 0, 36), ("MK", 0, 36), T1, Op.mult, -1.0, Op.mult)
+        mm([(("SQ", 128 * b, 128 * b + 128, 1, 32), ("MKG", x, x + 32), y, y[0] == "ISY", y[0] == "PM")
+            for b in range(3) for x, y in ((3 - b, M("ISY")), (0, PM(b)))])
+        act(("SPM", 0, 384, 1, 32), ("SQ", 0, 384, 1, 32), Fn.Copy)
+        fill(("SPM", 0, 384, 1, (32, 33)), MAGIC)
+        fill(("ET", 0, 768, 1, (32, 33)), 1.0)
+        for k, (x, scale) in enumerate(((0, 1.0), (1, 32.0), (1, 1.0))):
+            ts(("W0", k, 105, 3), ("MK", 0, 35), ("wS", x, x + 1), Op.mult, scale, Op.mult)
+        mm([(("SP", 96 * b, 96 * b + 96), y, ("W0", x, x + 96), y[0] == "ISY", y[0] == "PM")
+            for b in range(3) for x, y in ((9 - 3 * b, M("ISY")), (0, PM(b)))])
+        act(("W1", 0, 288), ("SP", 0, 288), Fn.Copy, scale=-1.0)
+        ts(("W2", 0, 288), ("W1", 0, 288), -1.0, Op.mult)
+        iota(("OF", 0, 96, 1, 2), [[0, 96]], 4096, -4097)
+        iota(("OF", 1, 96, 3, 2), [[0, 32]], -393216, 393184)
+        fill(("MG", 1, 96, 3), 1.5 * 2.0 ** 40)
+        fill(("D0", 0, 288), 0.0)
+        fill(("HW", 0, 524), 0.0)
+        ts(("WS", 0, 8), ("MK", 3, 35, 4), T6, Op.mult, KLT, Op.mult)
+        iota(M("T2K", 2), [[0, 128]], 2048, 0)
+        iota(M("CST", 2), [[32, 4], [0, 32]], -236, 0)
+        fill(("MS", 1, 984, 2), 0.0)
+        fill(("MS", 0, 984, 2), 1.0)
+        for c in range(NC):
+            fill(("B%d" % c, 352, 512, 5), NONE)
+        zero(M("ZM"))
+        pick(M("I8K"), M("ZM"), [[-1, 128]], Op.not_equal, 8192.0, 0, 1)
 
     def consts_edits():
-        iota(M("SRC"), [[0, 8], [1, 4], [1, 4]], 13, 0)
+        iota(("JR", 0, 96), [[0, 6], [1, 16]], 0, 0)
+        ts(("LT", 0, 96), ("JR", 0, 96), KC, Op.is_gt, KLT, Op.mult)
+        zero(("mkE", W, MKW))
+        for j in range(4):
+            pick(LJ(j), M("ONE"), [[-16, 8], [0, 16]], Op.is_equal, 0.0, -j, 1)
         iota(("IT", 0, 192), [[0, 2], [1, 96]], 0, 0)
         iota(("w1", 0, 12), [[0, 2], [16, 6]], W, 0)
-        act(KA, KC, Fn.Copy, bias=-7.5)
-        act(M("AB"), M("XP"), Fn.Abs, bias=KA)
-        ts(M("JP"), M("XP"), KC, Op.add)
-        ts(M("BD"), M("AB"), 8.0, Op.is_lt)
-        ts(M("CAQ"), M("SRC"), KC, Op.is_equal)
-        tt(M("CA"), M("CAQ"), M("BD"), Op.mult)
-        ts(("ci", 0, 1), ("ki", 0, 1), 3, Op.bitwise_and)
-        ts(T2, KC, 11.5, Op.is_gt, 500.0, Op.mult)
-        ts(T3, ("ci", 0, 1), 12.0, Op.add)
-        tt(RCOL, T2, T3, Op.add)
-        ts(M("RS"), M("JP"), RCOL, Op.is_equal)
+        pick(M("CA"), M("ONE"), [[-16, 8], [-1, 4], [-1, 4]], Op.is_equal, 0.0, -13, 1)
+        pick(M("CA"), M("CA"), [[0, 8], [-1, 4], [-1, 4]], Op.is_ge, 0.0, 2, 0)
         ts(("ci", 1, 2), ("ki", 0, 1), 2, Op.arith_shift_right)
-        ts(KK, ("ci", 1, 2), -1.0, Op.mult, 3.0, Op.add)
-        ts(T4, KC, 11.5, Op.is_lt, 500.0, Op.mult)
-        ts(T5, KC, 1.0, Op.add)
-        tt(KP1, T4, T5, Op.add)
-        ts(M15, KC, 14.5, Op.is_lt)
-        ts(M("DN"), M("JP"), KP1, Op.is_equal, M15, Op.mult)
-        diag("R12", RC0)
-        diag("I256", 1.0 / 256)
-        ts(("WD", 1, 24, 2), ("w1", 0, 12), KC, Op.add)
+        ts(KK, ("ci", 1, 2), -16.0, Op.mult, -80.0, Op.add)
+        pick(M("I13"), M("ZM"), [[-1, 128]], Op.not_equal, 2.0 ** -13, 0, 1)
+        fill(("hf2", 0, 32), 0.5)
+        fill(("hf2", 32, 64), 136 / 4096)
+        fill(("HV", 0, 908), 0.0)
+        pick(M("DN"), M("ONE"), [[-16, 8], [-1, 16]], Op.is_equal, 0.0, 1, 1)
+        pick(M("DN"), M("DN"), [[0, 8], [1, 16]], Op.is_ge, 0.0, -13, 0)
+        pick(M("R12"), M("ONE"), [[-16, 8], [1000, 16]], Op.is_equal, 0.0, -12012, 1)
+        pick(M("I256"), M("ZM"), [[-1, 128]], Op.not_equal, 1.0 / 256, 0, 1)
+        pick(M("N8K"), M("ZM"), [[-1, 128]], Op.not_equal, -8192.0, 0, 1)
+        act(("WD", 1, 24, 2), ("w1", 0, 12), Fn.Identity, bias=KC)
+        act(("w2", 0, 12), ("WD", 1, 24, 2), Fn.Copy, bias=-2048.0)
         act(("TO", 0, 12), ("WD", 1, 24, 2), Fn.Copy, bias=-W / 256, scale=1.0 / 256)
-        fill(("HM", 0, 40), 0.0)
-        fill(("NEW", 0, NB), 0.0)
-        fill(("NEW", 0, NB, 96), 16384.0)
+        zero(("HM", 0, 40))
+        zero(("NM", 0, 160, 5))
+        zero(("NEW", 0, NB))
+        iota(("NEW", 0, NB, 96), [[0, 4]], 16384, 0)
 
     def sm(nm, c, k=0, n=1):
-        lo = c * NJ * n + k * NJ
-        return (nm, lo, lo + NJ)
-
-    def pair(nm, c, k=0, n=1):
-        lo = 2 * (c * NJ * n + k * NJ)
-        return (nm, lo, lo + 2 * NJ)
-
-    def even(b):
-        return (b[0], b[1], b[2], 2)
-
-    def odd(b):
-        return (b[0], b[1] + 1, b[2], 2)
-
-    def half(nm, c, h):
-        lo = c * CH + h * NB
-        return (nm, lo, lo + NB)
+        lo = (c * n + k) * NT
+        return (nm, lo, lo + NT)
 
     def chunk(nm, c):
         return (nm, c * CH, c * CH + CH)
 
-    def gb(c, h):
-        return ("g%d%d" % (c, h), 0, NB)
+    def half(nm, c, h):
+        lo = c * CH + h * CH // 2
+        return (nm, lo, lo + CH // 2)
 
-    def mo(r, c, s):
-        return sm("mo", 2 * r + c, s - 1, 4)
+    def block(nm, c, b):
+        return (nm, c * CH + b, c * CH + CH, 4)
 
-    def first_length(r, c, src):
-        k = ("k%d" % c, 2 * NJ, 3 * NJ)
-        word("ZL", k, src, c * CH)
-        act(mo(r, c, 1), k, Fn.Copy, bias=MO)
+    def chosen(c, s, k):
+        lo = 64 * ((3 * c + s - 1) * 3 + k - 1)
+        return ("sl", lo, lo + 64)
 
-    def first_rope(c, src):
-        for k, nm in enumerate(("ZH", "ZN")):
-            word(nm, ("k%d" % c, (3 + k) * NJ, (4 + k) * NJ), src, c * CH)
-        act(pair("rope", c), ("k%d" % c, 3 * NJ, 5 * NJ), Fn.Copy)
+    def rope(r, c, s, k):
+        if s == 1:
+            return sm("f0", 3 * r + c, k, 4)
+        b = chosen(c, s - 1, k + 1)
+        return (b[0], b[1] + 1, b[2], 2)
 
-    def jmajor(c, src):
-        for h in range(2):
-            bk = gb(c, h)
-            mm([((bk[0], x * NJ, x * NJ + NJ), M("ID"), (src, c * CH + 8 * h + x, c * CH + CH, 16), True, True) for x in range(8)])
-            if WAYS[h] != "va":
-                act(half("qj", c, h), bk, Fn.Copy)
-            else:
-                act(half("qv", c, h), bk, Fn.Identity, bias=QB, scale=0.125)
+    def put(k, nm="HW"):
+        return (nm, 128 * k + 12, 128 * k + 128, 16)
 
-    def from_length(r, c, s):
-        m = mo(r, c, s)
-        act(sm("m97", c, s % 2, 2), m, Fn.Copy, bias=-3104.0 * MO, scale=3104.0)
-        act(sm("Cw", c, s % 2, 2), m, Fn.Exp, bias=math.log(1.5) + (83 + 10 * MO) * LN2, scale=-10 * LN2)
-        act(sm("dead", c, s % 2, 2), m, Fn.Relu, bias=2.0 ** 80 * (MO + 0.5), scale=-2.0 ** 80)
-        act(sm("mt", c, s % 2, 2), m, Fn.Copy, bias=8192.0 * (2 - MO) + 131072.0 * s, scale=8192.0)
+    def turn(terms, more=(), early=False):
+        seq = [(out, (w[0], w[1] - 4 * e, w[1] + 128 - 4 * e), (x, e, 4 * wide(out), 4)) for out, w, x in terms for e in range(4)]
+        seq += list(more)
+        seq = [x + (i == 0, i == len(seq) - 1) for i, x in enumerate(seq)]
+        if early:
+            mm(seq[:4])
+        return mm(seq[4 * early:])
 
-    def mask(r, c, s):
-        m = odd(pair("Rb", c))
-        mins[r, c, s] = []
-        for h in range(2):
-            bk = gb(c, h)
-            if WAYS[h] == "aa":
-                mm([((bk[0], x * NJ, x * NJ + NJ), LJ(8 * h + x), m, x == 0, x == 7) for x in range(8)])
-            else:
-                mm([((bk[0], x * NJ, x * NJ + NJ), LJ(8 * h + x), m, True, True) for x in range(8)])
-        for h in range(2):
-            bk, z = gb(c, h), half("zz", c, h)
-            if WAYS[h] == "av":
-                act(bk, bk, Fn.Relu, bias=B1, scale=8.0)
-                mins[r, c, s].append(tt(z, half("qj", c, h), bk, Op.min))
-            elif WAYS[h] == "va":
-                mins[r, c, s].append(tt(half("zp", c, h), half("qv", c, h), bk, Op.min))
-                act(z, half("zp", c, h), Fn.Relu, bias=B1, scale=8.0)
-            elif WAYS[h] == "aa":
-                act(bk, bk, Fn.Relu, bias=R8, scale=-8.0)
-                mm([(bk, M("NI"), half("qj", c, h), False, True)])
-                act(z, bk, Fn.Relu, scale=-1.0)
-            else:
-                act(half("rr", c, h), bk, Fn.Relu, bias=R8, scale=-8.0)
-                mm([(bk, M("ID"), half("qj", c, h), True, False), (bk, M("NI"), half("rr", c, h), False, True)])
-                act(z, bk, Fn.Relu)
+    def first_rope(r, c, src, bank):
+        o = (bank, 0, 128)
+        mm([((bank, b, 128, 4), block(src, c, b), ("WS", 8, 40), b == 0, b == 3) for b in range(4)])
+        act(("f0", 128 * (3 * r + c), 128 * (3 * r + c) + 128), o, Fn.Copy)
 
-    def sums(c, strided):
-        hb = "h%d" % c
-        u1, u2 = (hb, 0, NJ), (hb, NJ + 1, 2 * NJ + 1)
-        if strided:
-            word("ZX", u1, "zz", c * CH)
-            word("ZY", u2, "zz", c * CH)
-            return
-        for h in range(2):
-            js = range(8 * h, 8 * h + 8)
-            word("ZX", u1, "zz", c * CH, False, h == 0, False, js)
-            word("ZY", u2, "zz", c * CH, False, False, h == 1, js)
+    def power(r, c, s, bank):
+        o, e = (bank, 128 + 128 * c, 256 + 128 * c, 1, 32), 2 * c + (r if s == 1 else 0)
+        if (r, s) == (0, 1):
+            mm([(o, ("M12", 3 - b, 35 - b), block("qN", c, b), b == 0, b == 3) for b in range(4)])
+        else:
+            mm([(o, rope(r, c, s, 0), M("ID"), True, True)])
+        act(("ET", 128 * e, 128 * e + 128, 1, 32), o, Fn.Exp, bias=math.log(1.5) + 65 * LN2, scale=-10 * LN2)
 
-    def place_of(c, s):
-        hb, o, u, x = "h%d" % c, c * 3 * NJ, c * 152, c * 296
-        cp(("U", u, u + 2 * NJ + 1), (hb, 0, 2 * NJ + 1))
-        tt(("U", u + 100, u + 100 + NJ), (hb, NJ + 1, 2 * NJ + 1), sm("m97", c, s % 2, 2), Op.add)
-        ts(("X", x, x + 291, 3), ("U", u, u + 2 * NJ + 1), 6, Op.arith_shift_right, 4095, Op.bitwise_and)
-        ts(("X", x + 2, x + 144, 3), ("U", u + 100, u + 100 + NJ), 131071, Op.bitwise_and)
-        scan(("UA", o, o + 3 * NJ), ("X", x + 145, x + 289), ("X", x, x + 144), Op.add)
-        ts(sm("H", c), ("UA", o + 2, o + 3 * NJ, 3), 5, Op.arith_shift_right, 4095, Op.bitwise_and)
-        cp(sm("OFF", c), sm("H", c))
+    def mask(r, c, s, src, late=None):
+        z, e = own("Z", r, c), 2 * c + (r if s == 1 else 0)
+        if s == 1:
+            pack(z, c, src, True, False)
+        else:
+            mm([((z, 0, 384), M("ID"), packed("qK", c), True, False)])
+        mm([((z, 128 * b, 128 * b + 128), ("SPM", 128 * b, 128 * b + 128, 1, 33), ("ET", 128 * e, 128 * e + 128, 1, 33), False,
+             b == 2 and late is None) for b in range(3)])
+        if late:
+            pack(z, c, late, False, True)
+        act(packed("zz", c), (z, 0, 384), Fn.Relu, bias=-MAGIC)
+
+    def packed(nm, c):
+        return (nm, 384 * c, 384 * c + 384)
+
+    def pack(bank, c, src, start, stop):
+        mm([((bank, 128 * b, 128 * b + 128), y, block(src, c, x), start and b == 0 and x == 0, stop and b == 2 and x == 3)
+            for b in range(3) for x, y in ((b, M("ISY")), (3, PM(b)))])
+
+    def keep(c, src, bank):
+        pack(bank, c, src, True, True)
+        act(packed("qK", c), (bank, 0, 384), Fn.Copy)
+
+    def own(nm, r, c):
+        return "%s%d" % (nm, (c + r) % NC)
+
+    def step(r, c, s, q0):
+        bk = own("B", r, c)
+        mu = rope(r, c, s, 0)
+        o, o1 = (bk, 256, 352), (bk, 257, 352, 3)
+
+        def zb(b):
+            return ("zz", 384 * c + 128 * b, 384 * c + 128 * b + 128)
+        cw, cx = sm("Cw", c, s % 2, 2), sm("Cx", c, s % 2, 2)
+        act(cw, mu, Fn.Exp, bias=math.log(1.5) + 83 * LN2, scale=-10 * LN2)
+        act(cx, mu, Fn.Exp, bias=math.log(1.5) + 83 * LN2 - 6.5 * TILT, scale=-10 * LN2 + TILT)
+        mm([(o, M("half", 2), ("OF", 0, 96, 1, 2), True, False)])
+        mm([(o, zb(b), ("W1", 96 * b, 96 * b + 96), False, False) for b in range(3)]
+           + [(o, M("ID"), ("MG", 0, 96), False, False), (o, M("NI"), ("MG", 0, 96), False, False), (o1, M("I97"), mu, False, False)]
+           + [(o, zb(b), ("W2", 96 * b, 96 * b + 96), False, b == 2) for b in range(3)])
+        act(("D0", 96 * c + 1, 96 * c + 96, 3), (bk, 258, 352, 3), Fn.Copy)
+        scan(("X", 96 * c, 96 * c + 96), ("D0", 96 * c, 96 * c + 96), o, Op.add)
+        ts(sm("H", c), ("X", 96 * c + 1, 96 * c + 96, 3), 5, Op.arith_shift_right, 4095, Op.bitwise_and)
+        ts(put(c), sm("H", c), -2048.0, Op.add)
+        turn([((bk, 256, 288), put(c), "ID")])
+        ts(sm("OFF", c), (bk, 256, 288), 2048.0, Op.add)
+        code = (bk, 352 + s, 512, 5)
+        mm([(code, M("I8K"), mu, True, False), (code, M("T2K", 2), ("CST", 32 * s - 32, 32 * s, 1, 2), False, False),
+            (code, M("ID"), put(c), False, True), ((bk, 0, 64, 2), M("ID"), cw, True, False)]
+           + [((bk, 64 * k + x, 64 * k + 64, 2), M(y), rope(r, c, s, k), False, False)
+              for k in range(1, 5 - s) for x, y in enumerate(("NI", "ID"))])
+        for x in range(0, 32, GW):
+            gathered(("nn", c * CH + 16 * x, c * CH + 16 * (x + GW)), ("OFF", 32 * c + x, 32 * c + x + GW),
+                     (q0, c * CH + 16 * x, c * CH + 16 * (x + GW)), Op.subtract, TABLE[r])
+        n = 5 - s
+        mm([((bk, 2 * b, 64 * n, 8), block("nn", c, b), ("WS", 0, 8 * n), False, b == 3) for b in range(4)])
+        lo = 328 * c + 8
+        flag = ("MS", lo + 2 * s, lo + 320, 10) if s < 4 else ("MB", 160 * c + 4, 160 * c + 160, 5)
+        tt(flag, (bk, 0, 64, 2), cx, Op.is_equal if s < 4 else Op.not_equal)
+        for k in range(1, 5 - s):
+            scan(chosen(c, s, k), ("MS", lo + 2 * s - 5, lo + 2 * s + 311, 5), (bk, 64 * k, 64 * k + 64), Op.add)
+        if s == 3:
+            act(("MB", 160 * c, 160 * c + 160), ("MS", lo, lo + 320, 2), Fn.Copy, bias=1.0, scale=-1.0)
+        if (r, c) == (0, 0):
+            act(sm("dead", s % 2), mu, Fn.Relu, bias=1.0, scale=-1.0)
+            tt(("NM", s, 160, 5), sm("dead", s % 2), flag, Op.max if s < 4 else Op.is_ge)
 
     def win(off, w=W):
         return T.mkE[:, 0:w].indirect(ap(off))
 
-    def gathered(o, off, q, op, nm, w=W, behind=()):
+    def gathered(o, off, q, op, nm, w=W):
         return emit("v", lambda: g.vector.tensor_tensor(ap(o), T[nm][:, 0:w].indirect(ap(off)), ap(q), op), [(nm, 0, w), off, q],
-                    [o], cost=0.05 + GAT * CYC * wide(o), behind=behind)
+                    [o], cost=0.05 + GAT * CYC * wide(o))
 
     def picked(o, off, nm, w=W):
         return emit("a", lambda: g.scalar.activation(ap(o), T[nm][:, 0:w].indirect(ap(off)), Fn.Copy), [(nm, 0, w), off], [o],
                     cost=0.065 + GAT * CYC * wide(o))
 
-    mins = {}
-
-    def step(r, c, s, q0):
-        hb, kb = "h%d" % c, ("k%d" % c, 0, 2 * NJ)
-        S, hit, m = (hb, 100, 100 + NJ), pair("HT", c, s - 1, 4), mo(r, c, s)
-        Rb = odd(pair("Rb", c))
-        place_of(c, s)
-        mm([(S, M("ID"), sm("Cw", c, s % 2, 2), True, False), (S, M("ID"), sm("dead", c, s % 2, 2), False, False)])
-        if s == 1:
-            hi, lo = sm("rope", c, 0, 2), sm("rope", c, 1, 2)
-            mm([(odd(kb), M("ID"), hi, True, False), (odd(kb), M("ID"), lo, False, True),
-                (even(kb), M("NI"), hi, True, False), (even(kb), M("NI"), lo, False, False)])
-        if s == 2:
-            mm([(odd(kb), M("I16"), sm("rest", c), True, True), (even(kb), M("N16"), sm("rest", c), True, False)])
-        if s == 3:
-            act(sm("m256", c), m, Fn.Copy, bias=-256.0 * MO, scale=256.0)
-            mm([(odd(kb), M("I16"), Rb, True, False), (odd(kb), M("N16"), sm("m256", c), False, True),
-                (even(kb), M("N16"), Rb, True, False), (even(kb), M("I16"), sm("m256", c), False, False)])
-        tt(even(pair("XB", c, s - 1, 5)), sm("H", c), sm("mt", c, s % 2, 2), Op.add)
-        other = mins.get((r, 1 - c, s + c), []) if APART else []
-        if SPLIT:
-            for h in range(2):
-                p = 2 * c + h
-                gathered(half("nn", c, h), ("OFF", 24 * p, 24 * p + 24), half(q0, c, h), Op.subtract, TABLE[r], behind=other)
-        else:
-            gathered(chunk("nn", c), sm("OFF", c), chunk(q0, c), Op.subtract, TABLE[r], behind=other)
-        word("ZS", S, "nn", c * CH, start=False)
-        if s < 4:
-            word("Z1" if s == 1 else "Z2", even(kb), "nn", c * CH, start=False)
-        tt(odd(hit), S, sm("Cw", c, s % 2, 2), Op.is_equal)
-        if s < 4:
-            scan(pair("Rb", c), hit, kb, Op.add)
-            act(mo(r, c, s + 1), Rb, Fn.Copy, bias=MO - 0.42, scale=1.0 / 256)
-        if s == 1:
-            scan(pair("Rf", c), hit, kb, Op.add)
-            act(sm("m256", c), mo(r, c, 2), Fn.Copy, bias=-256.0 * MO, scale=256.0)
-            tt(sm("rest", c), odd(pair("Rf", c)), sm("m256", c), Op.subtract)
-        scan(pair("XB", c, s, 5), hit, pair("XB", c, s - 1, 5), Op.max)
-
     def later_steps(r, q0):
-        for k in range(1, 8):
-            c, s = k % 2, k // 2 + 1
-            if k < 7:
-                mask(r, 1 - c, (k + 1) // 2 + 1)
-            if s > 1:
-                from_length(r, c, s)
-                sums(c, False)
-            step(r, c, s, q0)
+        for s in range(1, 5):
+            for c in range(NC):
+                if (r, s) == (1, 2):
+                    keep(c, q0, "SP")
+                if s > 1:
+                    power(r, c, s, "SP")
+                    mask(r, c, s, q0)
+                step(r, c, s, q0)
 
-    def learn(r, c, q0, dest, after):
-        B = odd(pair("XB", c, 4, 5))
-        ts(sm("Hb", c), B, 4095, Op.bitwise_and)
-        ts(sm("OL", c), B, 1.0 / 8192, Op.mult)
-        cp(sm("OB", c), sm("Hb", c))
+    def rounded(out, a, k):
+        ts(out, a, 1.5 * 2.0 ** (23 + k), Op.add, 1.5 * 2.0 ** (23 + k), Op.subtract)
+
+    def parts(code, k):
+        rounded(put(k, "HV"), code, 13)
+        tt(put(k), code, put(k, "HV"), Op.subtract)
+
+    def learn(r, c, q0, dests, after):
+        bk = own("B", r, c)
+        scan(("BT", 160 * c, 160 * c + 160), ("MB", 160 * c, 160 * c + 160), (bk, 352, 512), Op.min)
+        parts(("BT", 160 * c + 4, 160 * c + 160, 5), c)
+        turn([((bk, 288, 320), put(c, "HV"), "I13"), ((bk, 256, 288), put(c), "ID")],
+             [((bk, 256, 320), M("T2K", 2), ("hf2", 0, 64, 1, 2))], True)
+        cp(("OB", 64 * c, 64 * c + 64), (bk, 256, 320))
+        if r:
+            act(sm("none", c), (bk, 288, 320), Fn.Relu, bias=1.0, scale=-1.0)
+            turn([((bk, 288, 320), put(c), "ID")], [((bk, 288, 320), M("NI"), sm("none", c)),
+                                                    ((bk, 288, 320), M("T2K", 2), ("hf2", 0, 32, 1, 2))])
+            for j, w in runs(came, 4):
+                if j // 4 == c:
+                    x, y = 24 * came[j][0] + 8 * came[j][1], 288 + 8 * (j % 4)
+                    act(("yS", x, x + 8 * w), (bk, y, y + 8 * w), Fn.Copy)
+            if 2 * c + 1 not in ADD_V:
+                mm([((bk, 0, 256), M("ID"), half("qO", c, 1), True, False), ((bk, 0, 256), M("ID"), half("dR", c, 1), False, False)])
         for h in range(2):
             p = 2 * c + h
-            ob, ol, d = ("OB", 24 * p, 24 * p + 24), ("OL", 24 * p, 24 * p + 24), half("dd", c, h)
+            x = 64 * c + 16 * h
+            ob, d = ("OB", x, x + 16), half("dd", c, h)
             if p not in BY_SCALAR[r]:
                 gathered(d, ob, half(q0, c, h), Op.subtract, TABLE[r])
-                after(p, gathered(dest(p), ol, d, Op.mult, "LT", 96))
+                for i, n, to in dests(p):
+                    y = 64 * c + 32 + 8 * (i % 4)
+                    after(i, n, gathered(to, ("OB", y, y + 8 * n), units("dd", i, n), Op.mult, "LT", 96))
                 continue
-            bk = (("k%d", "h%d")[h] % c, 0, NB)
-            picked(half("rr", c, h), ol, "LT", 96)
+            picked(half("rr", c, h), ("OB", x + 32, x + 48), "LT", 96)
             picked(d, ob, TABLE[r])
-            mm([(bk, M("NI"), half(q0, c, h), True, False)])
-            mm([(bk, M("ID"), d, False, True)])
-            after(p, tt(dest(p), bk, half("rr", c, h), Op.mult))
+            mm([(("SQ", 0, 256), M("NI"), half(q0, c, h), True, False)])
+            mm([(("SQ", 0, 256), M("ID"), d, False, True)])
+            for i, n, to in dests(p):
+                x = NU * (i - 2 * p)
+                after(i, n, tt(to, ("SQ", x, x + NU * n), units("rr", i, n), Op.mult))
 
     sent, come = {}, {}
 
-    def send(k, p, after=(), behind=()):
-        s = goes[p]
-        if s == rank:
-            return
-        b = (("qN", "dS")[k], NB * p, NB * p + NB)
+    def send(k, s, piece, after=(), behind=()):
+        u, i, j, n = piece
+        b = units(("qN", "dS")[k], i, n)
         rel = relay_of(core, cores[s], cores, topo)
         to = cores[s] if rel is None else rel
         m = topo.mask(core, to)
         rid, pid = topo.addr(to, core)
-        x = NB * came_order(s, cores, topo).index(rank)
         if rel is None:
-            dst, sem = T[LANDS[k]][:, x:x + NB], "arr%d%d" % (k, rank)
+            dst, sem = ap(units(LANDS[k], j, n)), "arr%d%d%d" % (k, rank, u)
         else:
-            dst, sem = T["land%d" % k][:], "rin%d" % k
-        sent[k, s] = emit("g", lambda: g.remote_dma(dst, ap(b), T.sem[sem], T.sem.sent, pid, rid, m), [b], [], None, 0.3,
-                          ("sent", count(m)), after, behind)
+            dst, sem = ap(units("land%d" % k, u, n)), "rin%d%d" % (k, u)
+        last = [x for (kk, ss, uu), x in sent.items() if ss == s]
+        sent[k, s, u] = emit("g", lambda: g.remote_dma(dst, ap(b), T.sem[sem], T.sem.sent, pid, rid, m), [b], [], None, TSEND if sent else TFIRST,
+                             ("sent", count(m)), after, list(behind) + last)
+
+    def sends(k, c=None, after=(), behind=()):
+        todo = [(x[1], s, x) for s in range(len(cores)) if s != rank for x in pieces(k, rank, s, cores, topo)]
+        for i, s, x in sorted(todo):
+            if c is None or i // 4 == c:
+                send(k, s, x, after, behind)
 
     def arrivals(k):
-        for p in range(4):
-            s = came[p]
+        for s in range(len(cores)):
             if s == rank:
                 continue
             rel = relay_of(cores[s], core, cores, topo)
             n = count(topo.mask(cores[s] if rel is None else rel, core))
-            come[k, s] = emit("x%d%d" % (k, s), None, [], [(LANDS[k], NB * p, NB * p + NB)], None,
-                              (TNEAR if rel is None else TFAR) + 4 - 4 * k, ("arr%d%d" % (k, s), n))
+            for u, i, j, w in pieces(k, s, rank, cores, topo):
+                come[k, s, u] = emit("x%d%d%d" % (k, s, u), None, [], [units(LANDS[k], j, w)], None,
+                                     (TNEAR if rel is None else TFAR) + 7 - 7 * k, ("arr%d%d%d" % (k, s, u), n))
 
-    EB = "g11"
+    EB, EK = "B0", "Z0"
 
     def edits():
-        e = goes.index(0)
-        c, h0 = e // 2, 24 * (e % 2)
-        qe, de = ("q0", NB * e, NB * e + 96), ("dd", NB * e, NB * e + 96)
-        def six(b):
-            return (b[0], b[1] + 2 * h0, b[1] + 2 * h0 + 12)
+        qe, de = ("q0", 0, 96), ("dd", 0, 96)
+        scan(("FT", 0, 160), ("NM", 0, 160), (EB, 352, 512), Op.min)
+        F, Bb = ("FT", 4, 160, 5), ("BT", 4, 160, 5)
+        act(("ed", 0, 32), Bb, Fn.Relu, bias=16.0 * (NONE + 2.0 ** 17), scale=-16.0)
+        tt(("ed", 32, 64), Bb, ("ed", 0, 32), Op.add)
+        parts(F, 3)
+        tt(put(4, "HV"), F, ("ed", 32, 64), Op.is_le)
+        rounded(put(5, "HV"), put(0, "HV"), 17)
+        rounded(("ed", 64, 96), put(3, "HV"), 17)
+        tt(put(6, "HV"), put(3, "HV"), ("ed", 64, 96), Op.subtract)
+        keys = (EB, 320, 332)
+        turn([((EB, 320 + 6 * x, 326 + 6 * x), w, y) for x in (1, 0) for w, y in ((put(3 - 3 * x), "ID"), (put(4, "HV"), "N8K"))])
+        ts(("key", 0, 12), keys, -2048.5, Op.max)
+        tt(("WD", 0, 24, 2), keys, ("w2", 0, 12), Op.subtract)
 
-        fk = [("fc", NJ * k + h0, NJ * k + h0 + 6) for k in range(3)]
-        act(("al", 0, 144), ("mo", 192 * c, 192 * c + 144), Fn.Sign, bias=-MO)
-        act(("al", 144, 150), ("mo", 192 * c + 144 + h0, 192 * c + 150 + h0), Fn.Sign, bias=-MO)
-        tt(("ms", 0, 144), ("al", 0, 144), ("HT", 384 * c + 1, 384 * c + 288, 2), Op.subtract)
-        tt(("fc", 0, 144), ("XB", 480 * c, 480 * c + 288, 2), ("ms", 0, 144), Op.mult)
-        tt(("f1", 0, 6), fk[0], fk[1], Op.max)
-        tt(("XF", 1, 12, 2), ("f1", 0, 6), fk[2], Op.max)
-        cp(("XF", 0, 12, 2), even(six(pair("XB", c, 3, 5))))
-        hit = six(pair("HT", c, 3, 4))
-        tt(("HM", 1, 12, 2), ("al", 144, 150), odd(hit), Op.subtract)
-        scan(("XG", 0, 12), ("HM", 0, 12), ("XF", 0, 12), Op.max)
-        scan(("XG", 12, 24), hit, six(pair("XB", c, 3, 5)), Op.max)
-        F, Bb, ned = ("XG", 1, 12, 2), ("XG", 13, 24, 2), ("ed", 16, 22)
-        FB = ("XG", 1, 24, 2)
-        tt(("ed", 0, 6), F, Bb, Op.is_gt)
-        ts(("ed", 8, 14), Bb, 0.0, Op.is_gt, -8192.0, Op.mult)
-        tt(ned, ("ed", 0, 6), ("ed", 8, 14), Op.mult)
-        far = ("ed", 24, 30)
-        act(far, ned, Fn.Copy, bias=16384.0, scale=3.0)
-        ts(("cl", 0, 12), FB, 4095, Op.bitwise_and)
-        ts(("kh", 0, 12), FB, 4032, Op.bitwise_and)
-        ts(("kh", 12, 24), FB, 63, Op.bitwise_and)
-        ts(("si", 0, 6), Bb, 17, Op.arith_shift_right)
-        ts(("si", 6, 12), F, 13, Op.arith_shift_right, 15, Op.bitwise_and)
-        cp(("sb", 0, 12), ("si", 0, 12))
-        cp(("khb", 16, 28), ("kh", 12, 24))
-        for o in (0, 6):
-            tt(("khb", o, o + 6), ("kh", o, o + 6), ned, Op.add)
-            tt(("key", o, o + 6), ("cl", o, o + 6), far, Op.add)
-        tt(("WD", 0, 24, 2), ("cl", 0, 12), ("WD", 1, 24, 2), Op.subtract)
-        mm([(("k0", 0, 192), M("I256"), ("IT", 0, 192), True, False)])
-        mm([(("k0", j, 192, 16), LJ(j), ("khb", 16, 28), False, False) for j in range(16)])
-        mm([(("k0", j, 192, 16), LJ(j), ("khb", 0, 12), False, j == 15) for j in range(16)])
-        mm([((EB, j, 192, 16), LJ(j), ("sb", 0, 12), True, True) for j in range(16)])
+        def flat(bank, lo, terms):
+            mm([((bank, lo + 24 * x, lo + 24 * x + 24), (w[0], w[1], w[1] + 128), (y, 0, 24), i == 0, i == len(terms) - 1)
+                for i, (x, w, y) in enumerate(terms)])
+        flat("SP", 0, [(x, w, y) for x in (1, 0) for w, y in ((put(3 - 3 * x), "ID"), (put(4, "HV"), "N8K"))])
+        cp(("khb", 0, 48), ("SP", 0, 48))
+        flat("SP", 48, [(x, put(5 + x, "HV"), "I13") for x in range(2)])
+        act(("sb", 0, 48), ("SP", 48, 96), Fn.Copy)
+        mm([((EK, 0, 192), M("I256"), ("IT", 0, 192), True, False)])
+        mm([((EK, b, 192, 4), LJ(b), ("khb", 0, 48), False, b == 3) for b in range(4)])
+        mm([((EB, b, 192, 4), LJ(b), ("sb", 0, 48), True, True) for b in range(4)])
         mm([((EB, 192, 288), M("CA"), de, True, True)])
-        act(("mf", 0, 96), (EB, 96, 192), Fn.Copy, bias=-2.0)
+        act(("mf", 0, 96), (EB, 96, 192), Fn.Copy, bias=6.0)
         ts(("mk1", 0, 96), (EB, 0, 96), KK, Op.is_equal)
         tt(("cm", 0, 96), (EB, 192, 288), ("mk1", 0, 96), Op.mult)
-        mm([((EB, 0, 96), M("ISY"), qe, True, False), ((EB, 0, 96), M("RS"), ("cm", 0, 96), False, True)])
+        mm([((EB, 0, 96), M("ISY"), qe, True, False)] + [((EB, 0, 96), PM(b), ("cm", 0, 96), False, b == 2) for b in range(3)])
         for x in range(12):
             w = x // 6
             eq = ("EQ", 96 * x, 96 * x + 96)
-            act(eq, ("k0", 96 * w, 96 * w + 96), Fn.Abs, bias=("key", x, x + 1), scale=-1.0)
+            act(eq, (EK, 96 * w, 96 * w + 96), Fn.Abs, bias=("key", x, x + 1), scale=-1.0)
             if x % 4 == 3:
-                a, o = ("EQ", 96 * x - 288, 96 * x + 96), ("MN", 96 * x - 288, 96 * x + 96)
-                emit("v", lambda a=a, o=o: g.vector.tensor_tensor_scan(ap(o), ap(("NEW", 0, NB)), ap(a), 0.0, Op.add, Op.min),
-                     [a, ("NEW", 0, NB)], [o], cost=cost(o, [a]))
+                scan(("MN", 96 * x - 288, 96 * x + 96), ("NEW", 0, NB), ("EQ", 96 * x - 288, 96 * x + 96), Op.min, Op.add)
         act(("Eb", 0, 96), (EB, 0, 96), Fn.Copy)
         tt(("HM", 17, 40, 2), ("MN", 95, 1152, 96), ("TO", 0, 12), Op.is_equal)
         scan(("WO", 0, 24), ("HM", 16, 40), ("WD", 0, 24), Op.add)
@@ -763,72 +781,70 @@ def calls(g, rank, T, topo):
         oF, oB, full_w = ("OE", 0, 6), ("OE", 6, 12), ("mkE", 0, MKW)
         emit("v", lambda: g.vector.tensor_copy(win(oF, MKW), ap(("Eb", 0, 96))), [oF, ("Eb", 0, 96)], [full_w], cost=0.35)
         emit("v", lambda: g.vector.tensor_copy(ap(("vb", 0, 96)), win(oB, MKW)), [oB, full_w], [("vb", 0, 96)], cost=0.2)
-        o = ("k0", 0, 96)
+        o = ("SP", 128, 224)
         mm([(o, M("R12"), ("mf", 0, 96), True, False)])
         mm([(o, M("ISY"), ("vb", 0, 96), False, False), (o, M("DN"), ("vb", 0, 96), False, True)])
         act(("Sb", 0, 96), o, Fn.Copy)
         emit("v", lambda: g.vector.tensor_copy(win(oB, MKW), ap(("Sb", 0, 96))), [oB, ("Sb", 0, 96)], [full_w], cost=0.35)
 
     consts_search()
+    for c in range(NC):
+        ts(chunk("q0", c), chunk("qN", c), KLT, Op.mult)
+        first_rope(0, c, "qN", "B%d" % c)
+        power(0, c, 1, "SP")
+        mask(0, c, 1, "qN")
+        keep(c, "qN", "SQ")
     consts_edits()
-    for p in range(4):
-        send(0, p, tab, made)
+    sends(0, None, tab)
     arrivals(0)
-    load(("mkE", 0, W), T.mk[:], "dm2", 6.0, [len(ops) - 3, len(ops) - 2, len(ops) - 1])
-    for c in range(2):
-        for h in range(2):
-            mm([(gb(c, h), LJ(12), half("qN", c, h), True, True)])
-            act(gb(c, h), gb(c, h), Fn.Relu, bias=NBI, scale=256.0)
-            tt(half("zz", c, h), half("qN", c, h), gb(c, h), Op.min)
-        first_length(0, c, "qN")
-        from_length(0, c, 1)
-        sums(c, True)
-        for h in range(2):
-            act(half("q0", c, h), half("qN", c, h), Fn.Copy, scale=KLT)
-        first_rope(c, "qN")
-        jmajor(c, "qN")
-    step(0, 0, 1, "q0")
+    load(("mkE", 0, W), T.mk[:], "dm2", 6.0, list(come.values()))
     later_steps(0, "q0")
-    for c in range(2):
-        for h in range(2):
-            mm([(gb(c, h), LJ(12), half("qO", c, h), True, True)])
-            act(half("r1", c, h), gb(c, h), Fn.Relu, bias=NBI, scale=256.0)
-        first_length(1, c, "qO")
-        first_rope(c, "qO")
-        from_length(1, c, 1)
-    for c in range(2):
-        learn(0, c, "q0", lambda p: ("dR", own, own + NB) if goes[p] == rank else ("dS", NB * p, NB * p + NB),
-              lambda p, i: send(1, p, [i]))
+    for c in range(NC):
+        first_rope(1, c, "qO", "SQ")
+        power(1, c, 1, "SQ")
+
+    def learnt(p):
+        out = []
+        for i in (2 * p, 2 * p + 1):
+            at = came.index((rank, goes[i][1])) if goes[i][0] == rank else None
+            to = units("dS", i) if at is None else units("dR", at)
+            if out and out[-1][2][0] == to[0] and out[-1][2][2] == to[1]:
+                out[-1] = (out[-1][0], 2, (to[0], out[-1][2][1], to[2]))
+            else:
+                out.append((i, 1, to))
+        return out
+
+    for c in range(NC):
+        learn(0, c, "q0", learnt, lambda i, n, x: None)
+        sends(1, c)
     edits()
     arrivals(1)
-    for c in range(2):
-        for h in range(2):
-            mm([(gb(c, h), M("ISY"), half("qO", c, h), True, False)])
-            mm([(gb(c, h), M("ID"), half("dR", c, h), False, True)])
-            tt(half("zz", c, h), gb(c, h), half("r1", c, h), Op.min)
-            act(half("q1", c, h), gb(c, h), Fn.Copy)
-        sums(c, True)
-        jmajor(c, "q1")
-    step(1, 0, 1, "q1")
+    for c in range(NC):
+        mask(1, c, 1, "qO", "dR")
+        mm([(("SQ", 0, 512), M("ISY"), chunk("qO", c), True, False)])
+        mm([(("SQ", 0, 512), M("ID"), chunk("dR", c), False, True)])
+        act(chunk("q1", c), ("SQ", 0, 512), Fn.Copy)
     later_steps(1, "q1")
 
-    def out(p, i):
-        c, h = p // 2, p % 2
-        b, x = half("qF", c, h), NB * came[p]
+    def out(i, n, x):
+        c, p = i // 4, i // 2
+        b, z = units("qF", i, n), (own("Z", 1, c), NU * (i % 4), NU * (i % 4 + n))
+        if p % 2 and p not in ADD_V:
+            z = (own("B", 1, c), 0, 256)
         if p in ADD_V:
-            tt(b, gb(c, h), half("dF", c, h), Op.add)
+            tt(b, z, units("dF", i, n), Op.add)
         else:
-            mm([(gb(c, h), M("ID"), half("dF", c, h), False, True)])
-            act(b, gb(c, h), Fn.Copy)
-        lead[emit("s", lambda: g.sync.dma_start(T.yq[:, x:x + NB], ap(b)), [b], [], "dy%d" % p, 1.5)] = (1 - c, 0.6 - 0.6 * h)
+            mm([(z, M("ID"), units("dF", i, n), False, True)])
+            act(b, z, Fn.Copy)
+        for j, w in runs(came, 2):
+            if j // 2 == p:
+                lead[emit("s", lambda j=j, w=w: g.sync.dma_start(hbm(T.yq, came[j], w), ap(units("qF", j, w))), [units("qF", j, w)], [],
+                          "dy%d" % j, 1.5)] = AHEAD[c]
 
-    for c in range(2):
-        for h in range(2):
-            mm([(gb(c, h), M("ID"), half("qO", c, h), True, False), (gb(c, h), M("ID"), half("dR", c, h), False,
-                                                                    2 * c + h in ADD_V)])
-        learn(1, c, "q1", lambda p: ("dF", NB * p, NB * p + NB), out)
-        ts(sm("Bm", c), odd(pair("XB", c, 4, 5)), -1.0, Op.add)
-        for p in (2 * c, 2 * c + 1):
-            tt(("yS", 24 * came[p], 24 * came[p] + 24), ("Hb", 24 * p, 24 * p + 24), ("Bm", 24 * p, 24 * p + 24), Op.min)
-    emit("s", lambda: g.sync.dma_start(T.yb[:], T.yS[:]), [("yS", 0, 96)], [], "db0", 1.2)
-    return ops, lead, sent, come, issue
+    for c in range(NC):
+        for h in (1, 0) if 2 * c + 1 in ADD_V else (0,):
+            z = (own("Z", 1, c), 256 * h, 256 * h + 256)
+            mm([(z, M("ID"), half("qO", c, h), True, False), (z, M("ID"), half("dR", c, h), False, 2 * c + h in ADD_V)])
+        learn(1, c, "q1", lambda p: [(2 * p, 2, units("dF", 2 * p, 2))], out)
+    emit("s", lambda: g.sync.dma_start(T.yb[:], T.yS[:]), [("yS", 0, 96)], [], "db", 1.2)
+    return ops, lead, sent, come, issue, names

@@ -7,23 +7,25 @@ CH, NT, NC = 512, 32, 3
 MKW = W + 128
 LN2 = math.log(2.0)
 MAGIC = 1.5 * 2.0 ** 23
-NONE = -136.0 * 8192 - 2048
+NONE = -234.0 * 8192 - 2048
 TILT = 0.000435
 CYC, PEC, WAKE, ISSUE = 0.00083, 0.00042, 0.19, 0.05
-GAT, TMK, TFAR, TNEAR, APART, TSEND, TFIRST = 1.5, 6.0, 4.0, 2.0, 1.9, 0.5, 3.0
-FIXV, FIXA, GW = 0.035, 0.055, 32
-AHEAD = (3.2, 2.0, 0.0)
+GAT, TMK, TFAR, TNEAR, APART, TSEND, TFIRST = 1.5, 6.0, 4.3, 2.2, 1.9, 0.5, 3.0
+FIXV, FIXA, FIXP = 0.035, 0.055, 0.03
+AHEAD, FAST, SPLIT = (3.2, 2.0, 0.0), 1, ((0, 6), (6, 12))
 LEAD, SLOW, FACTORS = 1.0, 1.05, ((1.0, 0.2, 1.0), (1.0, 0.16, 1.2), (1.35, 0.16, 1.35))
-TRIES, SPAN, SHIFT, SHARE = 1200, 15.0, 0.4, 0.06
-BY_SCALAR = ((0, 1, 3), (1, 3, 5))
+TRIES, SPAN, SHIFT, SHARE, SWAPS = 380, 15.0, 0.4, 0.06, 1500
+KEEP, ACC, TACC, TLATE, GATE, SEED = (3, 3), False, 2.8, 5.0, 0, 1
+PART, TAIL, EASE, UPPER_V, HALVES, EARLY = 6, 6.5, 0.0, (2,), True, 0.0
+FINE = ((0, 1, 2, 3, 4, 5), (0, 1, 2, 3))
 ADD_V = (4, 5)
 
-_mats = ["XP", "ID", "NI", "I97", "I8K", "I256", "ISY", "N8K", "CA", "DN", "R12", "T2K", "CST", "ZM", "half", "I13", "hf2"]
-SCRATCH = {"mkT": ("sbuf", [128, W], "bfloat16"), "mkE": ("sbuf", [128, MKW], "bfloat16"),
+_mats = ["XP", "ID", "NI", "I97", "I8K", "I256", "ISY", "N8K", "CA", "DN", "R12", "T2K", "CST", "ZM", "half", "I13", "hf2", "I32"]
+SCRATCH = {"mkE": ("sbuf", [128, MKW], "bfloat16"),
            "LB": ("sbuf", [128, 512], "bfloat16"), "HW": ("sbuf", [128, 32 * 4 + 3, 4], "float16"),
-           "HV": ("sbuf", [128, 32 * 7 + 3, 4], "bfloat16"),
+           "HV": ("sbuf", [128, 32 * 11 + 3, 4], "bfloat16"), "TJ": ("sbuf", [128, 32], "float16"),
            "khb": ("sbuf", [128, 48], "float16")}
-for _n in ("qN", "q0", "qO", "qP", "q1", "dR", "dS", "dF", "qF", "zz", "nn", "dd", "rr"):
+for _n in ("qN", "q0", "qO", "qP", "q1", "dR", "dS", "dF", "qF", "zz", "rr"):
     SCRATCH[_n] = ("sbuf", [128, K], "bfloat16")
 for _n in _mats:
     SCRATCH[_n] = ("sbuf", [128, 128], "bfloat16")
@@ -35,10 +37,10 @@ def _add(dtype, **widths):
 
 
 _add("bfloat16", wS=2, land0=NB, land1=NB, JR=96, LT=96, ONE=128, IO=36, MK=36, W0=106, W1=288, W2=288, WS=40, MB=480, SPM=384, MG=96,
-     MKG=36, M12=36, PM=384, OF=96, qK=1152, f0=768, sl=1728, ET=768, Cw=192, Cx=192, dead=64, none=96, MS=984, NM=160, sb=48, cm=96, Eb=96, vb=96, mf=96, Sb=96, IT=192,
+     nn=4 * K, dd=96, MKG=36, M12=36, PM=384, OF=96, qK=1152, f0=768, sl=1728, ET=768, Cw=192, Cx=192, dead=64, none=96, MS=984, NM=160, sb=48, cm=96, Eb=96, vb=96, mf=96, Sb=96, IT=192,
      J16=16, EQ=1152, MN=1152, NEW=NB)
 _add("int32", pi=1, ki=2, ci=4, X=288, H=96)
-_add("float32", col=48, D0=288, yS=96, HM=40, WD=24, WO=24, TO=12, ed=96, key=12, w1=12, w2=12, mk1=96, BT=480, FT=160)
+_add("float32", col=48, geo=64, D0=192, yS=96, HM=40, WD=24, WO=24, TO=12, key=24, w1=12, w2=12, mk1=96, BT=480, FT=160)
 _add("uint16", OFF=96, OB=192, OE=12)
 BANKS = ("Z0", "Z1", "Z2", "B0", "B1", "B2", "SP", "SQ")
 for _n in BANKS:
@@ -78,7 +80,7 @@ def goes_order(rank, cores, topo):
 def came_order(rank, cores, topo):
     def when(x):
         at = goes_order(x[0], cores, topo).index((rank, x[1])) // 4
-        return (APART * at + (0.0, TNEAR, TFAR)[way(x[0], rank, cores, topo)], x[0] ^ rank, x[1])
+        return (APART * at + (0.0, TNEAR - EARLY, TFAR)[way(x[0], rank, cores, topo)], x[0] ^ rank, x[1])
     return sorted([(s, u) for s in range(len(cores)) for u in range(3)], key=when)
 
 
@@ -108,7 +110,6 @@ def count(mask):
     return bin(mask).count("1")
 
 
-TABLE = ("mkT", "mkE")
 LANDS = ("qO", "dR")
 
 
@@ -228,15 +229,108 @@ def orders(ranks):
     for i in reversed(first):
         tail[i] = max([cost[i] + LEAD * lead.get(i, 0)] + [tail[j] + lag for j, lag in succ[i]])
     best = tight(sweep([-x for x in tail], False))
-    rnd = np.random.default_rng(1)
+    rnd = np.random.default_rng(SEED)
     for k in range(TRIES):
         lo = float(rnd.random()) * best[0] - SPAN / 2
         move = (rnd.normal(size=len(names)) * SHIFT * (rnd.random(len(names)) < SHARE)).tolist()
         new = tight([a + move[name[i]] if lo < a < lo + SPAN else a for i, a in enumerate(best[1])], best[3] + 0.2)
         if new[0] <= best[0]:
             best = new
-    NOTE[:] = [best[0], length(best[2], 1.0), length(best[2], 1.4)]
-    return [[i - base[r] for i in best[2] if ops[i][0][0] == r] for r in range(len(ranks))]
+    seq = swapped(ops, base, name, succ, best[2], rnd)
+    NOTE[:] = [best[0], sum(length(seq, f, w, pf) / f for f, w, pf in FACTORS) / len(FACTORS), length(seq, 1.0), length(seq, 1.4)]
+    return [[i - base[r] for i in seq if ops[i][0][0] == r] for r in range(len(ranks))]
+
+
+def swapped(ops, base, name, succ, seq, rnd):
+    n, ranks = len(ops), len(base) - 1
+    byname = {(ops[i][0][0], name[i]): i for i in range(n)}
+    dep = [x[4] | x[5] for x in ops]
+    costs = [[x[3] * ((pf if x[0][1] == "p" else f) if x[2] else 1.0) for x in ops] for f, w, pf in FACTORS]
+    prv, nxt, last = [-1] * n, [-1] * n, {}
+    for i in seq:
+        if ops[i][0] in last:
+            prv[i], nxt[last[ops[i][0]]] = last[ops[i][0]], i
+        last[ops[i][0]] = i
+
+    after = [[x[0] for x in y] for y in succ]
+    waits = [list(x[4]) for x in ops]
+    order = [[d for d in x[5] if ops[d][0] != x[0]] for x in ops]
+    final = [[i for i in range(base[r], base[r + 1]) if not after[i]] for r in range(ranks)]
+    held = [[ISSUE if x[1] else y for x, y in zip(ops, c)] for c in costs]
+
+    def listed():
+        need = [len(d) + (p >= 0) for d, p in zip(dep, prv)]
+        out = [i for i in range(n) if need[i] == 0]
+        for i in out:
+            for j in after[i]:
+                need[j] -= 1
+                if need[j] == 0:
+                    out.append(j)
+            j = nxt[i]
+            if j >= 0:
+                need[j] -= 1
+                if need[j] == 0:
+                    out.append(j)
+        return out if len(out) == n else None
+
+    def run(seq, most=None):
+        total, ways = 0.0, []
+        for c, h, (f, wake, pf) in zip(costs, held, FACTORS):
+            start, seen, why = [0.0] * n, [0.0] * n, [-1] * n
+            for i in seq:
+                y = prv[i]
+                t = start[y] + h[y] if y >= 0 else 0.0
+                for d in waits[i]:
+                    if seen[d] > t:
+                        t, y = seen[d], d
+                for d in order[i]:
+                    if start[d] > t:
+                        t, y = start[d], d
+                start[i], seen[i], why[i] = t, t + c[i] + wake, y
+            ends = [max((seen[i], i) for i in x) for x in final]
+            t = (max(ends)[0] + sum(x[0] for x in ends) / ranks) / 2 / f
+            if most and not ways and t > most[0][2] + 0.15:
+                return 1e9, None
+            total += t
+            ways.append((why, [x[1] for x in ends], t))
+        return total, ways
+
+    def swap(u, v):
+        a, b = prv[u], nxt[v]
+        prv[v], nxt[v], prv[u], nxt[u] = a, u, v, b
+        if a >= 0:
+            nxt[a] = v
+        if b >= 0:
+            prv[b] = u
+
+    best, ways = run(seq)
+    for k in range(SWAPS):
+        why, ends = ways[int(rnd.integers(len(ways)))][:2]
+        i, arcs = ends[int(rnd.integers(ranks))], []
+        while why[i] >= 0:
+            if why[i] == prv[i] and why[i] not in dep[i]:
+                arcs.append((why[i], i))
+            i = why[i]
+        u, v = arcs[int(rnd.integers(len(arcs)))]
+        steps, ahead, done = int(rnd.integers(1, 4)), rnd.random() < 0.5, []
+        for r in range(ranks):
+            a, b = byname.get((r, name[u])), byname.get((r, name[v]))
+            if a is None or b is None or prv[b] != a:
+                continue
+            for x in range(steps):
+                a, b = (prv[b], b) if ahead else (a, nxt[a])
+                if a < 0 or b < 0 or a in dep[b]:
+                    break
+                swap(a, b)
+                done.append((b, a))
+        new = listed()
+        t = run(new, ways) if new and done else (1e9, None)
+        if t[0] <= best + EASE * (1 - k / SWAPS) * float(rnd.random()):
+            seq, (best, ways) = new, t
+        else:
+            for a, b in reversed(done):
+                swap(a, b)
+    return seq
 
 
 NOTE = []
@@ -329,7 +423,10 @@ def calls(g, rank, T, topo):
             c = dict(clock[q])
             c[evs[i][0]] = evs[i][1]
             clkat[evs[i]] = c
-        await_all("g", list(total.items()))
+        stores = [x for x in total.items() if x[0][:2] in ("dy", "db")]
+        await_all("g", [x for x in total.items() if x not in stores])
+        for x in stores:
+            await_all("g", [x])
 
     def wide(b):
         step = b[3] if len(b) > 3 else 1
@@ -392,7 +489,10 @@ def calls(g, rank, T, topo):
             return ins
         reads = sorted(set(x[1][:3] for x in seq) | set(x[2][:3] for x in seq))
         reads += [y[:3] + (1, (32, 33)) for x in seq for y in x[1:3] if len(y) == 5 and y[4] == 33]
-        return emit("p", go, reads, [seq[0][0]], cost=sum(max(min(64, wide(x[1])), wide(x[0])) for x in seq) * PEC + 0.03)
+        return emit("p", go, reads, [seq[0][0]], cost=sum(max(min(64, wide(x[1])), wide(x[0])) for x in seq) * PEC + FIXP,
+                    behind=list(gate))
+
+    gate, sums = [], []
 
     def LJ(j):
         return ("LB", 128 * j, 128 * j + 128)
@@ -416,16 +516,20 @@ def calls(g, rank, T, topo):
     emit("a", lambda: g.scalar.dma_start(ap(("wS", 0, 2)), T.wt[:]), [], [("wS", 0, 2)], "dw", 1.0)
     for i, n in runs(goes, 4):
         load(units("qN", i, n), hbm(T.qs, goes[i], n), "dq%d" % i, 1.4 + 0.15 * (i + n))
-    tab = [load(("mkT", x, x + W // 2), T.mk[:, x:x + W // 2], "dm%d" % (2 * x // W), TMK) for x in (0, W // 2)]
+    tab = [load(("mkE", x, x + W // 2), T.mk[:, x:x + W // 2], "dm%d" % (2 * x // W), TMK) for x in (0, W // 2)]
     for u, i, j, n in pieces(0, rank, rank, cores, topo):
-        load(units("qO", j, n), hbm(T.qs, (rank, u), n), "do%d" % u, TMK + 0.5)
+        if ACC:
+            emit("g", lambda j=j, n=n, u=u: g.dma_start(ap(units("qO", j, n)), hbm(T.qs, (rank, u), n)), [], [units("qO", j, n)],
+                 "do%d" % u, 4.0, None, tab)
+        else:
+            load(units("qO", j, n), hbm(T.qs, (rank, u), n), "do%d" % u, TMK + 0.5)
 
     def C(i):
         return ("col", i, i + 1)
     KC, KA, KLT, KGE, KP1, RCOL, KK, G4, G8, GE, GS, OFS, OF32, N32, P97 = [C(i) for i in range(15)]
     T1, T2, T3, T4, T5, M15, T6, T7 = [C(16 + i) for i in range(8)]
     RC0 = ("E16", 12, 13)
-    made = []
+    made, soon = [], []
 
     def iota(out, pattern, base, cm, flag=True, behind=()):
         c = 0.13 + 2 * wide(out) * CYC
@@ -457,7 +561,9 @@ def calls(g, rank, T, topo):
         cp(KC, ki)
         fill(("MG", 0, 96), 1.5 * 2.0 ** 35)
         x = act(M("half"), M("ONE"), Fn.Exp, scale=-LN2, more=1.3)
-        act(T1, KC, Fn.Exp, bias=-57 * LN2, scale=10 * LN2, behind=[x])
+        ts(("geo", 0, 16), ("IO", 0, 16), KC, Op.is_lt, 2.0 ** -10, Op.max)
+        emit("v", lambda: g.vector.tensor_tensor_scan(ap(("geo", 16, 32)), ap(("geo", 0, 16)), ap(("geo", 0, 16)), -2.0 ** 93, Op.mult,
+                                                      Op.min), [("geo", 0, 16)], [("geo", 16, 32)], cost=0.09)
         act(T6, KC, Fn.Exp, bias=50 * LN2, scale=-10 * LN2, behind=[x])
         ts(KLT, ki, 11.5, Op.is_lt)
         ts(G4, kg, 4.0, Op.mult, 3.0, Op.add)
@@ -466,28 +572,32 @@ def calls(g, rank, T, topo):
             diag(nm, x)
         pick(("WS", 8, 40), ("ONE", 0, 32), [[-1, 4], [-16, 8]], Op.is_equal, 0.0, -12, 1)
         pick(("M12", 0, 36), ("ONE", 0, 36), [[-16, 9], [1000, 4]], Op.is_equal, 0.0, -3012, 1)
+        ts(("ci", 1, 2), ki, 2, Op.arith_shift_right)
+        ts(("col", 32, 35), ("IO", 0, 3), ("ci", 1, 2), Op.is_equal)
         for b in range(3):
-            pick(PM(b), M("ONE"), [[-16, 8], [1000, 4], [-1, 4]], Op.is_equal, 0.0, -3000 - 4 * b, 1)
-        ts(("MKG", 0, 36), ("MK", 0, 36), T1, Op.mult, -1.0, Op.mult)
+            ts(PM(b), M("XP"), 12.0 - 4 * b, Op.is_equal, C(32 + b), Op.mult)
+        ts(("MKG", 0, 36), ("MK", 0, 36), ("geo", 30, 31), Op.mult)
         mm([(("SQ", 128 * b, 128 * b + 128, 1, 32), ("MKG", x, x + 32), y, y[0] == "ISY", y[0] == "PM")
             for b in range(3) for x, y in ((3 - b, M("ISY")), (0, PM(b)))])
-        act(("SPM", 0, 384, 1, 32), ("SQ", 0, 384, 1, 32), Fn.Copy)
+        cp(("SPM", 0, 384, 1, 32), ("SQ", 0, 384, 1, 32))
         fill(("SPM", 0, 384, 1, (32, 33)), MAGIC)
-        fill(("ET", 0, 768, 1, (32, 33)), 1.0)
-        for k, (x, scale) in enumerate(((0, 1.0), (1, 32.0), (1, 1.0))):
-            ts(("W0", k, 105, 3), ("MK", 0, 35), ("wS", x, x + 1), Op.mult, scale, Op.mult)
-        mm([(("SP", 96 * b, 96 * b + 96), y, ("W0", x, x + 96), y[0] == "ISY", y[0] == "PM")
-            for b in range(3) for x, y in ((9 - 3 * b, M("ISY")), (0, PM(b)))])
-        act(("W1", 0, 288), ("SP", 0, 288), Fn.Copy, scale=-1.0)
+        fill(("ET", 0, 128, 1, (32, 33)), 1.0)
+        fill(("ET", 128, 768, 1, (32, 33)), 1.0)
+        for o, x, scale in ((("W0", 0, 70, 2), 0, 1.0), (("W0", 1, 70, 2), 1, 32.0), (("W0", 70, 105), 1, 1.0)):
+            ts(o, ("MK", 0, 35), ("wS", x, x + 1), Op.mult, scale, Op.mult)
+        mm([(("Z2", 96 * b + lo, 96 * b + lo + 32 * n), y, ("W0", at + n * x, at + n * (x + 32)), y[0] == "ISY", y[0] == "PM")
+            for b in range(3) for lo, at, n in ((0, 0, 2), (64, 70, 1)) for x, y in ((3 - b, M("ISY")), (0, PM(b)))])
+        sums.append(len(ops) - 1)
+        act(("W1", 0, 288), ("Z2", 0, 288), Fn.Copy, scale=-1.0)
         ts(("W2", 0, 288), ("W1", 0, 288), -1.0, Op.mult)
         iota(("OF", 0, 96, 1, 2), [[0, 96]], 4096, -4097)
-        iota(("OF", 1, 96, 3, 2), [[0, 32]], -393216, 393184)
-        fill(("MG", 1, 96, 3), 1.5 * 2.0 ** 40)
-        fill(("D0", 0, 288), 0.0)
+        iota(("OF", 1, 64, 2, 2), [[0, 32]], -393216, 393184)
+        fill(("MG", 1, 64, 2), 1.5 * 2.0 ** 40)
+        fill(("D0", 0, 192, 2), 0.0)
         fill(("HW", 0, 524), 0.0)
         ts(("WS", 0, 8), ("MK", 3, 35, 4), T6, Op.mult, KLT, Op.mult)
         iota(M("T2K", 2), [[0, 128]], 2048, 0)
-        iota(M("CST", 2), [[32, 4], [0, 32]], -236, 0)
+        iota(M("CST", 2), [[32, 4], [0, 32]], -464, 0)
         fill(("MS", 1, 984, 2), 0.0)
         fill(("MS", 0, 984, 2), 1.0)
         for c in range(NC):
@@ -502,15 +612,18 @@ def calls(g, rank, T, topo):
         for j in range(4):
             pick(LJ(j), M("ONE"), [[-16, 8], [0, 16]], Op.is_equal, 0.0, -j, 1)
         iota(("IT", 0, 192), [[0, 2], [1, 96]], 0, 0)
-        iota(("w1", 0, 12), [[0, 2], [16, 6]], W, 0)
+        soon.append(iota(("w1", 0, 12), [[0, 2], [16, 6]], W, 0))
         pick(M("CA"), M("ONE"), [[-16, 8], [-1, 4], [-1, 4]], Op.is_equal, 0.0, -13, 1)
         pick(M("CA"), M("CA"), [[0, 8], [-1, 4], [-1, 4]], Op.is_ge, 0.0, 2, 0)
-        ts(("ci", 1, 2), ("ki", 0, 1), 2, Op.arith_shift_right)
-        ts(KK, ("ci", 1, 2), -16.0, Op.mult, -80.0, Op.add)
+        ts(KK, ("ci", 1, 2), -16.0, Op.mult, 2096.0, Op.add)
         pick(M("I13"), M("ZM"), [[-1, 128]], Op.not_equal, 2.0 ** -13, 0, 1)
-        fill(("hf2", 0, 32), 0.5)
-        fill(("hf2", 32, 64), 136 / 4096)
-        fill(("HV", 0, 908), 0.0)
+        pick(M("I32"), M("ZM"), [[-1, 128]], Op.not_equal, 32.0, 0, 1)
+        for x, y in enumerate((-66048, 250, 2048)):
+            fill(("hf2", 32 * x, 32 * x + 32), y / 4096)
+        iota(("geo", 32, 64), [[16, 32]], 0, 0)
+        ts(("TJ", 0, 32), ("geo", 32, 64), KC, Op.add)
+        fill(("HV", 0, 780), 0.0)
+        zero(("HV", 780, 1420))
         pick(M("DN"), M("ONE"), [[-16, 8], [-1, 16]], Op.is_equal, 0.0, 1, 1)
         pick(M("DN"), M("DN"), [[0, 8], [1, 16]], Op.is_ge, 0.0, -13, 0)
         pick(M("R12"), M("ONE"), [[-16, 8], [1000, 16]], Op.is_equal, 0.0, -12012, 1)
@@ -566,7 +679,7 @@ def calls(g, rank, T, topo):
 
     def power(r, c, s, bank):
         o, e = (bank, 128 + 128 * c, 256 + 128 * c, 1, 32), 2 * c + (r if s == 1 else 0)
-        if (r, s) == (0, 1):
+        if (r, s) == (0, 1) and c < FAST:
             mm([(o, ("M12", 3 - b, 35 - b), block("qN", c, b), b == 0, b == 3) for b in range(4)])
         else:
             mm([(o, rope(r, c, s, 0), M("ID"), True, True)])
@@ -574,13 +687,18 @@ def calls(g, rank, T, topo):
 
     def mask(r, c, s, src, late=None):
         z, e = own("Z", r, c), 2 * c + (r if s == 1 else 0)
-        if s == 1:
+        if s < KEEP[r]:
             pack(z, c, src, True, False)
         else:
             mm([((z, 0, 384), M("ID"), packed("qK", c), True, False)])
         mm([((z, 128 * b, 128 * b + 128), ("SPM", 128 * b, 128 * b + 128, 1, 33), ("ET", 128 * e, 128 * e + 128, 1, 33), False,
              b == 2 and late is None) for b in range(3)])
-        if late:
+        if late and HALVES:
+            for h in range(2):
+                lo = c * CH + 256 * h
+                mm([((z, 128 * b + 64 * h, 128 * b + 64 * h + 64), y, (late, lo + x, lo + 256, 4), False, (h, b, x) == (1, 2, 3))
+                    for b in range(3) for x, y in ((b, M("ISY")), (3, PM(b)))])
+        elif late:
             pack(z, c, late, False, True)
         act(packed("zz", c), (z, 0, 384), Fn.Relu, bias=-MAGIC)
 
@@ -588,8 +706,10 @@ def calls(g, rank, T, topo):
         return (nm, 384 * c, 384 * c + 384)
 
     def pack(bank, c, src, start, stop):
-        mm([((bank, 128 * b, 128 * b + 128), y, block(src, c, x), start and b == 0 and x == 0, stop and b == 2 and x == 3)
-            for b in range(3) for x, y in ((b, M("ISY")), (3, PM(b)))])
+        seq = [((bank, 128 * b, 128 * b + 128), y, block(src, c, x), start and b == 0 and x == 0, stop and b == 2 and x == 3)
+               for b in range(3) for x, y in ((b, M("ISY")), (3, PM(b)))]
+        for x in range(0, 6, PART if start else 6):
+            mm(seq[x:x + (PART if start else 6)])
 
     def keep(c, src, bank):
         pack(bank, c, src, True, True)
@@ -601,7 +721,7 @@ def calls(g, rank, T, topo):
     def step(r, c, s, q0):
         bk = own("B", r, c)
         mu = rope(r, c, s, 0)
-        o, o1 = (bk, 256, 352), (bk, 257, 352, 3)
+        o = (bk, 256, 352)
 
         def zb(b):
             return ("zz", 384 * c + 128 * b, 384 * c + 128 * b + 128)
@@ -610,11 +730,11 @@ def calls(g, rank, T, topo):
         act(cx, mu, Fn.Exp, bias=math.log(1.5) + 83 * LN2 - 6.5 * TILT, scale=-10 * LN2 + TILT)
         mm([(o, M("half", 2), ("OF", 0, 96, 1, 2), True, False)])
         mm([(o, zb(b), ("W1", 96 * b, 96 * b + 96), False, False) for b in range(3)]
-           + [(o, M("ID"), ("MG", 0, 96), False, False), (o, M("NI"), ("MG", 0, 96), False, False), (o1, M("I97"), mu, False, False)]
+           + [(o, M(x), ("MG", 0, 96), False, False) for x in ("ID", "NI")] + [((bk, 257, 320, 2), M("I97"), mu, False, False)]
            + [(o, zb(b), ("W2", 96 * b, 96 * b + 96), False, b == 2) for b in range(3)])
-        act(("D0", 96 * c + 1, 96 * c + 96, 3), (bk, 258, 352, 3), Fn.Copy)
-        scan(("X", 96 * c, 96 * c + 96), ("D0", 96 * c, 96 * c + 96), o, Op.add)
-        ts(sm("H", c), ("X", 96 * c + 1, 96 * c + 96, 3), 5, Op.arith_shift_right, 4095, Op.bitwise_and)
+        act(("D0", 64 * c + 1, 64 * c + 64, 2), (bk, 320, 352), Fn.Copy)
+        scan(("X", 64 * c, 64 * c + 64), ("D0", 64 * c, 64 * c + 64), (bk, 256, 320), Op.add)
+        ts(sm("H", c), ("X", 64 * c + 1, 64 * c + 64, 2), 5, Op.arith_shift_right, 4095, Op.bitwise_and)
         ts(put(c), sm("H", c), -2048.0, Op.add)
         turn([((bk, 256, 288), put(c), "ID")])
         ts(sm("OFF", c), (bk, 256, 288), 2048.0, Op.add)
@@ -623,11 +743,11 @@ def calls(g, rank, T, topo):
             (code, M("ID"), put(c), False, True), ((bk, 0, 64, 2), M("ID"), cw, True, False)]
            + [((bk, 64 * k + x, 64 * k + 64, 2), M(y), rope(r, c, s, k), False, False)
               for k in range(1, 5 - s) for x, y in enumerate(("NI", "ID"))])
-        for x in range(0, 32, GW):
-            gathered(("nn", c * CH + 16 * x, c * CH + 16 * (x + GW)), ("OFF", 32 * c + x, 32 * c + x + GW),
-                     (q0, c * CH + 16 * x, c * CH + 16 * (x + GW)), Op.subtract, TABLE[r])
+        x = gathered(chunk("nn", 4 * c + s - 1), sm("OFF", c), chunk(q0, c), Op.subtract, "mkE")
+        if (r, s) == (1, 4) and TAIL:
+            lead[x] = TAIL + AHEAD[c]
         n = 5 - s
-        mm([((bk, 2 * b, 64 * n, 8), block("nn", c, b), ("WS", 0, 8 * n), False, b == 3) for b in range(4)])
+        mm([((bk, 2 * b, 64 * n, 8), block("nn", 4 * c + s - 1, b), ("WS", 0, 8 * n), False, b == 3) for b in range(4)])
         lo = 328 * c + 8
         flag = ("MS", lo + 2 * s, lo + 320, 10) if s < 4 else ("MB", 160 * c + 4, 160 * c + 160, 5)
         tt(flag, (bk, 0, 64, 2), cx, Op.is_equal if s < 4 else Op.not_equal)
@@ -642,9 +762,9 @@ def calls(g, rank, T, topo):
     def win(off, w=W):
         return T.mkE[:, 0:w].indirect(ap(off))
 
-    def gathered(o, off, q, op, nm, w=W):
-        return emit("v", lambda: g.vector.tensor_tensor(ap(o), T[nm][:, 0:w].indirect(ap(off)), ap(q), op), [(nm, 0, w), off, q],
-                    [o], cost=0.05 + GAT * CYC * wide(o))
+    def gathered(o, off, q, op, nm, w=W, lo=0):
+        return emit("v", lambda: g.vector.tensor_tensor(ap(o), T[nm][:, lo:lo + w].indirect(ap(off)), ap(q), op),
+                    [(nm, lo, lo + w), off, q], [o], cost=0.05 + GAT * CYC * wide(o))
 
     def picked(o, off, nm, w=W):
         return emit("a", lambda: g.scalar.activation(ap(o), T[nm][:, 0:w].indirect(ap(off)), Fn.Copy), [(nm, 0, w), off], [o],
@@ -653,31 +773,34 @@ def calls(g, rank, T, topo):
     def later_steps(r, q0):
         for s in range(1, 5):
             for c in range(NC):
-                if (r, s) == (1, 2):
-                    keep(c, q0, "SP")
+                if s == KEEP[r]:
+                    keep(c, q0, "SP" if (r, s) == (1, 2) else "SQ")
                 if s > 1:
                     power(r, c, s, "SP")
                     mask(r, c, s, q0)
                 step(r, c, s, q0)
 
-    def rounded(out, a, k):
-        ts(out, a, 1.5 * 2.0 ** (23 + k), Op.add, 1.5 * 2.0 ** (23 + k), Op.subtract)
-
-    def parts(code, k):
-        rounded(put(k, "HV"), code, 13)
-        tt(put(k), code, put(k, "HV"), Op.subtract)
+    def step_of(out, code):
+        act(out, code, Fn.Copy, bias=2291.0, scale=2.0 ** -13)
 
     def learn(r, c, q0, dests, after):
         bk = own("B", r, c)
         scan(("BT", 160 * c, 160 * c + 160), ("MB", 160 * c, 160 * c + 160), (bk, 352, 512), Op.min)
-        parts(("BT", 160 * c + 4, 160 * c + 160, 5), c)
-        turn([((bk, 288, 320), put(c, "HV"), "I13"), ((bk, 256, 288), put(c), "ID")],
-             [((bk, 256, 320), M("T2K", 2), ("hf2", 0, 64, 1, 2))], True)
+        code = ("BT", 160 * c + 4, 160 * c + 160, 5)
+        step_of(put(8 + c, "HV"), code)
+        if c in UPPER_V:
+            cp(put(c, "HV"), code)
+        else:
+            act(put(c, "HV"), code, Fn.Copy)
+        turn([((bk, 288, 320), put(c, "HV"), "I13"), ((bk, 256, 288), put(8 + c, "HV"), "I32")],
+             [((bk, 256, 288), M("ID"), ("TJ", 0, 32)), ((bk, 256, 320), M("T2K", 2), ("hf2", 0, 64, 1, 2))], True)
         cp(("OB", 64 * c, 64 * c + 64), (bk, 256, 320))
+        if r or c == 0:
+            tt(put(c), code, put(c, "HV"), Op.subtract)
         if r:
-            act(sm("none", c), (bk, 288, 320), Fn.Relu, bias=1.0, scale=-1.0)
+            act(sm("none", c), (bk, 288, 320), Fn.Relu, bias=17.0, scale=-1.0)
             turn([((bk, 288, 320), put(c), "ID")], [((bk, 288, 320), M("NI"), sm("none", c)),
-                                                    ((bk, 288, 320), M("T2K", 2), ("hf2", 0, 32, 1, 2))])
+                                                    ((bk, 288, 320), M("T2K", 2), ("hf2", 64, 96, 1, 2))])
             for j, w in runs(came, 4):
                 if j // 4 == c:
                     x, y = 24 * came[j][0] + 8 * came[j][1], 288 + 8 * (j % 4)
@@ -687,20 +810,13 @@ def calls(g, rank, T, topo):
         for h in range(2):
             p = 2 * c + h
             x = 64 * c + 16 * h
-            ob, d = ("OB", x, x + 16), half("dd", c, h)
-            if p not in BY_SCALAR[r]:
-                gathered(d, ob, half(q0, c, h), Op.subtract, TABLE[r])
-                for i, n, to in dests(p):
-                    y = 64 * c + 32 + 8 * (i % 4)
-                    after(i, n, gathered(to, ("OB", y, y + 8 * n), units("dd", i, n), Op.mult, "LT", 96))
-                continue
             picked(half("rr", c, h), ("OB", x + 32, x + 48), "LT", 96)
-            picked(d, ob, TABLE[r])
-            mm([(("SQ", 0, 256), M("NI"), half(q0, c, h), True, False)])
-            mm([(("SQ", 0, 256), M("ID"), d, False, True)])
             for i, n, to in dests(p):
-                x = NU * (i - 2 * p)
-                after(i, n, tt(to, ("SQ", x, x + NU * n), units("rr", i, n), Op.mult))
+                for u, w in ((0, n),) if p not in FINE[r] else [(u, 1) for u in range(n)]:
+                    y = 64 * c + 8 * ((i + u) % 4)
+                    gathered((to[0], to[1] + NU * u, to[1] + NU * (u + w)), ("OB", y, y + 8 * w), units("rr", i + u, w), Op.mult,
+                             "nn", 4 * CH, 4 * CH * c)
+                after(i, n, None)
 
     sent, come = {}, {}
 
@@ -733,7 +849,7 @@ def calls(g, rank, T, topo):
             n = count(topo.mask(cores[s] if rel is None else rel, core))
             for u, i, j, w in pieces(k, s, rank, cores, topo):
                 come[k, s, u] = emit("x%d%d%d" % (k, s, u), None, [], [units(LANDS[k], j, w)], None,
-                                     (TNEAR if rel is None else TFAR) + 7 - 7 * k, ("arr%d%d%d" % (k, s, u), n))
+                                     (TNEAR if rel is None else TFAR) + TLATE * (1 - k), ("arr%d%d%d" % (k, s, u), n))
 
     EB, EK = "B0", "Z0"
 
@@ -741,30 +857,31 @@ def calls(g, rank, T, topo):
         qe, de = ("q0", 0, 96), ("dd", 0, 96)
         scan(("FT", 0, 160), ("NM", 0, 160), (EB, 352, 512), Op.min)
         F, Bb = ("FT", 4, 160, 5), ("BT", 4, 160, 5)
-        act(("ed", 0, 32), Bb, Fn.Relu, bias=16.0 * (NONE + 2.0 ** 17), scale=-16.0)
-        tt(("ed", 32, 64), Bb, ("ed", 0, 32), Op.add)
-        parts(F, 3)
-        tt(put(4, "HV"), F, ("ed", 32, 64), Op.is_le)
-        rounded(put(5, "HV"), put(0, "HV"), 17)
-        rounded(("ed", 64, 96), put(3, "HV"), 17)
-        tt(put(6, "HV"), put(3, "HV"), ("ed", 64, 96), Op.subtract)
+        act(put(3, "HV"), F, Fn.Copy)
+        tt(put(3), F, put(3, "HV"), Op.subtract)
+        tt(put(4, "HV"), F, Bb, Op.is_le)
+        act(put(7, "HV"), put(0, "HV"), Fn.Relu, bias=-233.0, scale=-2.0 ** -13)
+        step_of(put(6, "HV"), F)
+        picked(de, ("OB", 0, 6), "nn", 4 * CH)
         keys = (EB, 320, 332)
-        turn([((EB, 320 + 6 * x, 326 + 6 * x), w, y) for x in (1, 0) for w, y in ((put(3 - 3 * x), "ID"), (put(4, "HV"), "N8K"))])
-        ts(("key", 0, 12), keys, -2048.5, Op.max)
+        terms = [(x, w, y) for x in (1, 0) for w, y in ((put(3 - 3 * x), "ID"), (put(7, "HV"), "N8K"), (put(4, "HV"), "N8K"))]
+        turn([((EB, 320 + 6 * x, 326 + 6 * x), put(3 - 3 * x), "ID") for x in (1, 0)], [], True)
+        act(("key", 0, 12), keys, Fn.Copy)
         tt(("WD", 0, 24, 2), keys, ("w2", 0, 12), Op.subtract)
 
-        def flat(bank, lo, terms):
-            mm([((bank, lo + 24 * x, lo + 24 * x + 24), (w[0], w[1], w[1] + 128), (y, 0, 24), i == 0, i == len(terms) - 1)
-                for i, (x, w, y) in enumerate(terms)])
-        flat("SP", 0, [(x, w, y) for x in (1, 0) for w, y in ((put(3 - 3 * x), "ID"), (put(4, "HV"), "N8K"))])
+        def flat(bank, lo, terms, more=()):
+            seq = [((bank, lo + 24 * x, lo + 24 * x + 24), (w[0], w[1], w[1] + 128), (y, 0, 24)) for x, w, y in terms] + list(more)
+            mm([x + (i == 0, i == len(seq) - 1) for i, x in enumerate(seq)])
+        flat("SP", 0, terms)
         cp(("khb", 0, 48), ("SP", 0, 48))
-        flat("SP", 48, [(x, put(5 + x, "HV"), "I13") for x in range(2)])
+        flat("SP", 48, [(0, put(8, "HV"), "ID"), (1, put(3, "HV"), "I13"), (1, put(6, "HV"), "NI")],
+             [(("SP", 72, 96), M("T2K", 2), ("hf2", 64, 88, 1, 2))])
         act(("sb", 0, 48), ("SP", 48, 96), Fn.Copy)
         mm([((EK, 0, 192), M("I256"), ("IT", 0, 192), True, False)])
         mm([((EK, b, 192, 4), LJ(b), ("khb", 0, 48), False, b == 3) for b in range(4)])
         mm([((EB, b, 192, 4), LJ(b), ("sb", 0, 48), True, True) for b in range(4)])
         mm([((EB, 192, 288), M("CA"), de, True, True)])
-        act(("mf", 0, 96), (EB, 96, 192), Fn.Copy, bias=6.0)
+        act(("mf", 0, 96), (EB, 96, 192), Fn.Copy, bias=248.0)
         ts(("mk1", 0, 96), (EB, 0, 96), KK, Op.is_equal)
         tt(("cm", 0, 96), (EB, 192, 288), ("mk1", 0, 96), Op.mult)
         mm([((EB, 0, 96), M("ISY"), qe, True, False)] + [((EB, 0, 96), PM(b), ("cm", 0, 96), False, b == 2) for b in range(3)])
@@ -772,12 +889,13 @@ def calls(g, rank, T, topo):
             w = x // 6
             eq = ("EQ", 96 * x, 96 * x + 96)
             act(eq, (EK, 96 * w, 96 * w + 96), Fn.Abs, bias=("key", x, x + 1), scale=-1.0)
-            if x % 4 == 3:
-                scan(("MN", 96 * x - 288, 96 * x + 96), ("NEW", 0, NB), ("EQ", 96 * x - 288, 96 * x + 96), Op.min, Op.add)
+            if x % 3 == 2:
+                scan(("MN", 96 * x - 192, 96 * x + 96), ("NEW", 0, 288), ("EQ", 96 * x - 192, 96 * x + 96), Op.min, Op.add)
         act(("Eb", 0, 96), (EB, 0, 96), Fn.Copy)
-        tt(("HM", 17, 40, 2), ("MN", 95, 1152, 96), ("TO", 0, 12), Op.is_equal)
-        scan(("WO", 0, 24), ("HM", 16, 40), ("WD", 0, 24), Op.add)
-        cp(("OE", 0, 12), ("WO", 1, 24, 2))
+        for lo, hi in SPLIT:
+            tt(("HM", 17 + 2 * lo, 16 + 2 * hi, 2), ("MN", 95 + 96 * lo, 96 * hi, 96), ("TO", lo, hi), Op.is_equal)
+            scan(("WO", 2 * lo, 2 * hi), ("HM", 16 + 2 * lo, 16 + 2 * hi), ("WD", 2 * lo, 2 * hi), Op.add)
+            cp(("OE", lo, hi), ("WO", 2 * lo + 1, 2 * hi, 2))
         oF, oB, full_w = ("OE", 0, 6), ("OE", 6, 12), ("mkE", 0, MKW)
         emit("v", lambda: g.vector.tensor_copy(win(oF, MKW), ap(("Eb", 0, 96))), [oF, ("Eb", 0, 96)], [full_w], cost=0.35)
         emit("v", lambda: g.vector.tensor_copy(ap(("vb", 0, 96)), win(oB, MKW)), [oB, full_w], [("vb", 0, 96)], cost=0.2)
@@ -790,14 +908,16 @@ def calls(g, rank, T, topo):
     consts_search()
     for c in range(NC):
         ts(chunk("q0", c), chunk("qN", c), KLT, Op.mult)
-        first_rope(0, c, "qN", "B%d" % c)
+        if c >= FAST:
+            first_rope(0, c, "qN", "B%d" % c)
         power(0, c, 1, "SP")
         mask(0, c, 1, "qN")
-        keep(c, "qN", "SQ")
+        gate[:] = [len(ops) - 3] + sums if c < GATE else []
+        if c < FAST:
+            first_rope(0, c, "qN", "B%d" % c)
     consts_edits()
-    sends(0, None, tab)
+    sends(0, None, tab, soon)
     arrivals(0)
-    load(("mkE", 0, W), T.mk[:], "dm2", 6.0, list(come.values()))
     later_steps(0, "q0")
     for c in range(NC):
         first_rope(1, c, "qO", "SQ")
@@ -821,6 +941,11 @@ def calls(g, rank, T, topo):
     arrivals(1)
     for c in range(NC):
         mask(1, c, 1, "qO", "dR")
+        if ACC:
+            act(chunk("q1", c), chunk("qO", c), Fn.Copy, scale=KLT)
+            emit("g", lambda c=c: g.dma_start(ap(chunk("q1", c)), ap(chunk("dR", c)), accum_op=Op.add), [chunk("dR", c)],
+                 [chunk("q1", c)], "do%d" % (5 + c), TACC)
+            continue
         mm([(("SQ", 0, 512), M("ISY"), chunk("qO", c), True, False)])
         mm([(("SQ", 0, 512), M("ID"), chunk("dR", c), False, True)])
         act(chunk("q1", c), ("SQ", 0, 512), Fn.Copy)
@@ -839,7 +964,7 @@ def calls(g, rank, T, topo):
         for j, w in runs(came, 2):
             if j // 2 == p:
                 lead[emit("s", lambda j=j, w=w: g.sync.dma_start(hbm(T.yq, came[j], w), ap(units("qF", j, w))), [units("qF", j, w)], [],
-                          "dy%d" % j, 1.5)] = AHEAD[c]
+                          "dy%d" % j, 1.5)] = 0 if TAIL else AHEAD[c]
 
     for c in range(NC):
         for h in (1, 0) if 2 * c + 1 in ADD_V else (0,):

import math
import numpy as np
from concourse.mybir import AluOpType as Op, ActivationFunctionType as Fn, AxisListType

W, K, NB, NU = 4096, 1536, 384, 128
CH, NT, NC = 512, 32, 3
MKW = W + 128
LN2 = math.log(2.0)
MAGIC = 1.5 * 2.0 ** 23
NONE = -234.0 * 8192 - 2048
TILT = 0.000435
CYC, PEC, WAKE, ISSUE = 0.00083, 0.00042, 0.19, 0.05
GAT, TMK, TFAR, TNEAR, APART, TSEND, TFIRST = 1.5, 6.0, 4.3, 2.2, 1.9, 0.5, 3.0
FIXV, FIXA, FIXP = 0.035, 0.055, 0.03
AHEAD, FAST, SPLIT = (3.2, 2.0, 0.0), 1, ((0, 6), (6, 12))
LEAD, SLOW, FACTORS = 1.0, 1.05, ((1.0, 0.2, 1.0), (1.0, 0.16, 1.2), (1.35, 0.16, 1.35))
TRIES, SPAN, SHIFT, SHARE, SWAPS = 380, 15.0, 0.4, 0.06, 1500
KEEP, ACC, TACC, TLATE, GATE, SEED = (3, 3), False, 2.8, 5.0, 0, 1
PART, TAIL, EASE, UPPER_V, HALVES, EARLY = 6, 6.5, 0.0, (2,), True, 0.0
FINE = ((0, 1, 2, 3, 4, 5), (0, 1, 2, 3))
ADD_V = (4, 5)

_mats = ["XP", "ID", "NI", "I97", "I8K", "I256", "ISY", "N8K", "CA", "DN", "R12", "T2K", "CST", "ZM", "half", "I13", "hf2", "I32"]
SCRATCH = {"mkE": ("sbuf", [128, MKW], "bfloat16"),
           "LB": ("sbuf", [128, 512], "bfloat16"), "HW": ("sbuf", [128, 32 * 4 + 3, 4], "float16"),
           "HV": ("sbuf", [128, 32 * 11 + 3, 4], "bfloat16"), "TJ": ("sbuf", [128, 32], "float16"),
           "khb": ("sbuf", [128, 48], "float16")}
for _n in ("qN", "q0", "qO", "qP", "q1", "dR", "dS", "dF", "qF", "zz", "rr"):
    SCRATCH[_n] = ("sbuf", [128, K], "bfloat16")
for _n in _mats:
    SCRATCH[_n] = ("sbuf", [128, 128], "bfloat16")


def _add(dtype, **widths):
    for n, w in widths.items():
        SCRATCH[n] = ("sbuf", [128, w], dtype)


_add("bfloat16", wS=2, land0=NB, land1=NB, JR=96, LT=96, ONE=128, IO=36, MK=36, W0=106, W1=288, W2=288, WS=40, MB=480, SPM=384, MG=96,
     nn=4 * K, dd=96, MKG=36, M12=36, PM=384, OF=96, qK=1152, f0=768, sl=1728, ET=768, Cw=192, Cx=192, dead=64, none=96, MS=984, NM=160, sb=48, cm=96, Eb=96, vb=96, mf=96, Sb=96, IT=192,
     J16=16, EQ=1152, MN=1152, NEW=NB)
_add("int32", pi=1, ki=2, ci=4, X=288, H=96)
_add("float32", col=48, geo=64, D0=192, yS=96, HM=40, WD=24, WO=24, TO=12, key=24, w1=12, w2=12, mk1=96, BT=480, FT=160)
_add("uint16", OFF=96, OB=192, OE=12)
BANKS = ("Z0", "Z1", "Z2", "B0", "B1", "B2", "SP", "SQ")
for _n in BANKS:
    SCRATCH[_n] = ("psum", [128, 512], "float32")
SEMAPHORES = ["sV", "sA", "sP", "sG", "dw", "dm0", "dm1", "dm2", "db", "sent", "rls"]
SEMAPHORES += ["d%s%d" % (_k, _i) for _k in "qoy" for _i in range(12)]
SEMAPHORES += ["rin%d%d" % (_k, _u) for _k in range(2) for _u in range(3)]
SEMAPHORES += ["arr%d%d%d" % (_k, _r, _u) for _k in range(2) for _r in range(4) for _u in range(3)]


def relay_of(src, dst, cores, topo):
    k = 0
    for d in cores:
        if d == src or topo.may_write(src, d):
            if d == dst:
                return None
            continue
        own = [c for c in topo.cores_of(src) if c != src and topo.may_write(c, d)]
        near = [c for c in own if topo.die(c) == topo.die(src)]
        far = [c for c in own if topo.die(c) != topo.die(src)]
        if d == dst:
            return near[0] if k % 2 == 0 else far[0]
        k += 1
    return None


def way(a, b, cores, topo):
    return 0 if a == b else 1 if topo.may_write(cores[a], cores[b]) else 2


def goes_order(rank, cores, topo):
    n = len(cores)
    blocks = sorted(range(n), key=lambda s: (-way(rank, s, cores, topo), s ^ rank))
    return [(0, 0)] + [(s, u) for s in blocks for u in range(3) if (s, u) != (0, 0)]


def came_order(rank, cores, topo):
    def when(x):
        at = goes_order(x[0], cores, topo).index((rank, x[1])) // 4
        return (APART * at + (0.0, TNEAR - EARLY, TFAR)[way(x[0], rank, cores, topo)], x[0] ^ rank, x[1])
    return sorted([(s, u) for s in range(len(cores)) for u in range(3)], key=when)


def runs(order, cut):
    out = []
    for i, x in enumerate(order):
        if i % cut and order[i - 1] == (x[0], x[1] - 1):
            out[-1][1] += 1
        else:
            out.append([i, 1])
    return out


def pieces(k, a, b, cores, topo):
    src, dst = goes_order(a, cores, topo), came_order(b, cores, topo)
    out = []
    for u in range(3):
        i, j = src.index((b, u)), dst.index((a, u))
        if out and (i, j) == (out[-1][1] + out[-1][3], out[-1][2] + out[-1][3]) and not (k and i % 4 == 0):
            out[-1][3] += 1
        else:
            out.append([u, i, j, 1])
    return out


def count(mask):
    return bin(mask).count("1")


LANDS = ("qO", "dR")


def rank_program(g, core, T, topo):
    cores = list(T.cores)
    rank = T.rank_of(core)
    if rank is None:
        for a in cores:
            for b in cores:
                if a == b or relay_of(a, b, cores, topo) != core:
                    continue
                ra, rb = T.rank_of(a), T.rank_of(b)
                m_out = topo.mask(core, b)
                rid, pid = topo.addr(b, core)
                n = 0
                for k in range(2):
                    for u, i, j, w in sorted(pieces(k, ra, rb, cores, topo), key=lambda x: x[1]):
                        g.wait_ge(T.sem["rin%d%d" % (k, u)], count(topo.mask(a, core)))
                        g.remote_dma(T[LANDS[k]][:, NU * j:NU * (j + w)], T["land%d" % k][:, NU * u:NU * (u + w)],
                                     T.sem["arr%d%d%d" % (k, ra, u)], T.sem.rls, pid, rid, m_out)
                        n += count(m_out)
                g.wait_ge(T.sem.rls, n)
        return
    if not ORDER:
        ORDER.extend(orders([calls(g, r, T, topo) for r in range(len(cores))]))
    calls(g, rank, T, topo)[4](ORDER[rank])


ORDER = []


def orders(ranks):
    ops, lead, base = [], {}, [0]
    for x in ranks:
        base.append(base[-1] + len(x[0]))
    for r, (own, ahead, sent, come, issue, names) in enumerate(ranks):
        far = {i: base[s] + ranks[s][2][k, r, u] for (k, s, u), i in come.items()}
        for i, (q, fn, sem, cost, waits, order, ev) in enumerate(own):
            ops.append(((r, q), sem is not None, sem is None and ev is None, cost,
                        set(base[r] + d for d in waits) | ({far[i]} if i in far else set()), set(base[r] + d for d in order)))
        lead.update({base[r] + i: x for i, x in ahead.items()})
    n = len(ops)
    names = {}
    name = [names.setdefault(x, len(names)) for y in ranks for x in y[5]]
    cost = [x[3] * (SLOW if x[2] and x[0][1] == "p" else 1.0) for x in ops]
    hold = [ISSUE if x[1] else c for x, c in zip(ops, cost)]
    pred = [[(d, cost[d] + WAKE) for d in x[4]] + [(d, hold[d] if ops[d][0] == x[0] else 0.0) for d in x[5]] for x in ops]
    succ = [[] for _ in ops]
    for i in range(n):
        for d, lag in pred[i]:
            succ[d].append((i, lag))

    def listed(key, before):
        key = list(key)
        for i in (first if before is pred else first[::-1]):
            for d, lag in before[i]:
                if key[d] >= key[i]:
                    key[i] = key[d] + 1e-7
        return sorted(range(n), key=lambda i: key[i])

    def length(seq, f, wake=WAKE, pf=None):
        end, start, free = [0.0] * n, [0.0] * n, {}
        for i in seq:
            q, dma, comp, c, waits, order = ops[i]
            t = free.get(q, 0.0)
            for d in waits:
                t = max(t, end[d] + wake)
            for d in order:
                t = max(t, start[d])
            start[i], end[i] = t, t + (c * (pf if pf and q[1] == "p" else f) if comp else c)
            free[q] = t + ISSUE if dma else end[i]
        ends = [max(end[base[r]:base[r + 1]]) for r in range(len(ranks))]
        return (max(ends) + sum(ends) / len(ends)) / 2

    def sweep(key, back):
        before = succ if back else pred
        at, slots = [0.0] * n, {}
        for i in listed(key, before):
            t = cost[i] + LEAD * lead.get(i, 0) if back else 0.0
            for j, lag in before[i]:
                t = max(t, at[j] + lag)
            h = hold[i]
            if back:
                t -= h
            s = slots.setdefault(ops[i][0], [])
            lo, hi = 0, len(s)
            while lo < hi:
                k = (lo + hi) // 2
                if s[k][1] <= t + 1e-9:
                    lo = k + 1
                else:
                    hi = k
            while lo < len(s) and s[lo][0] < t + h - 1e-9:
                t = s[lo][1]
                lo += 1
            s.insert(lo, (t, t + h))
            at[i] = t + h if back else t
        return at

    def tight(at, most=1e9):
        at = sweep([-x for x in sweep([-(a + h) for a, h in zip(at, hold)], True)], False)
        seq = listed(at, pred)
        t = [length(seq, *FACTORS[0])]
        if t[0] > most:
            return 1e9, at, seq, t[0]
        t += [length(seq, f, w, pf) / f for f, w, pf in FACTORS[1:]]
        return sum(t) / len(t), at, seq, t[0]

    need = [len(x) for x in pred]
    first = [i for i in range(n) if need[i] == 0]
    for i in first:
        for j, lag in succ[i]:
            need[j] -= 1
            if need[j] == 0:
                first.append(j)
    tail = [0.0] * n
    for i in reversed(first):
        tail[i] = max([cost[i] + LEAD * lead.get(i, 0)] + [tail[j] + lag for j, lag in succ[i]])
    best = tight(sweep([-x for x in tail], False))
    rnd = np.random.default_rng(SEED)
    for k in range(TRIES):
        lo = float(rnd.random()) * best[0] - SPAN / 2
        move = (rnd.normal(size=len(names)) * SHIFT * (rnd.random(len(names)) < SHARE)).tolist()
        new = tight([a + move[name[i]] if lo < a < lo + SPAN else a for i, a in enumerate(best[1])], best[3] + 0.2)
        if new[0] <= best[0]:
            best = new
    seq = swapped(ops, base, name, succ, best[2], rnd)
    NOTE[:] = [best[0], sum(length(seq, f, w, pf) / f for f, w, pf in FACTORS) / len(FACTORS), length(seq, 1.0), length(seq, 1.4)]
    return [[i - base[r] for i in seq if ops[i][0][0] == r] for r in range(len(ranks))]


def swapped(ops, base, name, succ, seq, rnd):
    n, ranks = len(ops), len(base) - 1
    byname = {(ops[i][0][0], name[i]): i for i in range(n)}
    dep = [x[4] | x[5] for x in ops]
    costs = [[x[3] * ((pf if x[0][1] == "p" else f) if x[2] else 1.0) for x in ops] for f, w, pf in FACTORS]
    prv, nxt, last = [-1] * n, [-1] * n, {}
    for i in seq:
        if ops[i][0] in last:
            prv[i], nxt[last[ops[i][0]]] = last[ops[i][0]], i
        last[ops[i][0]] = i

    after = [[x[0] for x in y] for y in succ]
    waits = [list(x[4]) for x in ops]
    order = [[d for d in x[5] if ops[d][0] != x[0]] for x in ops]
    final = [[i for i in range(base[r], base[r + 1]) if not after[i]] for r in range(ranks)]
    held = [[ISSUE if x[1] else y for x, y in zip(ops, c)] for c in costs]

    def listed():
        need = [len(d) + (p >= 0) for d, p in zip(dep, prv)]
        out = [i for i in range(n) if need[i] == 0]
        for i in out:
            for j in after[i]:
                need[j] -= 1
                if need[j] == 0:
                    out.append(j)
            j = nxt[i]
            if j >= 0:
                need[j] -= 1
                if need[j] == 0:
                    out.append(j)
        return out if len(out) == n else None

    def run(seq, most=None):
        total, ways = 0.0, []
        for c, h, (f, wake, pf) in zip(costs, held, FACTORS):
            start, seen, why = [0.0] * n, [0.0] * n, [-1] * n
            for i in seq:
                y = prv[i]
                t = start[y] + h[y] if y >= 0 else 0.0
                for d in waits[i]:
                    if seen[d] > t:
                        t, y = seen[d], d
                for d in order[i]:
                    if start[d] > t:
                        t, y = start[d], d
                start[i], seen[i], why[i] = t, t + c[i] + wake, y
            ends = [max((seen[i], i) for i in x) for x in final]
            t = (max(ends)[0] + sum(x[0] for x in ends) / ranks) / 2 / f
            if most and not ways and t > most[0][2] + 0.15:
                return 1e9, None
            total += t
            ways.append((why, [x[1] for x in ends], t))
        return total, ways

    def swap(u, v):
        a, b = prv[u], nxt[v]
        prv[v], nxt[v], prv[u], nxt[u] = a, u, v, b
        if a >= 0:
            nxt[a] = v
        if b >= 0:
            prv[b] = u

    best, ways = run(seq)
    for k in range(SWAPS):
        why, ends = ways[int(rnd.integers(len(ways)))][:2]
        i, arcs = ends[int(rnd.integers(ranks))], []
        while why[i] >= 0:
            if why[i] == prv[i] and why[i] not in dep[i]:
                arcs.append((why[i], i))
            i = why[i]
        u, v = arcs[int(rnd.integers(len(arcs)))]
        steps, ahead, done = int(rnd.integers(1, 4)), rnd.random() < 0.5, []
        for r in range(ranks):
            a, b = byname.get((r, name[u])), byname.get((r, name[v]))
            if a is None or b is None or prv[b] != a:
                continue
            for x in range(steps):
                a, b = (prv[b], b) if ahead else (a, nxt[a])
                if a < 0 or b < 0 or a in dep[b]:
                    break
                swap(a, b)
                done.append((b, a))
        new = listed()
        t = run(new, ways) if new and done else (1e9, None)
        if t[0] <= best + EASE * (1 - k / SWAPS) * float(rnd.random()):
            seq, (best, ways) = new, t
        else:
            for a, b in reversed(done):
                swap(a, b)
    return seq


NOTE = []


def calls(g, rank, T, topo):
    cores = list(T.cores)
    core = cores[rank]
    Q = {"v": g.vector, "a": g.scalar, "p": g.tensor, "g": g, "s": g.sync}
    SEM = {"v": "sV", "a": "sA", "p": "sP", "g": "sG"}
    ops, names, seen = [], [], {}
    rec = {}
    lead = {}

    def emit(q, fn, reads, writes, sem=None, cost=0.1, ev=None, after=(), behind=()):
        i = len(ops)
        waits, order = set(after), set(behind)
        for kind, lst in (("r", reads), ("w", writes)):
            for b in lst:
                nm, lo, hi, step = (b + (1,))[:4]
                if nm in ("HW", "HV"):
                    step = 1
                if isap(b[-1]):
                    nm += "32"
                r = rec.setdefault(nm, [])
                if nm in BANKS:
                    for x in r:
                        if x[3] == i:
                            continue
                        if x[2] != q or (x[4] == "w" and q != "p"):
                            waits.add(x[3])
                        else:
                            order.add(x[3])
                    r[:] = [x for x in r if x[2] == q or x[3] == i]
                else:
                    for x in r:
                        if (x[3] != i and x[0] < hi and lo < x[1] and (kind == "w" or x[4] == "w")
                                and not (x[5] == step and (x[0] - lo) % step)):
                            waits.add(x[3])
                    if kind == "w":
                        r[:] = [x for x in r if not (lo <= x[0] and x[1] <= hi
                                                     and (step == 1 or (x[5] == step and (x[0] - lo) % step == 0)))]
                r.append((lo, hi, q, i, kind, step))
        x = (q,) + tuple((writes + reads)[0][:3])
        seen[x] = seen.get(x, 0) + 1
        names.append(x + (seen[x],))
        ops.append((q, fn, sem, cost, waits, order - waits, ev))
        return i

    def issue(seq):
        cnt = {"v": 0, "a": 0, "p": 0, "g": 0}
        clock = {q: {} for q in Q}
        clkat, evs, total = {}, {}, {}

        def see(q, ev):
            c = clock[q]
            for s, x in list(clkat.get(ev, {}).items()) + [ev]:
                if c.get(s, 0) < x:
                    c[s] = x

        def await_all(q, want):
            best = {}
            for s, x in want:
                best[s] = max(best.get(s, 0), x)
            todo = [(s, x) for s, x in best.items() if clock[q].get(s, 0) < x]
            for e in [e for e in todo if not any(o != e and clkat.get(o, {}).get(e[0], 0) >= e[1] for o in todo)]:
                Q[q].wait_ge(T.sem[e[0]], e[1])
                see(q, e)

        for i in seq:
            q, fn, sem, cost, waits, order, ev = ops[i]
            if fn is None:
                evs[i] = ev
                clkat[ev] = {}
                total[ev[0]] = ev[1]
                continue
            await_all(q, [evs[d] for d in waits if evs.get(d) is not None])
            ins = fn()
            if ev is not None:
                total[ev[0]] = total.get(ev[0], 0) + ev[1]
                continue
            if sem is None:
                cnt[q] += 1
                evs[i] = (SEM[q], cnt[q])
                ins.then_inc(T.sem[SEM[q]], 1)
            else:
                evs[i] = (sem, 16)
                ins.then_inc(T.sem[sem], 16)
            total[evs[i][0]] = evs[i][1]
            c = dict(clock[q])
            c[evs[i][0]] = evs[i][1]
            clkat[evs[i]] = c
        stores = [x for x in total.items() if x[0][:2] in ("dy", "db")]
        await_all("g", [x for x in total.items() if x not in stores])
        for x in stores:
            await_all("g", [x])

    def wide(b):
        step = b[3] if len(b) > 3 else 1
        return (b[2] - b[1] + step - 1) // step * (4 if b[0] in ("HW", "HV") and step > 1 else 1)

    def cost(out, ins, two=False):
        n = wide(out)
        if two:
            n *= 1 if any(b[0] in BANKS for b in ins) else 2
        elif all(SCRATCH[b[0]][2] in ("bfloat16", "uint16", "float16") for b in [out] + ins):
            n /= 2
        return max(64, n) * CYC + FIXV

    def ap(b):
        nm, lo, hi, step, rows = (b + (1, 128)[len(b) - 3:])[:5]
        if nm in ("HW", "HV"):
            return T[nm][:, lo // 4:hi // 4:max(step // 4, 1), :]
        p, q = rows if isap(rows) else (0, rows)
        return T[nm][p:q, lo:hi:step]

    def isap(x):
        return isinstance(x, tuple)

    def tt(out, a, b, op):
        return emit("v", lambda: g.vector.tensor_tensor(ap(out), ap(a), ap(b), op), [a, b], [out], cost=cost(out, [a, b], True))

    def ts(out, a, s1, op0, s2=None, op1=None):
        rd = [a] + [s for s in (s1, s2) if isap(s)]
        x1 = ap(s1) if isap(s1) else s1
        x2 = ap(s2) if isap(s2) else s2
        if op1 is None:
            return emit("v", lambda: g.vector.tensor_scalar(ap(out), ap(a), x1, None, op0), rd, [out], cost=cost(out, [a]))
        return emit("v", lambda: g.vector.tensor_scalar(ap(out), ap(a), x1, x2, op0, op1), rd, [out], cost=cost(out, [a]))

    def cp(out, a):
        return emit("v", lambda: g.vector.tensor_copy(ap(out), ap(a)), [a], [out], cost=cost(out, [a]))

    def fill(out, x):
        return emit("v", lambda: g.vector.memset(ap(out), x), [], [out], cost=cost(out, []))

    def scan(out, d0, d1, op1, op0=Op.mult):
        return emit("v", lambda: g.vector.tensor_tensor_scan(ap(out), ap(d0), ap(d1), 0.0, op0, op1), [d0, d1], [out],
                    cost=cost(out, [d0, d1]))

    def act(out, a, fn, bias=0.0, scale=1.0, more=0.0, behind=()):
        rd = [a] + [s for s in (bias, scale) if isap(s)]
        kw = {}
        if isap(bias) or bias != 0.0:
            kw["bias"] = ap(bias) if isap(bias) else bias
        if isap(scale) or scale != 1.0:
            kw["scale"] = ap(scale) if isap(scale) else scale
        return emit("a", lambda: g.scalar.activation(ap(out), ap(a), fn, **kw), rd, [out],
                    cost=max(64, wide(out)) * CYC + FIXA + more, behind=behind)

    def mm(seq):
        def go():
            ins = None
            for o, l, r, st, sp in seq:
                ins = g.tensor.matmul(ap(o), ap(l), ap(r), st, sp)
            return ins
        reads = sorted(set(x[1][:3] for x in seq) | set(x[2][:3] for x in seq))
        reads += [y[:3] + (1, (32, 33)) for x in seq for y in x[1:3] if len(y) == 5 and y[4] == 33]
        return emit("p", go, reads, [seq[0][0]], cost=sum(max(min(64, wide(x[1])), wide(x[0])) for x in seq) * PEC + FIXP,
                    behind=list(gate))

    gate, sums = [], []

    def LJ(j):
        return ("LB", 128 * j, 128 * j + 128)

    def M(nm, rows=128):
        return (nm, 0, 128, 1, rows)

    def units(nm, i, n=1):
        return (nm, NU * i, NU * (i + n))

    goes, came = goes_order(rank, cores, topo), came_order(rank, cores, topo)
    loads = []

    def load(b, src, sem, t, after=()):
        loads.append(emit("s", lambda: g.sync.dma_start(ap(b), src), [], [b], sem, t, None, after, loads[-1:]))
        return loads[-1]

    def hbm(t, x, n):
        return t[:, NB * x[0] + NU * x[1]:NB * x[0] + NU * (x[1] + n)]

    emit("a", lambda: g.scalar.dma_start(ap(("wS", 0, 2)), T.wt[:]), [], [("wS", 0, 2)], "dw", 1.0)
    for i, n in runs(goes, 4):
        load(units("qN", i, n), hbm(T.qs, goes[i], n), "dq%d" % i, 1.4 + 0.15 * (i + n))
    tab = [load(("mkE", x, x + W // 2), T.mk[:, x:x + W // 2], "dm%d" % (2 * x // W), TMK) for x in (0, W // 2)]
    for u, i, j, n in pieces(0, rank, rank, cores, topo):
        if ACC:
            emit("g", lambda j=j, n=n, u=u: g.dma_start(ap(units("qO", j, n)), hbm(T.qs, (rank, u), n)), [], [units("qO", j, n)],
                 "do%d" % u, 4.0, None, tab)
        else:
            load(units("qO", j, n), hbm(T.qs, (rank, u), n), "do%d" % u, TMK + 0.5)

    def C(i):
        return ("col", i, i + 1)
    KC, KA, KLT, KGE, KP1, RCOL, KK, G4, G8, GE, GS, OFS, OF32, N32, P97 = [C(i) for i in range(15)]
    T1, T2, T3, T4, T5, M15, T6, T7 = [C(16 + i) for i in range(8)]
    RC0 = ("E16", 12, 13)
    made, soon = [], []

    def iota(out, pattern, base, cm, flag=True, behind=()):
        c = 0.13 + 2 * wide(out) * CYC
        kw = {"allow_small_or_imprecise_dtypes": True} if flag else {}
        made.append(emit("g", lambda: g.iota(ap(out), pattern, base, cm, **kw), [], [out], cost=c, behind=behind))
        return made[-1]

    def pick(out, a, pattern, op, x, base, cm):
        made.append(emit("g", lambda: g.affine_select(ap(out), ap(a), pattern, op, x, base, cm), [a], [out],
                         cost=0.17 + 2 * wide(out) * CYC))

    def diag(nm, x):
        ts(M(nm), M("XP"), 0.0, Op.is_equal, x, Op.mult)

    def zero(out):
        iota(out, [[0, wide(out)]], 0, 0)

    def PM(b):
        return ("PM", 128 * b, 128 * b + 128)

    def consts_search():
        first = iota(("pi", 0, 1), [[0, 1]], 0, 1, False)
        iota(M("XP"), [[1, 128]], 0, -1, True, [first])
        iota(("IO", 0, 36), [[1, 36]], 0, 0)
        fill(("ONE", 0, 128), 1.0)
        ki, kg = ("ki", 0, 1), ("ki", 1, 2)
        ts(ki, ("pi", 0, 1), 15, Op.bitwise_and)
        ts(kg, ("pi", 0, 1), 4, Op.arith_shift_right)
        cp(KC, ki)
        fill(("MG", 0, 96), 1.5 * 2.0 ** 35)
        x = act(M("half"), M("ONE"), Fn.Exp, scale=-LN2, more=1.3)
        ts(("geo", 0, 16), ("IO", 0, 16), KC, Op.is_lt, 2.0 ** -10, Op.max)
        emit("v", lambda: g.vector.tensor_tensor_scan(ap(("geo", 16, 32)), ap(("geo", 0, 16)), ap(("geo", 0, 16)), -2.0 ** 93, Op.mult,
                                                      Op.min), [("geo", 0, 16)], [("geo", 16, 32)], cost=0.09)
        act(T6, KC, Fn.Exp, bias=50 * LN2, scale=-10 * LN2, behind=[x])
        ts(KLT, ki, 11.5, Op.is_lt)
        ts(G4, kg, 4.0, Op.mult, 3.0, Op.add)
        ts(("MK", 0, 36), ("IO", 0, 36), G4, Op.is_equal)
        for nm, x in (("ID", 1.0), ("ISY", KLT), ("NI", -1.0), ("I97", 3104.0)):
            diag(nm, x)
        pick(("WS", 8, 40), ("ONE", 0, 32), [[-1, 4], [-16, 8]], Op.is_equal, 0.0, -12, 1)
        pick(("M12", 0, 36), ("ONE", 0, 36), [[-16, 9], [1000, 4]], Op.is_equal, 0.0, -3012, 1)
        ts(("ci", 1, 2), ki, 2, Op.arith_shift_right)
        ts(("col", 32, 35), ("IO", 0, 3), ("ci", 1, 2), Op.is_equal)
        for b in range(3):
            ts(PM(b), M("XP"), 12.0 - 4 * b, Op.is_equal, C(32 + b), Op.mult)
        ts(("MKG", 0, 36), ("MK", 0, 36), ("geo", 30, 31), Op.mult)
        mm([(("SQ", 128 * b, 128 * b + 128, 1, 32), ("MKG", x, x + 32), y, y[0] == "ISY", y[0] == "PM")
            for b in range(3) for x, y in ((3 - b, M("ISY")), (0, PM(b)))])
        cp(("SPM", 0, 384, 1, 32), ("SQ", 0, 384, 1, 32))
        fill(("SPM", 0, 384, 1, (32, 33)), MAGIC)
        fill(("ET", 0, 128, 1, (32, 33)), 1.0)
        fill(("ET", 128, 768, 1, (32, 33)), 1.0)
        for o, x, scale in ((("W0", 0, 70, 2), 0, 1.0), (("W0", 1, 70, 2), 1, 32.0), (("W0", 70, 105), 1, 1.0)):
            ts(o, ("MK", 0, 35), ("wS", x, x + 1), Op.mult, scale, Op.mult)
        mm([(("Z2", 96 * b + lo, 96 * b + lo + 32 * n), y, ("W0", at + n * x, at + n * (x + 32)), y[0] == "ISY", y[0] == "PM")
            for b in range(3) for lo, at, n in ((0, 0, 2), (64, 70, 1)) for x, y in ((3 - b, M("ISY")), (0, PM(b)))])
        sums.append(len(ops) - 1)
        act(("W1", 0, 288), ("Z2", 0, 288), Fn.Copy, scale=-1.0)
        ts(("W2", 0, 288), ("W1", 0, 288), -1.0, Op.mult)
        iota(("OF", 0, 96, 1, 2), [[0, 96]], 4096, -4097)
        iota(("OF", 1, 64, 2, 2), [[0, 32]], -393216, 393184)
        fill(("MG", 1, 64, 2), 1.5 * 2.0 ** 40)
        fill(("D0", 0, 192, 2), 0.0)
        fill(("HW", 0, 524), 0.0)
        ts(("WS", 0, 8), ("MK", 3, 35, 4), T6, Op.mult, KLT, Op.mult)
        iota(M("T2K", 2), [[0, 128]], 2048, 0)
        iota(M("CST", 2), [[32, 4], [0, 32]], -464, 0)
        fill(("MS", 1, 984, 2), 0.0)
        fill(("MS", 0, 984, 2), 1.0)
        for c in range(NC):
            fill(("B%d" % c, 352, 512, 5), NONE)
        zero(M("ZM"))
        pick(M("I8K"), M("ZM"), [[-1, 128]], Op.not_equal, 8192.0, 0, 1)

    def consts_edits():
        iota(("JR", 0, 96), [[0, 6], [1, 16]], 0, 0)
        ts(("LT", 0, 96), ("JR", 0, 96), KC, Op.is_gt, KLT, Op.mult)
        zero(("mkE", W, MKW))
        for j in range(4):
            pick(LJ(j), M("ONE"), [[-16, 8], [0, 16]], Op.is_equal, 0.0, -j, 1)
        iota(("IT", 0, 192), [[0, 2], [1, 96]], 0, 0)
        soon.append(iota(("w1", 0, 12), [[0, 2], [16, 6]], W, 0))
        pick(M("CA"), M("ONE"), [[-16, 8], [-1, 4], [-1, 4]], Op.is_equal, 0.0, -13, 1)
        pick(M("CA"), M("CA"), [[0, 8], [-1, 4], [-1, 4]], Op.is_ge, 0.0, 2, 0)
        ts(KK, ("ci", 1, 2), -16.0, Op.mult, 2096.0, Op.add)
        pick(M("I13"), M("ZM"), [[-1, 128]], Op.not_equal, 2.0 ** -13, 0, 1)
        pick(M("I32"), M("ZM"), [[-1, 128]], Op.not_equal, 32.0, 0, 1)
        for x, y in enumerate((-66048, 250, 2048)):
            fill(("hf2", 32 * x, 32 * x + 32), y / 4096)
        iota(("geo", 32, 64), [[16, 32]], 0, 0)
        ts(("TJ", 0, 32), ("geo", 32, 64), KC, Op.add)
        fill(("HV", 0, 780), 0.0)
        zero(("HV", 780, 1420))
        pick(M("DN"), M("ONE"), [[-16, 8], [-1, 16]], Op.is_equal, 0.0, 1, 1)
        pick(M("DN"), M("DN"), [[0, 8], [1, 16]], Op.is_ge, 0.0, -13, 0)
        pick(M("R12"), M("ONE"), [[-16, 8], [1000, 16]], Op.is_equal, 0.0, -12012, 1)
        pick(M("I256"), M("ZM"), [[-1, 128]], Op.not_equal, 1.0 / 256, 0, 1)
        pick(M("N8K"), M("ZM"), [[-1, 128]], Op.not_equal, -8192.0, 0, 1)
        act(("WD", 1, 24, 2), ("w1", 0, 12), Fn.Identity, bias=KC)
        act(("w2", 0, 12), ("WD", 1, 24, 2), Fn.Copy, bias=-2048.0)
        act(("TO", 0, 12), ("WD", 1, 24, 2), Fn.Copy, bias=-W / 256, scale=1.0 / 256)
        zero(("HM", 0, 40))
        zero(("NM", 0, 160, 5))
        zero(("NEW", 0, NB))
        iota(("NEW", 0, NB, 96), [[0, 4]], 16384, 0)

    def sm(nm, c, k=0, n=1):
        lo = (c * n + k) * NT
        return (nm, lo, lo + NT)

    def chunk(nm, c):
        return (nm, c * CH, c * CH + CH)

    def half(nm, c, h):
        lo = c * CH + h * CH // 2
        return (nm, lo, lo + CH // 2)

    def block(nm, c, b):
        return (nm, c * CH + b, c * CH + CH, 4)

    def chosen(c, s, k):
        lo = 64 * ((3 * c + s - 1) * 3 + k - 1)
        return ("sl", lo, lo + 64)

    def rope(r, c, s, k):
        if s == 1:
            return sm("f0", 3 * r + c, k, 4)
        b = chosen(c, s - 1, k + 1)
        return (b[0], b[1] + 1, b[2], 2)

    def put(k, nm="HW"):
        return (nm, 128 * k + 12, 128 * k + 128, 16)

    def turn(terms, more=(), early=False):
        seq = [(out, (w[0], w[1] - 4 * e, w[1] + 128 - 4 * e), (x, e, 4 * wide(out), 4)) for out, w, x in terms for e in range(4)]
        seq += list(more)
        seq = [x + (i == 0, i == len(seq) - 1) for i, x in enumerate(seq)]
        if early:
            mm(seq[:4])
        return mm(seq[4 * early:])

    def first_rope(r, c, src, bank):
        o = (bank, 0, 128)
        mm([((bank, b, 128, 4), block(src, c, b), ("WS", 8, 40), b == 0, b == 3) for b in range(4)])
        act(("f0", 128 * (3 * r + c), 128 * (3 * r + c) + 128), o, Fn.Copy)

    def power(r, c, s, bank):
        o, e = (bank, 128 + 128 * c, 256 + 128 * c, 1, 32), 2 * c + (r if s == 1 else 0)
        if (r, s) == (0, 1) and c < FAST:
            mm([(o, ("M12", 3 - b, 35 - b), block("qN", c, b), b == 0, b == 3) for b in range(4)])
        else:
            mm([(o, rope(r, c, s, 0), M("ID"), True, True)])
        act(("ET", 128 * e, 128 * e + 128, 1, 32), o, Fn.Exp, bias=math.log(1.5) + 65 * LN2, scale=-10 * LN2)

    def mask(r, c, s, src, late=None):
        z, e = own("Z", r, c), 2 * c + (r if s == 1 else 0)
        if s < KEEP[r]:
            pack(z, c, src, True, False)
        else:
            mm([((z, 0, 384), M("ID"), packed("qK", c), True, False)])
        mm([((z, 128 * b, 128 * b + 128), ("SPM", 128 * b, 128 * b + 128, 1, 33), ("ET", 128 * e, 128 * e + 128, 1, 33), False,
             b == 2 and late is None) for b in range(3)])
        if late and HALVES:
            for h in range(2):
                lo = c * CH + 256 * h
                mm([((z, 128 * b + 64 * h, 128 * b + 64 * h + 64), y, (late, lo + x, lo + 256, 4), False, (h, b, x) == (1, 2, 3))
                    for b in range(3) for x, y in ((b, M("ISY")), (3, PM(b)))])
        elif late:
            pack(z, c, late, False, True)
        act(packed("zz", c), (z, 0, 384), Fn.Relu, bias=-MAGIC)

    def packed(nm, c):
        return (nm, 384 * c, 384 * c + 384)

    def pack(bank, c, src, start, stop):
        seq = [((bank, 128 * b, 128 * b + 128), y, block(src, c, x), start and b == 0 and x == 0, stop and b == 2 and x == 3)
               for b in range(3) for x, y in ((b, M("ISY")), (3, PM(b)))]
        for x in range(0, 6, PART if start else 6):
            mm(seq[x:x + (PART if start else 6)])

    def keep(c, src, bank):
        pack(bank, c, src, True, True)
        act(packed("qK", c), (bank, 0, 384), Fn.Copy)

    def own(nm, r, c):
        return "%s%d" % (nm, (c + r) % NC)

    def step(r, c, s, q0):
        bk = own("B", r, c)
        mu = rope(r, c, s, 0)
        o = (bk, 256, 352)

        def zb(b):
            return ("zz", 384 * c + 128 * b, 384 * c + 128 * b + 128)
        cw, cx = sm("Cw", c, s % 2, 2), sm("Cx", c, s % 2, 2)
        act(cw, mu, Fn.Exp, bias=math.log(1.5) + 83 * LN2, scale=-10 * LN2)
        act(cx, mu, Fn.Exp, bias=math.log(1.5) + 83 * LN2 - 6.5 * TILT, scale=-10 * LN2 + TILT)
        mm([(o, M("half", 2), ("OF", 0, 96, 1, 2), True, False)])
        mm([(o, zb(b), ("W1", 96 * b, 96 * b + 96), False, False) for b in range(3)]
           + [(o, M(x), ("MG", 0, 96), False, False) for x in ("ID", "NI")] + [((bk, 257, 320, 2), M("I97"), mu, False, False)]
           + [(o, zb(b), ("W2", 96 * b, 96 * b + 96), False, b == 2) for b in range(3)])
        act(("D0", 64 * c + 1, 64 * c + 64, 2), (bk, 320, 352), Fn.Copy)
        scan(("X", 64 * c, 64 * c + 64), ("D0", 64 * c, 64 * c + 64), (bk, 256, 320), Op.add)
        ts(sm("H", c), ("X", 64 * c + 1, 64 * c + 64, 2), 5, Op.arith_shift_right, 4095, Op.bitwise_and)
        ts(put(c), sm("H", c), -2048.0, Op.add)
        turn([((bk, 256, 288), put(c), "ID")])
        ts(sm("OFF", c), (bk, 256, 288), 2048.0, Op.add)
        code = (bk, 352 + s, 512, 5)
        mm([(code, M("I8K"), mu, True, False), (code, M("T2K", 2), ("CST", 32 * s - 32, 32 * s, 1, 2), False, False),
            (code, M("ID"), put(c), False, True), ((bk, 0, 64, 2), M("ID"), cw, True, False)]
           + [((bk, 64 * k + x, 64 * k + 64, 2), M(y), rope(r, c, s, k), False, False)
              for k in range(1, 5 - s) for x, y in enumerate(("NI", "ID"))])
        x = gathered(chunk("nn", 4 * c + s - 1), sm("OFF", c), chunk(q0, c), Op.subtract, "mkE")
        if (r, s) == (1, 4) and TAIL:
            lead[x] = TAIL + AHEAD[c]
        n = 5 - s
        mm([((bk, 2 * b, 64 * n, 8), block("nn", 4 * c + s - 1, b), ("WS", 0, 8 * n), False, b == 3) for b in range(4)])
        lo = 328 * c + 8
        flag = ("MS", lo + 2 * s, lo + 320, 10) if s < 4 else ("MB", 160 * c + 4, 160 * c + 160, 5)
        tt(flag, (bk, 0, 64, 2), cx, Op.is_equal if s < 4 else Op.not_equal)
        for k in range(1, 5 - s):
            scan(chosen(c, s, k), ("MS", lo + 2 * s - 5, lo + 2 * s + 311, 5), (bk, 64 * k, 64 * k + 64), Op.add)
        if s == 3:
            act(("MB", 160 * c, 160 * c + 160), ("MS", lo, lo + 320, 2), Fn.Copy, bias=1.0, scale=-1.0)
        if (r, c) == (0, 0):
            act(sm("dead", s % 2), mu, Fn.Relu, bias=1.0, scale=-1.0)
            tt(("NM", s, 160, 5), sm("dead", s % 2), flag, Op.max if s < 4 else Op.is_ge)

    def win(off, w=W):
        return T.mkE[:, 0:w].indirect(ap(off))

    def gathered(o, off, q, op, nm, w=W, lo=0):
        return emit("v", lambda: g.vector.tensor_tensor(ap(o), T[nm][:, lo:lo + w].indirect(ap(off)), ap(q), op),
                    [(nm, lo, lo + w), off, q], [o], cost=0.05 + GAT * CYC * wide(o))

    def picked(o, off, nm, w=W):
        return emit("a", lambda: g.scalar.activation(ap(o), T[nm][:, 0:w].indirect(ap(off)), Fn.Copy), [(nm, 0, w), off], [o],
                    cost=0.065 + GAT * CYC * wide(o))

    def later_steps(r, q0):
        for s in range(1, 5):
            for c in range(NC):
                if s == KEEP[r]:
                    keep(c, q0, "SP" if (r, s) == (1, 2) else "SQ")
                if s > 1:
                    power(r, c, s, "SP")
                    mask(r, c, s, q0)
                step(r, c, s, q0)

    def step_of(out, code):
        act(out, code, Fn.Copy, bias=2291.0, scale=2.0 ** -13)

    def learn(r, c, q0, dests, after):
        bk = own("B", r, c)
        scan(("BT", 160 * c, 160 * c + 160), ("MB", 160 * c, 160 * c + 160), (bk, 352, 512), Op.min)
        code = ("BT", 160 * c + 4, 160 * c + 160, 5)
        step_of(put(8 + c, "HV"), code)
        if c in UPPER_V:
            cp(put(c, "HV"), code)
        else:
            act(put(c, "HV"), code, Fn.Copy)
        turn([((bk, 288, 320), put(c, "HV"), "I13"), ((bk, 256, 288), put(8 + c, "HV"), "I32")],
             [((bk, 256, 288), M("ID"), ("TJ", 0, 32)), ((bk, 256, 320), M("T2K", 2), ("hf2", 0, 64, 1, 2))], True)
        cp(("OB", 64 * c, 64 * c + 64), (bk, 256, 320))
        if r or c == 0:
            tt(put(c), code, put(c, "HV"), Op.subtract)
        if r:
            act(sm("none", c), (bk, 288, 320), Fn.Relu, bias=17.0, scale=-1.0)
            turn([((bk, 288, 320), put(c), "ID")], [((bk, 288, 320), M("NI"), sm("none", c)),
                                                    ((bk, 288, 320), M("T2K", 2), ("hf2", 64, 96, 1, 2))])
            for j, w in runs(came, 4):
                if j // 4 == c:
                    x, y = 24 * came[j][0] + 8 * came[j][1], 288 + 8 * (j % 4)
                    act(("yS", x, x + 8 * w), (bk, y, y + 8 * w), Fn.Copy)
            if 2 * c + 1 not in ADD_V:
                mm([((bk, 0, 256), M("ID"), half("qO", c, 1), True, False), ((bk, 0, 256), M("ID"), half("dR", c, 1), False, False)])
        for h in range(2):
            p = 2 * c + h
            x = 64 * c + 16 * h
            picked(half("rr", c, h), ("OB", x + 32, x + 48), "LT", 96)
            for i, n, to in dests(p):
                for u, w in ((0, n),) if p not in FINE[r] else [(u, 1) for u in range(n)]:
                    y = 64 * c + 8 * ((i + u) % 4)
                    gathered((to[0], to[1] + NU * u, to[1] + NU * (u + w)), ("OB", y, y + 8 * w), units("rr", i + u, w), Op.mult,
                             "nn", 4 * CH, 4 * CH * c)
                after(i, n, None)

    sent, come = {}, {}

    def send(k, s, piece, after=(), behind=()):
        u, i, j, n = piece
        b = units(("qN", "dS")[k], i, n)
        rel = relay_of(core, cores[s], cores, topo)
        to = cores[s] if rel is None else rel
        m = topo.mask(core, to)
        rid, pid = topo.addr(to, core)
        if rel is None:
            dst, sem = ap(units(LANDS[k], j, n)), "arr%d%d%d" % (k, rank, u)
        else:
            dst, sem = ap(units("land%d" % k, u, n)), "rin%d%d" % (k, u)
        last = [x for (kk, ss, uu), x in sent.items() if ss == s]
        sent[k, s, u] = emit("g", lambda: g.remote_dma(dst, ap(b), T.sem[sem], T.sem.sent, pid, rid, m), [b], [], None, TSEND if sent else TFIRST,
                             ("sent", count(m)), after, list(behind) + last)

    def sends(k, c=None, after=(), behind=()):
        todo = [(x[1], s, x) for s in range(len(cores)) if s != rank for x in pieces(k, rank, s, cores, topo)]
        for i, s, x in sorted(todo):
            if c is None or i // 4 == c:
                send(k, s, x, after, behind)

    def arrivals(k):
        for s in range(len(cores)):
            if s == rank:
                continue
            rel = relay_of(cores[s], core, cores, topo)
            n = count(topo.mask(cores[s] if rel is None else rel, core))
            for u, i, j, w in pieces(k, s, rank, cores, topo):
                come[k, s, u] = emit("x%d%d%d" % (k, s, u), None, [], [units(LANDS[k], j, w)], None,
                                     (TNEAR if rel is None else TFAR) + TLATE * (1 - k), ("arr%d%d%d" % (k, s, u), n))

    EB, EK = "B0", "Z0"

    def edits():
        qe, de = ("q0", 0, 96), ("dd", 0, 96)
        scan(("FT", 0, 160), ("NM", 0, 160), (EB, 352, 512), Op.min)
        F, Bb = ("FT", 4, 160, 5), ("BT", 4, 160, 5)
        act(put(3, "HV"), F, Fn.Copy)
        tt(put(3), F, put(3, "HV"), Op.subtract)
        tt(put(4, "HV"), F, Bb, Op.is_le)
        act(put(7, "HV"), put(0, "HV"), Fn.Relu, bias=-233.0, scale=-2.0 ** -13)
        step_of(put(6, "HV"), F)
        picked(de, ("OB", 0, 6), "nn", 4 * CH)
        keys = (EB, 320, 332)
        terms = [(x, w, y) for x in (1, 0) for w, y in ((put(3 - 3 * x), "ID"), (put(7, "HV"), "N8K"), (put(4, "HV"), "N8K"))]
        turn([((EB, 320 + 6 * x, 326 + 6 * x), put(3 - 3 * x), "ID") for x in (1, 0)], [], True)
        act(("key", 0, 12), keys, Fn.Copy)
        tt(("WD", 0, 24, 2), keys, ("w2", 0, 12), Op.subtract)

        def flat(bank, lo, terms, more=()):
            seq = [((bank, lo + 24 * x, lo + 24 * x + 24), (w[0], w[1], w[1] + 128), (y, 0, 24)) for x, w, y in terms] + list(more)
            mm([x + (i == 0, i == len(seq) - 1) for i, x in enumerate(seq)])
        flat("SP", 0, terms)
        cp(("khb", 0, 48), ("SP", 0, 48))
        flat("SP", 48, [(0, put(8, "HV"), "ID"), (1, put(3, "HV"), "I13"), (1, put(6, "HV"), "NI")],
             [(("SP", 72, 96), M("T2K", 2), ("hf2", 64, 88, 1, 2))])
        act(("sb", 0, 48), ("SP", 48, 96), Fn.Copy)
        mm([((EK, 0, 192), M("I256"), ("IT", 0, 192), True, False)])
        mm([((EK, b, 192, 4), LJ(b), ("khb", 0, 48), False, b == 3) for b in range(4)])
        mm([((EB, b, 192, 4), LJ(b), ("sb", 0, 48), True, True) for b in range(4)])
        mm([((EB, 192, 288), M("CA"), de, True, True)])
        act(("mf", 0, 96), (EB, 96, 192), Fn.Copy, bias=248.0)
        ts(("mk1", 0, 96), (EB, 0, 96), KK, Op.is_equal)
        tt(("cm", 0, 96), (EB, 192, 288), ("mk1", 0, 96), Op.mult)
        mm([((EB, 0, 96), M("ISY"), qe, True, False)] + [((EB, 0, 96), PM(b), ("cm", 0, 96), False, b == 2) for b in range(3)])
        for x in range(12):
            w = x // 6
            eq = ("EQ", 96 * x, 96 * x + 96)
            act(eq, (EK, 96 * w, 96 * w + 96), Fn.Abs, bias=("key", x, x + 1), scale=-1.0)
            if x % 3 == 2:
                scan(("MN", 96 * x - 192, 96 * x + 96), ("NEW", 0, 288), ("EQ", 96 * x - 192, 96 * x + 96), Op.min, Op.add)
        act(("Eb", 0, 96), (EB, 0, 96), Fn.Copy)
        for lo, hi in SPLIT:
            tt(("HM", 17 + 2 * lo, 16 + 2 * hi, 2), ("MN", 95 + 96 * lo, 96 * hi, 96), ("TO", lo, hi), Op.is_equal)
            scan(("WO", 2 * lo, 2 * hi), ("HM", 16 + 2 * lo, 16 + 2 * hi), ("WD", 2 * lo, 2 * hi), Op.add)
            cp(("OE", lo, hi), ("WO", 2 * lo + 1, 2 * hi, 2))
        oF, oB, full_w = ("OE", 0, 6), ("OE", 6, 12), ("mkE", 0, MKW)
        emit("v", lambda: g.vector.tensor_copy(win(oF, MKW), ap(("Eb", 0, 96))), [oF, ("Eb", 0, 96)], [full_w], cost=0.35)
        emit("v", lambda: g.vector.tensor_copy(ap(("vb", 0, 96)), win(oB, MKW)), [oB, full_w], [("vb", 0, 96)], cost=0.2)
        o = ("SP", 128, 224)
        mm([(o, M("R12"), ("mf", 0, 96), True, False)])
        mm([(o, M("ISY"), ("vb", 0, 96), False, False), (o, M("DN"), ("vb", 0, 96), False, True)])
        act(("Sb", 0, 96), o, Fn.Copy)
        emit("v", lambda: g.vector.tensor_copy(win(oB, MKW), ap(("Sb", 0, 96))), [oB, ("Sb", 0, 96)], [full_w], cost=0.35)

    consts_search()
    for c in range(NC):
        ts(chunk("q0", c), chunk("qN", c), KLT, Op.mult)
        if c >= FAST:
            first_rope(0, c, "qN", "B%d" % c)
        power(0, c, 1, "SP")
        mask(0, c, 1, "qN")
        gate[:] = [len(ops) - 3] + sums if c < GATE else []
        if c < FAST:
            first_rope(0, c, "qN", "B%d" % c)
    consts_edits()
    sends(0, None, tab, soon)
    arrivals(0)
    later_steps(0, "q0")
    for c in range(NC):
        first_rope(1, c, "qO", "SQ")
        power(1, c, 1, "SQ")

    def learnt(p):
        out = []
        for i in (2 * p, 2 * p + 1):
            at = came.index((rank, goes[i][1])) if goes[i][0] == rank else None
            to = units("dS", i) if at is None else units("dR", at)
            if out and out[-1][2][0] == to[0] and out[-1][2][2] == to[1]:
                out[-1] = (out[-1][0], 2, (to[0], out[-1][2][1], to[2]))
            else:
                out.append((i, 1, to))
        return out

    for c in range(NC):
        learn(0, c, "q0", learnt, lambda i, n, x: None)
        sends(1, c)
    edits()
    arrivals(1)
    for c in range(NC):
        mask(1, c, 1, "qO", "dR")
        if ACC:
            act(chunk("q1", c), chunk("qO", c), Fn.Copy, scale=KLT)
            emit("g", lambda c=c: g.dma_start(ap(chunk("q1", c)), ap(chunk("dR", c)), accum_op=Op.add), [chunk("dR", c)],
                 [chunk("q1", c)], "do%d" % (5 + c), TACC)
            continue
        mm([(("SQ", 0, 512), M("ISY"), chunk("qO", c), True, False)])
        mm([(("SQ", 0, 512), M("ID"), chunk("dR", c), False, True)])
        act(chunk("q1", c), ("SQ", 0, 512), Fn.Copy)
    later_steps(1, "q1")

    def out(i, n, x):
        c, p = i // 4, i // 2
        b, z = units("qF", i, n), (own("Z", 1, c), NU * (i % 4), NU * (i % 4 + n))
        if p % 2 and p not in ADD_V:
            z = (own("B", 1, c), 0, 256)
        if p in ADD_V:
            tt(b, z, units("dF", i, n), Op.add)
        else:
            mm([(z, M("ID"), units("dF", i, n), False, True)])
            act(b, z, Fn.Copy)
        for j, w in runs(came, 2):
            if j // 2 == p:
                lead[emit("s", lambda j=j, w=w: g.sync.dma_start(hbm(T.yq, came[j], w), ap(units("qF", j, w))), [units("qF", j, w)], [],
                          "dy%d" % j, 1.5)] = 0 if TAIL else AHEAD[c]

    for c in range(NC):
        for h in (1, 0) if 2 * c + 1 in ADD_V else (0,):
            z = (own("Z", 1, c), 256 * h, 256 * h + 256)
            mm([(z, M("ID"), half("qO", c, h), True, False), (z, M("ID"), half("dR", c, h), False, 2 * c + h in ADD_V)])
        learn(1, c, "q1", lambda p: [(2 * p, 2, units("dF", 2 * p, 2))], out)
    emit("s", lambda: g.sync.dma_start(T.yb[:], T.yS[:]), [("yS", 0, 96)], [], "db", 1.2)
    return ops, lead, sent, come, issue, names
